import numpy as np, ml_dtypes
CORES = [6,15,38,47]
N = 4
BF = ml_dtypes.bfloat16
def f(rng, *shape):
    return (rng.standard_normal(shape, dtype=np.float32) * np.exp2(rng.integers(-2, 3, shape[:-1] + (1,)))).astype(BF)
def wide(rng, *shape):
    v = f(rng, *shape).astype(np.float32); k = shape[:-2] + (1, shape[-1])
    return (v * np.exp2(rng.integers(-6, 7, k)) * (rng.random(k) > 0.0625)).astype(BF)
def entries(a):
    return np.ascontiguousarray(a.T).reshape(-1)
def table(e):
    return np.ascontiguousarray(np.reshape(e, (-1, 16)).T).astype(np.int32)
K, V, A, R = 2048, 4096, 2048, 256
CAP, U, HS, AS = 96, 96, 4, 3
TM = 1048576
def fine(rng, v):
    return v.astype(np.float32) * (1 + rng.random(v.shape, dtype=np.float32))
def moments(rng, uneven, *shape):
    return np.floor(np.exp2(rng.random(shape) * 20)).astype(np.int64) - 1 if uneven else rng.integers(0, TM, shape)
def owners(rng, without=-1):
    return np.stack([rng.permutation(np.repeat(np.array([q for q in range(N) if q != without]), CAP))[:R] for r in range(N)])
def full(rng):
    o = []
    for r in range(N):
        a, b = (r + 1) % N, (r + 2) % N
        rest = rng.permutation(np.repeat(np.array([q for q in range(N) if q != a and q != b]), CAP))[:R - 2 * CAP]
        o.append(rng.permutation(np.concatenate([np.repeat(np.array([a, b]), CAP), rest])))
    return np.stack(o)
def make(rng, own, key, fall=True, share=False, edge=False, low=None, uneven=False):
    tt = moments(rng, uneven, N, 8, K, HS + AS)
    if fall: tt = -np.sort(-tt, axis=3)
    if low is not None: tt = tt // 2; tt[..., :HS] += TM // 2
    h = rng.integers(0, HS + 1, (N, 8, K))
    if edge: h = HS * rng.integers(0, 2, (N, 8, K)); h[:, :, :2] = HS
    ch = rng.integers(0, K, (N, 8, K)) if share else np.zeros((N, 8, K), np.int64) + np.arange(K)
    col, s = rng.integers(0, 8, (N, R)), rng.integers(0, HS + AS, (N, R)); tie = tt[own, col, ch[own, col, key], s]; u = rng.random((N, R))
    if edge: t = np.where(u < 0.2, 0, np.where(u < 0.4, TM - 1, np.where(u < 0.7, tie, np.maximum(tie - 1, 0))))
    else: t = np.where(u < 0.25, tie, moments(rng, uneven, N, R))
    if low is not None: t = np.where(low, rng.integers(0, TM // 2, (N, R)), t)
    M = min(3 * K // 4, 2 * A // (AS + 1))
    hd = np.zeros((N, 8, K), np.int32); vt = moments(rng, uneven, N, 8, V).astype(np.int32); at = moments(rng, uneven, N, 8, A).astype(np.int32)
    vp = rng.integers(0, V + A + 1, (N, 8, V)).astype(np.int32); ap = rng.integers(0, A + 1, (N, 8, A)).astype(np.int32)
    for q in range(N):
        got = own == q; kk, tk, z = key[got], t[got], (q + 1) % N
        for c in range(8):
            x = tt[q, c]; e = np.arange(HS)[:, None] < h[q, c]; no = np.cumsum(e.reshape(-1)).reshape(HS, K) - 1; e = e & (no < V); n = np.sum(e, axis=0)
            ln = rng.integers(1, AS + 1, M)
            if edge: ln = np.where(rng.integers(0, 2, M) > 0, AS, 1); ln[:2] = AS
            e2 = np.arange(AS)[:, None] < ln; no2 = np.cumsum(e2.reshape(-1)).reshape(AS, M) - 1; e2 = e2 & (no2 < A)
            sl, sl2 = rng.permutation(V), rng.permutation(A)
            if edge:
                sl, sl2 = np.arange(V), np.arange(A); sl[1], sl[V - 1] = V - 1, 1; sl2[1], sl2[A - 1] = A - 1, 1
            m = np.where(e2, sl2[np.minimum(no2, A - 1)], A)
            want = np.array([0, 1]) if edge else rng.permutation(kk[low[got]]) if low is not None else np.zeros(0, np.int64)
            p = rng.permutation(K); o = np.concatenate([want, p[~np.isin(p, want)]])[:M]
            cont = np.full(K, A); cont[o] = m[0][np.arange(M) // 2 if share else np.arange(M)]
            ci = ch[q, c][kk]; un = ~np.any((x[ci, :HS] <= tk[:, None]) & (np.arange(HS) < n[ci][:, None]), axis=1)
            w = np.bincount(ci[un], minlength=K); most = U if low is not None else int(rng.integers(U // 2, U + 1)); tot = 0
            for j in o[w[o] > 0].tolist():
                if tot + int(w[j]) <= most: tot += int(w[j])
                else: cont[j] = A
            nx = np.where(e, sl[np.minimum(no, V - 1)], V + cont)
            hd[q, c] = nx[0][ch[q, c]]; vp[q, c][nx[e]] = np.concatenate([nx[1:], (V + cont)[None]])[e]; vt[q, c][nx[e]] = x.T[:HS][e]
            ap[z, c][m[e2]] = np.concatenate([m[1:], np.full((1, M), A)])[e2]; at[z, c][m[e2]] = x[o, HS:].T[e2]
    vv, av = (fine(rng, wide(rng, N, 8, V)), fine(rng, wide(rng, N, 8, A))) if uneven else (fine(rng, f(rng, N, 8, V)), fine(rng, f(rng, N, 8, A)))
    return {"hd": hd, "vt": vt, "vp": vp, "vv": vv, "at": at, "ap": ap, "av": av, "rk": np.stack([table(own[r] * K + key[r]) for r in range(N)]), "rt": np.stack([table(t[r]) for r in range(N)])}
def setup_inputs(rng):
    return make(rng, owners(rng), rng.integers(0, K, (N, R)))
def setup_inputs_caps(rng):
    own = full(rng); key = np.zeros((N, R), np.int64)
    for q in range(N): key[own == q] = rng.permutation(K)[:np.count_nonzero(own == q)]
    far = (own - np.arange(N)[:, None]) % N
    return make(rng, own, key, low=(far == 1) | (far == 2))
def setup_inputs_few(rng):
    own = owners(rng, int(rng.integers(0, N))); pool = np.stack([rng.permutation(K)[:16] for q in range(N)])
    return make(rng, own, pool[own, rng.integers(0, 16, (N, R))])
def setup_inputs_edge(rng):
    pool = np.stack([np.concatenate([np.array([0, 1, K - 1]), 2 + rng.permutation(K - 3)[:29]]) for q in range(N)]); own = owners(rng)
    return make(rng, own, pool[own, rng.integers(0, 32, (N, R))], edge=True)
def setup_inputs_mixed(rng):
    return make(rng, owners(rng), rng.integers(0, K, (N, R)), fall=False, share=True)
def setup_inputs_spread(rng):
    return make(rng, owners(rng), rng.integers(0, K, (N, R)), uneven=True)
def check_inputs(d):
    bad = []
    for a, top in (("hd", V + A + 1), ("vt", TM), ("vp", V + A + 1), ("at", TM), ("ap", A + 1), ("rk", N * K), ("rt", TM)):
        if np.min(d[a]) < 0 or np.max(d[a]) >= top: bad.append(a + "_range")
    for a in ("vv", "av"):
        if not np.isfinite(d[a]).all(): bad.append(a + "_finite")
    if bad: return bad
    hd, vt, vp, n = d["hd"], d["vt"], d["vp"], d["hd"].astype(np.int64); ap = np.roll(d["ap"], -1, axis=0)
    for s in range(HS): n = np.where(n < V, np.take_along_axis(vp, np.minimum(n, V - 1), 2), n)
    if (n < V).any(): bad.append("chain_in_the_heap")
    n = np.maximum(n - V, 0)
    for s in range(AS): n = np.where(n < A, np.take_along_axis(ap, np.minimum(n, A - 1), 2), n)
    if (n < A).any(): bad.append("chain_in_the_archive")
    c = np.arange(8)[:, None]; un = np.zeros((N, 8), np.int64); most = 0
    for r in range(N):
        key, t = entries(d["rk"][r]), entries(d["rt"][r]); q = key // K; most = max(most, int(np.max(np.bincount(q, minlength=N)))); n = hd[q, c, key % K]
        for s in range(HS):
            i = np.minimum(n, V - 1); n = np.where(n < V, np.where(vt[q, c, i] <= t, V + A, vp[q, c, i]), n)
        for g in range(8): un[:, g] += np.bincount(q[(n[g] >= V) & (n[g] < V + A)], minlength=N)
    if most > CAP: bad.append("reads_of_a_pair")
    if np.max(un) > U: bad.append("unfinished_walks")
    return bad
def reference(hd, vt, vp, vv, at, ap, av, rk, rt):
    y = np.zeros((N, 8, R), np.float32); c = np.arange(8)[:, None]
    for r in range(N):
        key, t = entries(rk[r]), entries(rt[r]); q = key // K; z = (q + 1) % N
        n = hd[q, c, key % K]
        for s in range(HS):
            i = np.minimum(n, V - 1); hit = (n < V) & (vt[q, c, i] <= t)
            y[r] = np.where(hit, vv[q, c, i], y[r]); n = np.where(hit, V + A, np.where(n < V, vp[q, c, i], n))
        n = n - V
        for s in range(AS):
            i = np.minimum(n, A - 1); hit = (n < A) & (at[z, c, i] <= t)
            y[r] = np.where(hit, av[z, c, i], y[r]); n = np.where(hit, A, np.where(n < A, ap[z, c, i], n))
    return {"y": y}

@@ -1,0 +1,533 @@
+import numpy as np
+from concourse.bass import DstId, RemoteDMATransfer
+from concourse.mybir import AluOpType as A, AxisListType, ActivationFunctionType as F
+
+POOL = 100
+SCRATCH = {
+    "RKI": ("sbuf", [128, 2], "int32"), "RTI": ("sbuf", [128, 2], "int32"),
+    "PCI": ("sbuf", [128, 1], "int32"), "PBI": ("sbuf", [128, 8], "int32"), "PFC": ("sbuf", [128, 16], "float32"),
+    "EXC": ("sbuf", [128, 8], "float32"),
+    "I512": ("sbuf", [128, 512], "float32"), "RGH": ("sbuf", [128, 128], "float32"),
+    "J8": ("sbuf", [128, 384], "float32"), "J16": ("sbuf", [128, 384], "float32"), "JH": ("sbuf", [128, 64], "float32"),
+    "TRI": ("sbuf", [128, 128], "bfloat16"), "ONES": ("sbuf", [128, 128], "bfloat16"),
+    "OWI": ("sbuf", [128, 2], "int32"), "KLO": ("sbuf", [128, 2], "int32"), "E": ("sbuf", [128, 8], "bfloat16"),
+    "OWF": ("sbuf", [128, 2], "float32"), "OW8": ("sbuf", [128, 2], "float32"), "KLF": ("sbuf", [128, 2], "float32"),
+    "RTF": ("sbuf", [128, 2], "float32"), "Z": ("sbuf", [128, 8], "float32"), "SLF": ("sbuf", [128, 2], "float32"),
+    "SLI": ("sbuf", [128, 2], "int32"), "GMI": ("sbuf", [128, 4], "int32"), "GMF": ("sbuf", [128, 4], "float32"),
+    "MC": ("sbuf", [128, 2], "float32"), "K8": ("sbuf", [128, 2], "float32"), "KC": ("sbuf", [128, 2], "float32"),
+    "LT0": ("sbuf", [128, 128], "float32"), "LT1": ("sbuf", [128, 128], "float32"),
+    "RB0": ("sbuf", [128, 32], "float32"), "RB1": ("sbuf", [128, 32], "float32"),
+    "LK0": ("sbuf", [128, 128], "float16"), "LK1": ("sbuf", [128, 128], "float16"),
+    "RK0": ("sbuf", [128, 4], "float16"), "RK1": ("sbuf", [128, 4], "float16"),
+    "REQ": ("sbuf", [128, 32], "float32"), "RQ": ("sbuf", [128, 32], "float32"),
+    "SHLO": ("sbuf", [128, 128], "float32"), "SHHI": ("sbuf", [128, 128], "float32"), "UPHF": ("sbuf", [128, 128], "float32"),
+    "UPLO": ("sbuf", [128, 128], "bfloat16"), "UPHI": ("sbuf", [128, 128], "bfloat16"),
+    "MASKHD": ("sbuf", [128, 64], "float32"), "MASK8": ("sbuf", [128, 384], "float32"), "MASK16": ("sbuf", [128, 384], "float32"),
+    "RST8": ("sbuf", [128, 384], "float32"), "RST16": ("sbuf", [128, 384], "float32"),
+    "HD": ("sbuf", [128, 2048], "int32"), "C": ("sbuf", [128, 6152], "int32"), "VV": ("sbuf", [128, 4104], "float32"),
+    "AC": ("sbuf", [128, 2064], "int32"), "AV": ("sbuf", [128, 2064], "float32"),
+    "KLI": ("sbuf", [128, 4], "uint16"), "G0": ("sbuf", [128, 64], "float32"), "N0": ("sbuf", [128, 24], "float32"),
+    "L0": ("sbuf", [128, 24], "uint16"), "L1": ("sbuf", [128, 24], "uint16"), "L2": ("sbuf", [128, 24], "uint16"),
+    "L3": ("sbuf", [128, 24], "uint16"), "LF": ("sbuf", [128, 24], "uint16"), "LS": ("sbuf", [128, 24], "uint16"),
+    "LSA": ("sbuf", [128, 24], "uint16"), "M1": ("sbuf", [128, 24], "uint16"), "M2": ("sbuf", [128, 24], "uint16"),
+    "MF": ("sbuf", [128, 24], "uint16"),
+    "G": ("sbuf", [128, 384], "float32"), "S": ("sbuf", [128, 384], "float32"), "NH": ("sbuf", [128, 384], "bfloat16"),
+    "T24": ("sbuf", [128, 24], "float32"), "T24A": ("sbuf", [128, 24], "float32"),
+    "T48": ("sbuf", [128, 48], "float32"), "T48A": ("sbuf", [128, 48], "float32"),
+    "NL": ("sbuf", [128, 96], "float32"), "NF": ("sbuf", [128, 96], "float32"), "W": ("sbuf", [128, 24], "float32"),
+    "X": ("sbuf", [128, 24], "float32"), "ACC": ("sbuf", [128, 24], "float32"), "PX": ("sbuf", [128, 24], "float32"),
+    "HOUT": ("sbuf", [128, 32], "float32"), "AOUT": ("sbuf", [128, 32], "float32"),
+    "ANSH": ("sbuf", [128, 32], "float32"), "ANSA": ("sbuf", [128, 32], "float32"),
+    "LREP": ("sbuf", [128, 128], "bfloat16"), "RV0": ("sbuf", [128, 16], "bfloat16"), "RV1": ("sbuf", [128, 16], "bfloat16"),
+    "PERM0": ("sbuf", [128, 256], "float32"), "PERM1": ("sbuf", [128, 256], "float32"), "VL": ("sbuf", [128, 16], "uint16"),
+    "MSK": ("sbuf", [128, 256], "float32"), "SEL": ("sbuf", [128, 8], "float32"),
+    "XH": ("sbuf", [128, 256], "float32"), "XA": ("sbuf", [128, 256], "float32"), "YS": ("sbuf", [8, 256], "float32"),
+    "b0": ("psum", [128, 512], "float32"), "b1": ("psum", [128, 512], "float32"), "b2": ("psum", [128, 512], "float32"),
+    "b3": ("psum", [128, 512], "float32"), "b4": ("psum", [128, 512], "float32"), "b5": ("psum", [128, 512], "float32"),
+    "b6": ("psum", [128, 512], "float32"), "b7": ("psum", [128, 512], "float32"),
+}
+SEMAPHORES = ["vq", "tq", "aq", "rq", "tf", "ls", "ha", "aa", "l_rq", "l_tf", "l_ls", "l_ha", "l_aa", "sent",
+              "ld_rk", "ld_rt", "ld_hd", "ld_c", "ld_vv", "ld_ac", "ld_av", "st"] + ["k%d" % i for i in range(POOL)]
+
+
+def queue(eng, own):
+    return {"e": eng, "own": own, "n": 0, "w": 0, "p": [], "seen": {}}
+
+
+def do(Q, ins, sig=None):
+    if sig is None:
+        ins.then_inc(Q["own"], 1)
+        Q["n"] += 1
+    else:
+        ins.then_inc(sig["s"], 1)
+        sig["n"] += 1
+        if sig not in Q["p"]:
+            Q["p"].append(sig)
+
+
+def wait(Q, *sigs):
+    for s in sigs:
+        if Q["seen"].get(s["k"], 0) < s["n"]:
+            Q["e"].wait_ge(s["s"], s["n"])
+            Q["seen"][s["k"]] = s["n"]
+
+
+def sync(Q):
+    if Q["n"] > Q["w"]:
+        Q["e"].wait_ge(Q["own"], Q["n"])
+        Q["w"] = Q["n"]
+    wait(Q, *Q["p"])
+    Q["p"].clear()
+
+
+def rank_program(g, core, T, topo):
+    r = T.rank_of(core)
+    if r is None:
+        return
+    n_ranks = len(T.cores)
+    nxt, prv = (r + 1) % n_ranks, (r - 1) % n_ranks
+    others = [q for q in range(n_ranks) if q != r]
+    num = [0]
+
+    def sig():
+        k = num[0]
+        num[0] += 1
+        return {"s": T.sem["k%d" % k], "n": 0, "k": k}
+
+    V, PE, S = queue(g.vector, T.sem.vq), queue(g.tensor, T.sem.tq), queue(g.scalar, T.sem.aq)
+    GQ = {"e": g, "seen": {}}
+    SQ = {"e": g.sync, "seen": {}}
+    v, pe, act = g.vector, g.tensor, g.scalar
+
+    def addr(q):
+        rid, pid, _ = topo.addr(T.cores[q])
+        return rid, pid
+
+    def some(q, first, count):
+        m = 0
+        for e in topo.engines(core, T.cores[q])[first:first + count]:
+            m |= 1 << e
+        return m
+
+    def send3(src, dst_col, dst, rs, ls, counts):
+        first, trs = 0, []
+        for i, q in enumerate(others):
+            rid, pid = addr(q)
+            trs.append(RemoteDMATransfer(dst_ids=[DstId(rid=rid, pnc=pid)], dma_engine_mask=some(q, first, counts[i]),
+                                         remote_sem=rs, src=src(q), dst=dst[:, dst_col:dst_col + 8]))
+            first += counts[i]
+        g.remote_dma_fused(trs, local_sem=ls)
+
+    loads = {}
+
+    def load(q, name, out, in_):
+        q.dma_start(out, in_).then_inc(T.sem[name], 16)
+        loads[name] = loads.get(name, 0) + 16
+
+    load(g.sync, "ld_rk", T.RKI[:, :], T.rk[:, :])
+    load(g.scalar, "ld_rt", T.RTI[:, :], T.rt[:, :])
+    for k in range(8):
+        load(g.sync, "ld_hd", T.HD[16 * k:16 * k + 8, :], T.hd[:, :])
+        load(g.scalar, "ld_hd", T.HD[16 * k + 8:16 * k + 16, :], T.hd[:, :])
+    for k in range(8):
+        load(g.sync if k % 2 == 0 else g.scalar, "ld_c", T.C[16 * k:16 * k + 8, 0:4096], T.vp[:, :])
+
+    s_pc, s_i5, s_gh, s_j8, s_j16, s_jh = sig(), sig(), sig(), sig(), sig(), sig()
+
+    def iota(out, pattern, cm, s, flag=True):
+        if flag:
+            g.iota(out, pattern, 0, cm, allow_small_or_imprecise_dtypes=True).then_inc(s["s"], 1)
+        else:
+            g.iota(out, pattern, 0, cm).then_inc(s["s"], 1)
+        s["n"] += 1
+
+    iota(T.PCI[:, :], [[0, 1]], 1, s_pc, False)
+    iota(T.I512[:, :], [[1, 512]], 0, s_i5)
+    iota(T.RGH[:, :], [[1, 16], [0, 8]], 0, s_gh)
+    iota(T.J8[:, :], [[0, 48], [1, 8]], 0, s_j8)
+    iota(T.JH[:, :], [[0, 4], [1, 2], [0, 8]], 0, s_jh)
+    iota(T.J16[:, :], [[0, 24], [1, 16]], 0, s_j16)
+
+    def ts(out, in0, s1, op0, s2=None, op1=None, to=None):
+        if op1 is None:
+            do(V, v.tensor_scalar(out, in0, s1, None, op0), to)
+        else:
+            do(V, v.tensor_scalar(out, in0, s1, s2, op0, op1), to)
+
+    def tt(out, a, b, op, to=None):
+        do(V, v.tensor_tensor(out, a, b, op), to)
+
+    def cp(out, in_, to=None):
+        do(V, v.tensor_copy(out, in_), to)
+
+    s_one, s_ac0, s_av0 = sig(), sig(), sig()
+    do(V, v.memset(T.ONES[:, :], 1.0), s_one)
+    wait(V, s_pc)
+    pb, pf = T.PBI, T.PFC
+    ts(pb[:, 0:1], T.PCI[:, :], 15, A.bitwise_and)
+    ts(pb[:, 1:2], T.PCI[:, :], 3, A.arith_shift_right)
+    ts(pb[:, 2:3], T.PCI[:, :], 3, A.arith_shift_right, 1, A.bitwise_and)
+    ts(pb[:, 3:4], T.PCI[:, :], 7, A.bitwise_and)
+    cp(pb[:, 4:5], T.PCI[:, :])
+    sync(V)
+    cp(pf[:, 0:5], pb[:, 0:5])
+    sync(V)
+    ts(pf[:, 5:6], pf[:, 2:3], -1.0, A.mult, 1.0, A.add)
+    ts(pf[:, 6:7], pf[:, 4:5], 8.0, A.add)
+    ts(pf[:, 7:8], pf[:, 4:5], -8.0, A.add)
+    ts(pf[:, 10:11], pf[:, 3:4], 2.0, A.mult)
+    ts(pf[:, 11:12], pf[:, 3:4], 2.0, A.mult, 1.0, A.add)
+    ts(pf[:, 12:13], pf[:, 3:4], 32.0, A.mult)
+    sync(V)
+    tt(pf[:, 8:9], pf[:, 12:13], pf[:, 1:2], A.add)
+    wait(V, s_i5)
+    ts(T.TRI[:, :], T.I512[:, 0:128], pf[:, 4:5], A.is_gt, to=s_one)
+    sync(V)
+    ts(pf[:, 9:10], pf[:, 8:9], 16.0, A.add)
+    big = float(1048576)
+    for b in range(5):
+        ts(T.EXC[:, b:b + 1], pf[:, 5:6], float(4096 + 512 * b) - big, A.mult, big, A.add)
+
+    v.wait_ge(T.sem.ld_rk, loads["ld_rk"])
+    ts(T.OWI[:, :], T.RKI[:, :], 11, A.arith_shift_right)
+    ts(T.KLO[:, :], T.RKI[:, :], 2047, A.bitwise_and)
+    sync(V)
+    s_e = sig()
+    for q in range(n_ranks):
+        ts(T.E[:, q:8:4], T.OWI[:, :], q, A.is_equal, to=s_e)
+    cp(T.OWF[:, :], T.OWI[:, :])
+    ts(T.OW8[:, :], T.OWI[:, :], 8.0, A.mult)
+    cp(T.KLF[:, :], T.KLO[:, :])
+    v.wait_ge(T.sem.ld_rt, loads["ld_rt"])
+    cp(T.RTF[:, :], T.RTI[:, :])
+    wait(PE, s_one, s_e)
+    s_pos = sig()
+    do(PE, pe.matmul(T.b0[:, 0:4], T.TRI[:, :], T.E[:, 0:4], True, True), s_pos)
+    pe.matmul(T.b0[:, 4:8], T.TRI[:, :], T.E[:, 4:8], True, False)
+    do(PE, pe.matmul(T.b0[:, 4:8], T.ONES[:, :], T.E[:, 0:4], False, True), s_pos)
+    sync(V)
+    wait(V, s_pos)
+    tt(T.Z[:, :], T.b0[:, 0:8], T.E[:, :], A.mult)
+    sync(V)
+    do(V, v.tensor_reduce(T.SLF[:, 0:1], T.Z[:, 0:4], AxisListType.X, A.add))
+    do(V, v.tensor_reduce(T.SLF[:, 1:2], T.Z[:, 4:8], AxisListType.X, A.add))
+    sync(V)
+    cp(T.SLI[:, :], T.SLF[:, :])
+    sync(V)
+    ts(T.GMI[:, 0:2], T.SLI[:, :], 15, A.bitwise_and)
+    ts(T.GMI[:, 2:4], T.SLI[:, :], 4, A.arith_shift_right)
+    sync(V)
+    cp(T.GMF[:, :], T.GMI[:, :])
+    sync(V)
+    wait(V, s_gh)
+    tt(T.MC[:, :], T.GMF[:, 2:4], T.OW8[:, :], A.add)
+    ts(T.K8[:, :], T.GMF[:, 0:2], 8.0, A.mult)
+    s_c0, s_c1 = sig(), sig()
+    ts(T.LT0[:, :], T.RGH[:, :], T.GMF[:, 0:1], A.is_equal, to=s_c0)
+    sync(V)
+    ts(T.RB0[:, :], T.I512[:, 0:32], T.MC[:, 0:1], A.is_equal, T.RTF[:, 0:1], A.mult, to=s_c0)
+    tt(T.KC[:, :], T.K8[:, :], T.GMF[:, 2:4], A.add)
+    ts(T.LT1[:, :], T.RGH[:, :], T.GMF[:, 1:2], A.is_equal, to=s_c1)
+    ts(T.RB1[:, :], T.I512[:, 0:32], T.MC[:, 1:2], A.is_equal, T.RTF[:, 1:2], A.mult, to=s_c1)
+    s_kk = sig()
+    sync(V)
+    ts(T.LK0[:, :], T.I512[:, 0:128], T.KC[:, 0:1], A.is_equal, to=s_kk)
+    ts(T.RK0[:, :], T.I512[:, 0:4], T.OWF[:, 0:1], A.is_equal, T.KLF[:, 0:1], A.mult, to=s_kk)
+    ts(T.LK1[:, :], T.I512[:, 0:128], T.KC[:, 1:2], A.is_equal, to=s_kk)
+    ts(T.RK1[:, :], T.I512[:, 0:4], T.OWF[:, 1:2], A.is_equal, T.KLF[:, 1:2], A.mult, to=s_kk)
+    s_tp, s_kp = sig(), sig()
+    wait(PE, s_c0)
+    pe.matmul(T.b1[:, 0:32], T.LT0[:, :], T.RB0[:, :], True, False)
+    wait(PE, s_c1)
+    do(PE, pe.matmul(T.b1[:, 0:32], T.LT1[:, :], T.RB1[:, :], False, True), s_tp)
+    wait(PE, s_kk)
+    pe.matmul(T.b2[:, 0:4], T.LK0[:, :], T.RK0[:, :], True, False)
+    do(PE, pe.matmul(T.b2[:, 0:4], T.LK1[:, :], T.RK1[:, :], False, True), s_kp)
+    s_rq, s_own = sig(), sig()
+    sync(V)
+    wait(V, s_tp)
+    cp(T.REQ[:, :], T.b1[:, 0:32], s_rq)
+    sync(V)
+    wait(V, s_kp)
+    cp(T.REQ[:, 6:32:8], T.b2[:, 0:4], s_rq)
+    sync(V)
+    cp(T.RQ[:, 8 * r:8 * r + 8], T.REQ[:, 8 * r:8 * r + 8], s_own)
+    wait(GQ, s_rq)
+    send3(lambda q: T.REQ[:, 8 * q:8 * q + 8], 8 * r, T.RQ, T.sem.rq, T.sem.l_rq, [2, 2, 2])
+    g.sem_inc(T.sem.sent, 1)
+
+    s_rst, s_z = sig(), sig()
+    wait(S, s_j8, s_j16, s_i5)
+    do(S, act.activation(T.RST8[:, :], T.J8[:, :], F.Sign), s_rst)
+    do(S, act.activation(T.RST16[:, :], T.J16[:, :], F.Sign), s_rst)
+    do(S, act.activation(T.VV[:, 0:8], T.I512[:, 0:8], F.Copy, scale=0.0), s_z)
+    for b in range(8):
+        do(S, act.activation(T.VV[:, 8 + 512 * b:520 + 512 * b], T.I512[:, :], F.Copy, scale=0.0), s_z)
+    ys = g.sync
+    ys.wait_ge(T.sem.sent, 1)
+    for k in range(8):
+        load(ys, "ld_c", T.C[16 * k + 8:16 * k + 16, 0:4096], T.vt[:, :])
+    wait(SQ, s_z)
+    for k in range(8):
+        load(ys, "ld_vv", T.VV[16 * k:16 * k + 8, 8:4104], T.vv[:, :])
+    for k in range(8):
+        load(ys, "ld_ac", T.AC[16 * k:16 * k + 8, 8:2056], T["ap"][:, :])
+        load(ys, "ld_ac", T.AC[16 * k + 8:16 * k + 16, 8:2056], T["at"][:, :])
+    for k in range(16):
+        load(ys, "ld_av", T.AV[8 * k:8 * k + 8, 8:2056], T["av"][:, :])
+
+    s_sh = sig()
+    i128, p, lo, hi = T.I512[:, 0:128], pf[:, 4:5], pf[:, 5:6], pf[:, 2:3]
+    ts(T.SHHI[:, :], i128, pf[:, 6:7], A.is_equal, lo, A.mult, to=s_sh)
+    ts(T.UPHF[:, :], i128, p, A.is_equal, hi, A.mult, to=s_sh)
+    ts(T.SHLO[:, :], i128, p, A.is_equal, lo, A.mult, to=s_sh)
+    ts(T.UPLO[:, :], i128, pf[:, 7:8], A.is_equal, hi, A.mult, to=s_sh)
+    ts(T.UPHI[:, :], i128, p, A.is_equal, hi, A.mult, to=s_sh)
+    wait(V, s_jh, s_j8, s_j16)
+    ts(T.MASKHD[:, :], T.JH[:, :], hi, A.is_equal)
+    ts(T.MASK8[:, :], T.J8[:, :], pf[:, 3:4], A.is_equal)
+    for b in range(4):
+        ts(T.C[:, 4096 + 512 * b:4608 + 512 * b], T.I512[:, :], lo, A.mult, T.EXC[:, b:b + 1], A.add)
+    ts(T.C[:, 6144:6152], T.I512[:, 0:8], lo, A.mult, T.EXC[:, 4:5], A.add)
+    do(V, v.memset(T.AC[:, 0:8], 2048))
+    do(V, v.memset(T.AC[:, 2056:2064], 2048))
+    do(V, v.memset(T.AV[:, 0:8], 0.0))
+    do(V, v.memset(T.AV[:, 2056:2064], 0.0))
+    do(V, v.memset(T.HOUT[:, :], 0.0))
+    do(V, v.memset(T.AOUT[:, :], 0.0))
+    sync(V)
+
+    arrived = 2 * len(others)
+    act.wait_ge(T.sem.rq, arrived)
+    wait(S, s_own)
+    s_t24 = sig()
+    for q in range(n_ranks):
+        do(S, act.activation(T.T24[:, 6 * q:6 * q + 6], T.RQ[:, 8 * q:8 * q + 6], F.Copy), s_t24)
+
+    def spread(t24, bank, t48):
+        s1, s2 = sig(), sig()
+        do(PE, pe.matmul(bank[:, 0:24], T.SHHI[:, :], t24, True, True), s1)
+        do(PE, pe.matmul(bank[:, 24:48], T.UPHF[:, :], t24, True, True), s1)
+        wait(S, s1)
+        do(S, act.activation(t48[:, 0:48:2], bank[:, 0:24], F.Copy), s2)
+        do(S, act.activation(t48[:, 1:48:2], bank[:, 24:48], F.Copy), s2)
+        return s2
+
+    wait(PE, s_sh, s_t24)
+    s_t48 = spread(T.T24[:, :], T.b0, T.T48)
+    wait(GQ, s_t24)
+    rid, pid = addr(nxt)
+    all8 = topo.mask(core, T.cores[nxt])
+    n8 = len(topo.engines(core, T.cores[nxt]))
+    g.remote_dma(out_ap=T.T24A[:, :], in_ap=T.T24[:, :], remote_sem=T.sem.tf, local_sem=T.sem.l_tf, pid=pid, routing_id=rid,
+                 dma_engine_mask=all8)
+
+    v.wait_ge(T.sem.rq, arrived)
+    cp(T.KLI[:, :], T.RQ[:, 6:32:8])
+    sync(V)
+    v.wait_ge(T.sem.ld_hd, loads["ld_hd"])
+    tt(T.G0[:, :], T.HD[:, :].indirect(T.KLI[:, 0:4]), T.MASKHD[:, :], A.mult)
+    sync(V)
+    for q in range(n_ranks):
+        tt(T.N0[:, 6 * q:6 * q + 6], T.G0[:, 16 * q:16 * q + 6], T.G0[:, 16 * q + 8:16 * q + 14], A.add)
+    sync(V)
+    cp(T.L0[:, :], T.N0[:, :])
+
+    nbank, hbank = [T.b1, T.b2], [T.b3, T.b5]
+
+    def fetch(win, lst, mask, rst, to):
+        sync(V)
+        tt(T.G[:, :], win.indirect(lst), mask, A.mult)
+        sync(V)
+        do(V, v.tensor_tensor_scan(T.S[:, :], rst, T.G[:, :], 0.0, A.mult, A.add), to)
+
+    def follow(bank, s_in):
+        s = sig()
+        wait(PE, s_in)
+        pe.matmul(bank[:, 0:24], T.SHLO[:, :], T.S[:, 7:384:16], True, False)
+        do(PE, pe.matmul(bank[:, 0:24], T.SHHI[:, :], T.S[:, 15:384:16], False, True), s)
+        return s
+
+    def judge(bank, k, t48, op):
+        s1, s2 = sig(), sig()
+        sync(V)
+        nh = T.NH[:, 48 * k:48 * k + 48]
+        tt(nh, T.S[:, 7:384:8], t48, op, s1)
+        wait(PE, s1)
+        pe.matmul(bank[:, 0:24], T.UPLO[:, :], T.NH[:, 48 * k:48 * k + 48:2], True, False)
+        do(PE, pe.matmul(bank[:, 0:24], T.UPHI[:, :], T.NH[:, 48 * k + 1:48 * k + 48:2], False, True), s2)
+        return s2
+
+    def col(buf, k):
+        return buf[:, 24 * k:24 * k + 24]
+
+    def live(k, s_h):
+        wait(V, s_h)
+        if k == 0:
+            cp(col(T.NF, 0), hbank[0][:, 0:24])
+        else:
+            tt(col(T.NF, k), col(T.NF, k - 1), hbank[k % 2][:, 0:24], A.mult)
+
+    def place(k):
+        sync(V)
+        if k == 0:
+            ts(T.W[:, :], col(T.NF, 0), -1.0, A.mult, 1.0, A.add)
+        else:
+            tt(T.W[:, :], col(T.NF, k - 1), col(T.NF, k), A.subtract)
+        sync(V)
+        tt(T.ACC[:, :] if k == 0 else T.X[:, :], T.W[:, :], col(T.NL, k), A.mult)
+        if k:
+            sync(V)
+            tt(T.ACC[:, :], T.ACC[:, :], T.X[:, :], A.add)
+
+    lists = [T.L0, T.L1, T.L2, T.L3]
+    wait(V, s_rst)
+    s_n, s_h = None, None
+    for k in range(4):
+        if k == 0:
+            sync(V)
+            v.wait_ge(T.sem.ld_c, loads["ld_c"])
+        s_s = sig()
+        fetch(T.C[:, :], lists[k][:, 0:24], T.MASK8[:, :], T.RST8[:, :], s_s)
+        s_n1 = follow(nbank[k % 2], s_s)
+        wait(V, s_t48)
+        s_h1 = judge(hbank[k % 2], k, T.T48[:, :], A.is_gt)
+        ts(col(T.NL, k), T.N0[:, :] if k == 0 else nbank[(k - 1) % 2][:, 0:24], 8.0, A.add)
+        if k:
+            live(k - 1, s_h)
+            place(k - 1)
+        sync(V)
+        s_n, s_h = s_n1, s_h1
+        wait(V, s_n)
+        if k < 3:
+            cp(lists[k + 1][:, :], nbank[k % 2][:, 0:24])
+    live(3, s_h)
+    sync(V)
+    tt(T.PX[:, :], col(T.NF, 3), nbank[1][:, 0:24], A.mult)
+    sync(V)
+    s_ls = sig()
+    ts(T.LS[:, :], T.PX[:, :], -4088.0, A.add, 0.0, A.max, to=s_ls)
+    wait(GQ, s_ls)
+    g.remote_dma(out_ap=T.LSA[:, :], in_ap=T.LS[:, :], remote_sem=T.sem.ls, local_sem=T.sem.l_ls, pid=pid, routing_id=rid,
+                 dma_engine_mask=all8)
+
+    place(3)
+    sync(V)
+    cp(T.LF[:, :], T.ACC[:, :])
+    sync(V)
+    v.wait_ge(T.sem.ld_vv, loads["ld_vv"])
+    s_s = sig()
+    fetch(T.VV[:, :], T.LF[:, 0:24], T.MASK8[:, :], T.RST8[:, :], s_s)
+    s_v = follow(T.b4, s_s)
+    wait(PE, s_sh)
+    s_p4 = sig()
+    ts(T.LREP[:, :], T.J16[:, 0:128], pf[:, 1:2], A.is_equal, to=s_p4)
+    for x, rv in ((0, T.RV0), (1, T.RV1)):
+        ts(rv[:, :], T.I512[:, 0:16], pf[:, 10 + x:11 + x], A.is_equal, T.MC[:, x:x + 1], A.mult, to=s_p4)
+    sync(V)
+    wait(V, s_v)
+    s_ho = sig()
+    cp(T.HOUT[:, 0:24], T.b4[:, 0:24], s_ho)
+    sync(V)
+    wait(GQ, s_ho)
+    send3(lambda q: T.HOUT[:, 6 * q:6 * q + 8], 8 * r, T.ANSH, T.sem.ha, T.sem.l_ha, [4, 2, 2])
+    cp(T.ANSH[:, 8 * r:8 * r + 8], T.HOUT[:, 6 * r:6 * r + 8])
+    for x, pm in ((0, T.PERM0), (1, T.PERM1)):
+        ts(pm[:, :], T.I512[:, 0:256], pf[:, 8 + x:9 + x], A.is_equal, to=s_p4)
+    ts(T.MASK16[:, :], T.J16[:, :], pf[:, 0:1], A.is_equal)
+    ts(T.SEL[:, :], T.I512[:, 0:8], pf[:, 3:4], A.is_equal, to=s_p4)
+
+    pe.wait_ge(T.sem.tf, n8)
+    s_t48a = spread(T.T24A[:, :], T.b7, T.T48A)
+    s_vl, s_mp, s_mk = sig(), sig(), sig()
+    wait(PE, s_p4)
+    pe.matmul(T.b0[:, 0:16], T.LREP[:, :], T.RV0[:, :], True, False)
+    do(PE, pe.matmul(T.b0[:, 0:16], T.LREP[:, :], T.RV1[:, :], False, True), s_vl)
+    pe.matmul(T.b4[:, 0:256], T.LT0[:, :], T.PERM0[:, :], True, False)
+    do(PE, pe.matmul(T.b4[:, 0:256], T.LT1[:, :], T.PERM1[:, :], False, True), s_mp)
+    wait(S, s_mp)
+    do(S, act.activation(T.MSK[:, :], T.b4[:, 0:256], F.Copy), s_mk)
+    sync(V)
+    wait(V, s_vl)
+    cp(T.VL[:, :], T.b0[:, 0:16])
+
+    sync(V)
+    v.wait_ge(T.sem.ls, n8)
+    v.wait_ge(T.sem.ld_ac, loads["ld_ac"])
+    ml = [T.LSA, T.M1, T.M2]
+    s_n, s_hs = None, []
+    for k in range(3):
+        s_s = sig()
+        fetch(T.AC[:, :], ml[k][:, 0:24], T.MASK8[:, :], T.RST8[:, :], s_s)
+        if k < 2:
+            s_n = follow(nbank[k % 2], s_s)
+        wait(V, s_t48a)
+        s_hs.append(judge(hbank[k % 2], 4 + k, T.T48A[:, :], A.is_le))
+        if k == 0:
+            cp(col(T.NL, 0), T.LSA[:, :])
+        elif k == 1:
+            ts(col(T.NL, 1), nbank[0][:, 0:24], 8.0, A.add)
+            wait(V, s_hs[0])
+            tt(T.ACC[:, :], hbank[0][:, 0:24], col(T.NL, 0), A.mult)
+            ts(col(T.NF, 0), hbank[0][:, 0:24], -1.0, A.mult, 1.0, A.add)
+        else:
+            ts(col(T.NL, 2), nbank[1][:, 0:24], 8.0, A.add)
+            wait(V, s_hs[1])
+            tt(T.W[:, :], col(T.NF, 0), hbank[1][:, 0:24], A.mult)
+            sync(V)
+            tt(col(T.NF, 1), col(T.NF, 0), T.W[:, :], A.subtract)
+            tt(T.X[:, :], T.W[:, :], col(T.NL, 1), A.mult)
+            sync(V)
+            tt(T.ACC[:, :], T.ACC[:, :], T.X[:, :], A.add)
+            tt(T.PX[:, :], col(T.NF, 1), col(T.NL, 2), A.mult)
+        sync(V)
+        if k < 2:
+            wait(V, s_n)
+            ts(ml[k + 1][:, :], nbank[k % 2][:, 0:24], 8.0, A.add)
+    wait(V, s_hs[2])
+    tt(T.X[:, :], hbank[0][:, 0:24], T.PX[:, :], A.mult)
+    sync(V)
+    tt(T.ACC[:, :], T.ACC[:, :], T.X[:, :], A.add)
+    sync(V)
+    cp(T.MF[:, :], T.ACC[:, :])
+    sync(V)
+    v.wait_ge(T.sem.ld_av, loads["ld_av"])
+    fetch(T.AV[:, :], T.MF[:, 0:24], T.MASK16[:, :], T.RST16[:, :], None)
+    sync(V)
+    s_ao = sig()
+    cp(T.AOUT[:, 0:24], T.S[:, 15:384:16], s_ao)
+    sync(V)
+    wait(GQ, s_ao)
+    send3(lambda q: T.AOUT[:, 6 * q:6 * q + 8], 8 * prv, T.ANSA, T.sem.aa, T.sem.l_aa, [4, 2, 2])
+    cp(T.ANSA[:, 8 * prv:8 * prv + 8], T.AOUT[:, 6 * r:6 * r + 8])
+
+    def landed(senders, counts=(4, 2, 2)):
+        t = 0
+        for q in senders:
+            t += counts[[o for o in range(n_ranks) if o != q].index(r)]
+        return t
+
+    s_xh, s_xa, s_y, s_ys = sig(), sig(), sig(), sig()
+    sync(V)
+    wait(V, s_mk)
+    v.wait_ge(T.sem.ha, landed(others))
+    tt(T.XH[:, :], T.ANSH[:, :].indirect(T.VL[:, 0:16]), T.MSK[:, :], A.mult, s_xh)
+    v.wait_ge(T.sem.aa, landed(others))
+    tt(T.XA[:, :], T.ANSA[:, :].indirect(T.VL[:, 0:16]), T.MSK[:, :], A.mult, s_xa)
+    wait(PE, s_xh)
+    pe.matmul(T.b6[0:8, 0:256], T.SEL[:, :], T.XH[:, :], True, False)
+    wait(PE, s_xa)
+    do(PE, pe.matmul(T.b6[0:8, 0:256], T.SEL[:, :], T.XA[:, :], False, True), s_y)
+    wait(S, s_y)
+    do(S, act.activation(T.YS[:, :], T.b6[0:8, 0:256], F.Copy), s_ys)
+    wait(S, s_ys)
+    g.scalar.dma_start(T.y[:, :], T.YS[:, :]).then_inc(T.sem.st, 16)
+    sync(V)
+    sync(PE)
+    sync(S)
+    g.scalar.wait_ge(T.sem.st, 16)
+    g.wait_ge(T.sem.l_rq, 6)
+    g.wait_ge(T.sem.l_tf, n8)
+    g.wait_ge(T.sem.l_ls, n8)
+    g.wait_ge(T.sem.l_ha, 8)
+    g.wait_ge(T.sem.l_aa, 8)

@@ -2,52 +2,22 @@ import numpy as np
 from concourse.bass import DstId, RemoteDMATransfer
 from concourse.mybir import AluOpType as A, AxisListType, ActivationFunctionType as F
 
-POOL = 100
-SCRATCH = {
-    "RKI": ("sbuf", [128, 2], "int32"), "RTI": ("sbuf", [128, 2], "int32"),
-    "PCI": ("sbuf", [128, 1], "int32"), "PBI": ("sbuf", [128, 8], "int32"), "PFC": ("sbuf", [128, 16], "float32"),
-    "EXC": ("sbuf", [128, 8], "float32"),
-    "I512": ("sbuf", [128, 512], "float32"), "RGH": ("sbuf", [128, 128], "float32"),
-    "J8": ("sbuf", [128, 384], "float32"), "J16": ("sbuf", [128, 384], "float32"), "JH": ("sbuf", [128, 64], "float32"),
-    "TRI": ("sbuf", [128, 128], "bfloat16"), "ONES": ("sbuf", [128, 128], "bfloat16"),
-    "OWI": ("sbuf", [128, 2], "int32"), "KLO": ("sbuf", [128, 2], "int32"), "E": ("sbuf", [128, 8], "bfloat16"),
-    "OWF": ("sbuf", [128, 2], "float32"), "OW8": ("sbuf", [128, 2], "float32"), "KLF": ("sbuf", [128, 2], "float32"),
-    "RTF": ("sbuf", [128, 2], "float32"), "Z": ("sbuf", [128, 8], "float32"), "SLF": ("sbuf", [128, 2], "float32"),
-    "SLI": ("sbuf", [128, 2], "int32"), "GMI": ("sbuf", [128, 4], "int32"), "GMF": ("sbuf", [128, 4], "float32"),
-    "MC": ("sbuf", [128, 2], "float32"), "K8": ("sbuf", [128, 2], "float32"), "KC": ("sbuf", [128, 2], "float32"),
-    "LT0": ("sbuf", [128, 128], "float32"), "LT1": ("sbuf", [128, 128], "float32"),
-    "RB0": ("sbuf", [128, 32], "float32"), "RB1": ("sbuf", [128, 32], "float32"),
-    "LK0": ("sbuf", [128, 128], "float16"), "LK1": ("sbuf", [128, 128], "float16"),
-    "RK0": ("sbuf", [128, 4], "float16"), "RK1": ("sbuf", [128, 4], "float16"),
-    "REQ": ("sbuf", [128, 32], "float32"), "RQ": ("sbuf", [128, 32], "float32"),
-    "SHLO": ("sbuf", [128, 128], "float32"), "SHHI": ("sbuf", [128, 128], "float32"), "UPHF": ("sbuf", [128, 128], "float32"),
-    "UPLO": ("sbuf", [128, 128], "bfloat16"), "UPHI": ("sbuf", [128, 128], "bfloat16"),
-    "MASKHD": ("sbuf", [128, 64], "float32"), "MASK8": ("sbuf", [128, 384], "float32"), "MASK16": ("sbuf", [128, 384], "float32"),
-    "RST8": ("sbuf", [128, 384], "float32"), "RST16": ("sbuf", [128, 384], "float32"),
-    "HD": ("sbuf", [128, 2048], "int32"), "C": ("sbuf", [128, 6152], "int32"), "VV": ("sbuf", [128, 4104], "float32"),
-    "AC": ("sbuf", [128, 2064], "int32"), "AV": ("sbuf", [128, 2064], "float32"),
-    "KLI": ("sbuf", [128, 4], "uint16"), "G0": ("sbuf", [128, 64], "float32"), "N0": ("sbuf", [128, 24], "float32"),
-    "L0": ("sbuf", [128, 24], "uint16"), "L1": ("sbuf", [128, 24], "uint16"), "L2": ("sbuf", [128, 24], "uint16"),
-    "L3": ("sbuf", [128, 24], "uint16"), "LF": ("sbuf", [128, 24], "uint16"), "LS": ("sbuf", [128, 24], "uint16"),
-    "LSA": ("sbuf", [128, 24], "uint16"), "M1": ("sbuf", [128, 24], "uint16"), "M2": ("sbuf", [128, 24], "uint16"),
-    "MF": ("sbuf", [128, 24], "uint16"),
-    "G": ("sbuf", [128, 384], "float32"), "S": ("sbuf", [128, 384], "float32"), "NH": ("sbuf", [128, 384], "bfloat16"),
-    "T24": ("sbuf", [128, 24], "float32"), "T24A": ("sbuf", [128, 24], "float32"),
-    "T48": ("sbuf", [128, 48], "float32"), "T48A": ("sbuf", [128, 48], "float32"),
-    "NL": ("sbuf", [128, 96], "float32"), "NF": ("sbuf", [128, 96], "float32"), "W": ("sbuf", [128, 24], "float32"),
-    "X": ("sbuf", [128, 24], "float32"), "ACC": ("sbuf", [128, 24], "float32"), "PX": ("sbuf", [128, 24], "float32"),
-    "HOUT": ("sbuf", [128, 32], "float32"), "AOUT": ("sbuf", [128, 32], "float32"),
-    "ANSH": ("sbuf", [128, 32], "float32"), "ANSA": ("sbuf", [128, 32], "float32"),
-    "LREP": ("sbuf", [128, 128], "bfloat16"), "RV0": ("sbuf", [128, 16], "bfloat16"), "RV1": ("sbuf", [128, 16], "bfloat16"),
-    "PERM0": ("sbuf", [128, 256], "float32"), "PERM1": ("sbuf", [128, 256], "float32"), "VL": ("sbuf", [128, 16], "uint16"),
-    "MSK": ("sbuf", [128, 256], "float32"), "SEL": ("sbuf", [128, 8], "float32"),
-    "XH": ("sbuf", [128, 256], "float32"), "XA": ("sbuf", [128, 256], "float32"), "YS": ("sbuf", [8, 256], "float32"),
-    "b0": ("psum", [128, 512], "float32"), "b1": ("psum", [128, 512], "float32"), "b2": ("psum", [128, 512], "float32"),
-    "b3": ("psum", [128, 512], "float32"), "b4": ("psum", [128, 512], "float32"), "b5": ("psum", [128, 512], "float32"),
-    "b6": ("psum", [128, 512], "float32"), "b7": ("psum", [128, 512], "float32"),
+WIDTHS = {
+    "int32": dict(RKI=2, RTI=2, PCI=1, PBI=8, OWI=2, KLO=2, SLI=2, GMI=4, HD=2048, C=4104, AC=2064),
+    "float32": dict(PFC=16, I256=256, RGH=128, J8=384, J16=384, JH=64, OWF=2, OW8=2, KLF=2, RTF=2, Z=8, SLF=2, GMF=4,
+                    MC=2, K8=2, KC=2, LT0=128, LT1=128, RB0=32, RB1=32, REQ=32, RQ=32, SHLO=128, SHHI=128, UPHF=128,
+                    MASKHD=64, MASK8=384, MASK16=384, RST8=384, RST16=384, VV=4104, AV=2064, G0=64, N0=24, G=384, S=384,
+                    T24=24, T24A=24, T48=48, T48A=48, NL=96, NF=48, CM=120, W=96, X=96, ACC=24, PX=24, MX=24, HOUT=32,
+                    AOUT=32, ANSH=32, ANSA=32, PERM0=256, PERM1=256, MSK=256, SEL=8, XH=256, XA=256),
+    "bfloat16": dict(TRI=128, ONES=128, E=8, UL=512, UH=512, NH=384, LREP=128, RV0=16, RV1=16),
+    "float16": dict(LK0=128, LK1=128, RK0=4, RK1=4),
+    "uint16": dict(KLI=4, L=96, LF=24, LS=24, LSA=24, M1=24, M2=24, MF=24, VL=16),
 }
+SCRATCH = {b: ("sbuf", [128, w], d) for d in WIDTHS for b, w in WIDTHS[d].items()}
+SCRATCH["YS"] = ("sbuf", [8, 256], "float32")
+SCRATCH.update({"b%d" % i: ("psum", [128, 512], "float32") for i in range(8)})
 SEMAPHORES = ["vq", "tq", "aq", "rq", "tf", "ls", "ha", "aa", "l_rq", "l_tf", "l_ls", "l_ha", "l_aa", "sent",
-              "ld_rk", "ld_rt", "ld_hd", "ld_c", "ld_vv", "ld_ac", "ld_av", "st"] + ["k%d" % i for i in range(POOL)]
+              "ld_rk", "ld_rt", "ld_hd", "ld_c", "ld_vv", "ld_ac", "ld_av", "st"] + ["k%d" % i for i in range(100)]
 
 
 def queue(eng, own):
@@ -90,31 +60,20 @@ def rank_program(g, core, T, topo):
     num = [0]
 
     def sig():
-        k = num[0]
         num[0] += 1
-        return {"s": T.sem["k%d" % k], "n": 0, "k": k}
+        return {"s": T.sem["k%d" % (num[0] - 1)], "n": 0, "k": num[0]}
 
     V, PE, S = queue(g.vector, T.sem.vq), queue(g.tensor, T.sem.tq), queue(g.scalar, T.sem.aq)
-    GQ = {"e": g, "seen": {}}
-    SQ = {"e": g.sync, "seen": {}}
+    GQ, SQ = {"e": g, "seen": {}}, {"e": g.sync, "seen": {}}
     v, pe, act = g.vector, g.tensor, g.scalar
-
-    def addr(q):
-        rid, pid, _ = topo.addr(T.cores[q])
-        return rid, pid
-
-    def some(q, first, count):
-        m = 0
-        for e in topo.engines(core, T.cores[q])[first:first + count]:
-            m |= 1 << e
-        return m
 
     def send3(src, dst_col, dst, rs, ls, counts):
         first, trs = 0, []
         for i, q in enumerate(others):
-            rid, pid = addr(q)
-            trs.append(RemoteDMATransfer(dst_ids=[DstId(rid=rid, pnc=pid)], dma_engine_mask=some(q, first, counts[i]),
-                                         remote_sem=rs, src=src(q), dst=dst[:, dst_col:dst_col + 8]))
+            rid, pid, _ = topo.addr(T.cores[q])
+            m = sum(1 << e for e in topo.engines(core, T.cores[q])[first:first + counts[i]])
+            trs.append(RemoteDMATransfer(dst_ids=[DstId(rid=rid, pnc=pid)], dma_engine_mask=m, remote_sem=rs, src=src(q),
+                                         dst=dst[:, dst_col:dst_col + 8]))
             first += counts[i]
         g.remote_dma_fused(trs, local_sem=ls)
 
@@ -132,27 +91,22 @@ def rank_program(g, core, T, topo):
     for k in range(8):
         load(g.sync if k % 2 == 0 else g.scalar, "ld_c", T.C[16 * k:16 * k + 8, 0:4096], T.vp[:, :])
 
-    s_pc, s_i5, s_gh, s_j8, s_j16, s_jh = sig(), sig(), sig(), sig(), sig(), sig()
+    s_pc, s_i, s_gh, s_j8, s_j16, s_jh = sig(), sig(), sig(), sig(), sig(), sig()
 
     def iota(out, pattern, cm, s, flag=True):
-        if flag:
-            g.iota(out, pattern, 0, cm, allow_small_or_imprecise_dtypes=True).then_inc(s["s"], 1)
-        else:
-            g.iota(out, pattern, 0, cm).then_inc(s["s"], 1)
+        kw = {"allow_small_or_imprecise_dtypes": True} if flag else {}
+        g.iota(out, pattern, 0, cm, **kw).then_inc(s["s"], 1)
         s["n"] += 1
 
     iota(T.PCI[:, :], [[0, 1]], 1, s_pc, False)
-    iota(T.I512[:, :], [[1, 512]], 0, s_i5)
-    iota(T.RGH[:, :], [[1, 16], [0, 8]], 0, s_gh)
+    iota(T.I256[:, :], [[1, 256]], 0, s_i)
     iota(T.J8[:, :], [[0, 48], [1, 8]], 0, s_j8)
+    iota(T.RGH[:, :], [[1, 16], [0, 8]], 0, s_gh)
     iota(T.JH[:, :], [[0, 4], [1, 2], [0, 8]], 0, s_jh)
     iota(T.J16[:, :], [[0, 24], [1, 16]], 0, s_j16)
 
     def ts(out, in0, s1, op0, s2=None, op1=None, to=None):
-        if op1 is None:
-            do(V, v.tensor_scalar(out, in0, s1, None, op0), to)
-        else:
-            do(V, v.tensor_scalar(out, in0, s1, s2, op0, op1), to)
+        do(V, v.tensor_scalar(out, in0, s1, None, op0) if op1 is None else v.tensor_scalar(out, in0, s1, s2, op0, op1), to)
 
     def tt(out, a, b, op, to=None):
         do(V, v.tensor_tensor(out, a, b, op), to)
@@ -160,7 +114,7 @@ def rank_program(g, core, T, topo):
     def cp(out, in_, to=None):
         do(V, v.tensor_copy(out, in_), to)
 
-    s_one, s_ac0, s_av0 = sig(), sig(), sig()
+    s_one, s_sh = sig(), sig()
     do(V, v.memset(T.ONES[:, :], 1.0), s_one)
     wait(V, s_pc)
     pb, pf = T.PBI, T.PFC
@@ -172,27 +126,33 @@ def rank_program(g, core, T, topo):
     sync(V)
     cp(pf[:, 0:5], pb[:, 0:5])
     sync(V)
+    big = float(1048576)
     ts(pf[:, 5:6], pf[:, 2:3], -1.0, A.mult, 1.0, A.add)
     ts(pf[:, 6:7], pf[:, 4:5], 8.0, A.add)
     ts(pf[:, 7:8], pf[:, 4:5], -8.0, A.add)
     ts(pf[:, 10:11], pf[:, 3:4], 2.0, A.mult)
     ts(pf[:, 11:12], pf[:, 3:4], 2.0, A.mult, 1.0, A.add)
     ts(pf[:, 12:13], pf[:, 3:4], 32.0, A.mult)
+    ts(pf[:, 13:14], pf[:, 2:3], big - 4096.0, A.mult, 4096.0, A.add)
+    wait(V, s_i)
+    ts(T.TRI[:, :], T.I256[:, 0:128], pf[:, 4:5], A.is_gt, to=s_one)
     sync(V)
     tt(pf[:, 8:9], pf[:, 12:13], pf[:, 1:2], A.add)
-    wait(V, s_i5)
-    ts(T.TRI[:, :], T.I512[:, 0:128], pf[:, 4:5], A.is_gt, to=s_one)
+    i128, p, lo, hi = T.I256[:, 0:128], pf[:, 4:5], pf[:, 5:6], pf[:, 2:3]
+    ul, uh = [T.UL[:, 128 * i:128 * i + 128] for i in range(4)], [T.UH[:, 128 * i:128 * i + 128] for i in range(4)]
+    for out, at, role in ((T.SHHI[:, :], pf[:, 6:7], lo), (T.UPHF[:, :], p, hi), (T.SHLO[:, :], p, lo),
+                          (ul[3], pf[:, 7:8], hi), (uh[3], p, hi)):
+        ts(out, i128, at, A.is_equal, role, A.mult, to=s_sh)
     sync(V)
     ts(pf[:, 9:10], pf[:, 8:9], 16.0, A.add)
-    big = float(1048576)
-    for b in range(5):
-        ts(T.EXC[:, b:b + 1], pf[:, 5:6], float(4096 + 512 * b) - big, A.mult, big, A.add)
+    wait(V, s_j8)
+    ts(T.MASK8[:, :], T.J8[:, :], pf[:, 3:4], A.is_equal)
 
     v.wait_ge(T.sem.ld_rk, loads["ld_rk"])
     ts(T.OWI[:, :], T.RKI[:, :], 11, A.arith_shift_right)
     ts(T.KLO[:, :], T.RKI[:, :], 2047, A.bitwise_and)
     sync(V)
-    s_e = sig()
+    s_e, s_pos = sig(), sig()
     for q in range(n_ranks):
         ts(T.E[:, q:8:4], T.OWI[:, :], q, A.is_equal, to=s_e)
     cp(T.OWF[:, :], T.OWI[:, :])
@@ -201,7 +161,6 @@ def rank_program(g, core, T, topo):
     v.wait_ge(T.sem.ld_rt, loads["ld_rt"])
     cp(T.RTF[:, :], T.RTI[:, :])
     wait(PE, s_one, s_e)
-    s_pos = sig()
     do(PE, pe.matmul(T.b0[:, 0:4], T.TRI[:, :], T.E[:, 0:4], True, True), s_pos)
     pe.matmul(T.b0[:, 4:8], T.TRI[:, :], T.E[:, 4:8], True, False)
     do(PE, pe.matmul(T.b0[:, 4:8], T.ONES[:, :], T.E[:, 0:4], False, True), s_pos)
@@ -222,47 +181,42 @@ def rank_program(g, core, T, topo):
     wait(V, s_gh)
     tt(T.MC[:, :], T.GMF[:, 2:4], T.OW8[:, :], A.add)
     ts(T.K8[:, :], T.GMF[:, 0:2], 8.0, A.mult)
-    s_c0, s_c1 = sig(), sig()
+    s_c0, s_c1, s_kk, s_kp, s_rq, s_own = sig(), sig(), sig(), sig(), sig(), sig()
     ts(T.LT0[:, :], T.RGH[:, :], T.GMF[:, 0:1], A.is_equal, to=s_c0)
     sync(V)
-    ts(T.RB0[:, :], T.I512[:, 0:32], T.MC[:, 0:1], A.is_equal, T.RTF[:, 0:1], A.mult, to=s_c0)
+    ts(T.RB0[:, :], T.I256[:, 0:32], T.MC[:, 0:1], A.is_equal, T.RTF[:, 0:1], A.mult, to=s_c0)
     tt(T.KC[:, :], T.K8[:, :], T.GMF[:, 2:4], A.add)
     ts(T.LT1[:, :], T.RGH[:, :], T.GMF[:, 1:2], A.is_equal, to=s_c1)
-    ts(T.RB1[:, :], T.I512[:, 0:32], T.MC[:, 1:2], A.is_equal, T.RTF[:, 1:2], A.mult, to=s_c1)
-    s_kk = sig()
+    ts(T.RB1[:, :], T.I256[:, 0:32], T.MC[:, 1:2], A.is_equal, T.RTF[:, 1:2], A.mult, to=s_c1)
     sync(V)
-    ts(T.LK0[:, :], T.I512[:, 0:128], T.KC[:, 0:1], A.is_equal, to=s_kk)
-    ts(T.RK0[:, :], T.I512[:, 0:4], T.OWF[:, 0:1], A.is_equal, T.KLF[:, 0:1], A.mult, to=s_kk)
-    ts(T.LK1[:, :], T.I512[:, 0:128], T.KC[:, 1:2], A.is_equal, to=s_kk)
-    ts(T.RK1[:, :], T.I512[:, 0:4], T.OWF[:, 1:2], A.is_equal, T.KLF[:, 1:2], A.mult, to=s_kk)
-    s_tp, s_kp = sig(), sig()
+    for x, lk, rk in ((0, T.LK0, T.RK0), (1, T.LK1, T.RK1)):
+        ts(lk[:, :], i128, T.KC[:, x:x + 1], A.is_equal, to=s_kk)
+        ts(rk[:, :], T.I256[:, 0:4], T.OWF[:, x:x + 1], A.is_equal, T.KLF[:, x:x + 1], A.mult, to=s_kk)
+
+    def mm2(out, l0, r0, l1, r1, to, *between):
+        pe.matmul(out, l0, r0, True, False)
+        wait(PE, *between)
+        do(PE, pe.matmul(out, l1, r1, False, True), to)
+
     wait(PE, s_c0)
-    pe.matmul(T.b1[:, 0:32], T.LT0[:, :], T.RB0[:, :], True, False)
-    wait(PE, s_c1)
-    do(PE, pe.matmul(T.b1[:, 0:32], T.LT1[:, :], T.RB1[:, :], False, True), s_tp)
+    mm2(T.b1[:, 0:32], T.LT0[:, :], T.RB0[:, :], T.LT1[:, :], T.RB1[:, :], s_kp, s_c1)
     wait(PE, s_kk)
-    pe.matmul(T.b2[:, 0:4], T.LK0[:, :], T.RK0[:, :], True, False)
-    do(PE, pe.matmul(T.b2[:, 0:4], T.LK1[:, :], T.RK1[:, :], False, True), s_kp)
-    s_rq, s_own = sig(), sig()
-    sync(V)
-    wait(V, s_tp)
-    cp(T.REQ[:, :], T.b1[:, 0:32], s_rq)
+    mm2(T.b1[:, 6:32:8], T.LK0[:, :], T.RK0[:, :], T.LK1[:, :], T.RK1[:, :], s_kp)
     sync(V)
     wait(V, s_kp)
-    cp(T.REQ[:, 6:32:8], T.b2[:, 0:4], s_rq)
-    sync(V)
-    cp(T.RQ[:, 8 * r:8 * r + 8], T.REQ[:, 8 * r:8 * r + 8], s_own)
+    cp(T.REQ[:, :], T.b1[:, 0:32], s_rq)
+    cp(T.RQ[:, 8 * r:8 * r + 8], T.b1[:, 8 * r:8 * r + 8], s_own)
     wait(GQ, s_rq)
     send3(lambda q: T.REQ[:, 8 * q:8 * q + 8], 8 * r, T.RQ, T.sem.rq, T.sem.l_rq, [2, 2, 2])
     g.sem_inc(T.sem.sent, 1)
 
     s_rst, s_z = sig(), sig()
-    wait(S, s_j8, s_j16, s_i5)
+    wait(S, s_j8, s_j16)
     do(S, act.activation(T.RST8[:, :], T.J8[:, :], F.Sign), s_rst)
     do(S, act.activation(T.RST16[:, :], T.J16[:, :], F.Sign), s_rst)
-    do(S, act.activation(T.VV[:, 0:8], T.I512[:, 0:8], F.Copy, scale=0.0), s_z)
-    for b in range(8):
-        do(S, act.activation(T.VV[:, 8 + 512 * b:520 + 512 * b], T.I512[:, :], F.Copy, scale=0.0), s_z)
+    for b in range(0, 4104, 384):
+        n = min(384, 4104 - b)
+        do(S, act.activation(T.VV[:, b:b + n], T.J8[:, 0:n], F.Copy, scale=0.0), s_z)
     ys = g.sync
     ys.wait_ge(T.sem.sent, 1)
     for k in range(8):
@@ -276,25 +230,31 @@ def rank_program(g, core, T, topo):
     for k in range(16):
         load(ys, "ld_av", T.AV[8 * k:8 * k + 8, 8:2056], T["av"][:, :])
 
-    s_sh = sig()
-    i128, p, lo, hi = T.I512[:, 0:128], pf[:, 4:5], pf[:, 5:6], pf[:, 2:3]
-    ts(T.SHHI[:, :], i128, pf[:, 6:7], A.is_equal, lo, A.mult, to=s_sh)
-    ts(T.UPHF[:, :], i128, p, A.is_equal, hi, A.mult, to=s_sh)
-    ts(T.SHLO[:, :], i128, p, A.is_equal, lo, A.mult, to=s_sh)
-    ts(T.UPLO[:, :], i128, pf[:, 7:8], A.is_equal, hi, A.mult, to=s_sh)
-    ts(T.UPHI[:, :], i128, p, A.is_equal, hi, A.mult, to=s_sh)
-    wait(V, s_jh, s_j8, s_j16)
+    wait(V, s_jh, s_j16)
     ts(T.MASKHD[:, :], T.JH[:, :], hi, A.is_equal)
-    ts(T.MASK8[:, :], T.J8[:, :], pf[:, 3:4], A.is_equal)
-    for b in range(4):
-        ts(T.C[:, 4096 + 512 * b:4608 + 512 * b], T.I512[:, :], lo, A.mult, T.EXC[:, b:b + 1], A.add)
-    ts(T.C[:, 6144:6152], T.I512[:, 0:8], lo, A.mult, T.EXC[:, 4:5], A.add)
-    do(V, v.memset(T.AC[:, 0:8], 2048))
-    do(V, v.memset(T.AC[:, 2056:2064], 2048))
-    do(V, v.memset(T.AV[:, 0:8], 0.0))
-    do(V, v.memset(T.AV[:, 2056:2064], 0.0))
-    do(V, v.memset(T.HOUT[:, :], 0.0))
-    do(V, v.memset(T.AOUT[:, :], 0.0))
+    ts(T.C[:, 4096:4104], T.I256[:, 0:8], 0.0, A.mult, pf[:, 13:14], A.add)
+    for i in range(3):
+        ts(ul[i], ul[3], float(8 >> i), A.mult, to=s_sh)
+        ts(uh[i], uh[3], float(8 >> i), A.mult, to=s_sh)
+    s_p4, s_pm, s_vl, s_mp, s_mk = sig(), sig(), sig(), sig(), sig()
+    ts(T.LREP[:, :], T.J16[:, 0:128], pf[:, 1:2], A.is_equal, to=s_p4)
+    for x, rv in ((0, T.RV0), (1, T.RV1)):
+        ts(rv[:, :], T.I256[:, 0:16], pf[:, 10 + x:11 + x], A.is_equal, T.MC[:, x:x + 1], A.mult, to=s_p4)
+    for x, pm in ((0, T.PERM0), (1, T.PERM1)):
+        ts(pm[:, :], T.I256[:, :], pf[:, 8 + x:9 + x], A.is_equal, to=s_pm)
+    wait(PE, s_p4)
+    mm2(T.b0[:, 0:16], T.LREP[:, :], T.RV0[:, :], T.LREP[:, :], T.RV1[:, :], s_vl)
+    wait(PE, s_pm)
+    mm2(T.b4[:, 0:256], T.LT0[:, :], T.PERM0[:, :], T.LT1[:, :], T.PERM1[:, :], s_mp)
+    wait(S, s_mp)
+    do(S, act.activation(T.MSK[:, :], T.b4[:, 0:256], F.Copy), s_mk)
+    ts(T.SEL[:, :], T.I256[:, 0:8], pf[:, 3:4], A.is_equal, to=s_p4)
+    for ap, c in ((T.AC[:, 0:8], 2048), (T.AC[:, 2056:2064], 2048), (T.AV[:, 0:8], 0.0), (T.AV[:, 2056:2064], 0.0),
+                  (T.HOUT[:, :], 0.0), (T.AOUT[:, :], 0.0), (T.CM[:, 0:24], 0.0)):
+        do(V, v.memset(ap, c))
+    ts(T.MASK16[:, :], T.J16[:, :], pf[:, 0:1], A.is_equal)
+    wait(V, s_vl)
+    cp(T.VL[:, :], T.b0[:, 0:16])
     sync(V)
 
     arrived = 2 * len(others)
@@ -314,13 +274,23 @@ def rank_program(g, core, T, topo):
         return s2
 
     wait(PE, s_sh, s_t24)
-    s_t48 = spread(T.T24[:, :], T.b0, T.T48)
-    wait(GQ, s_t24)
-    rid, pid = addr(nxt)
-    all8 = topo.mask(core, T.cores[nxt])
+    s_t48 = spread(T.T24[:, :], T.b6, T.T48)
+    rid, pid, _ = topo.addr(T.cores[nxt])
     n8 = len(topo.engines(core, T.cores[nxt]))
-    g.remote_dma(out_ap=T.T24A[:, :], in_ap=T.T24[:, :], remote_sem=T.sem.tf, local_sem=T.sem.l_tf, pid=pid, routing_id=rid,
-                 dma_engine_mask=all8)
+
+    def to_archive(dst, src, rs, ls):
+        g.remote_dma(out_ap=dst[:, :], in_ap=src[:, :], remote_sem=rs, local_sem=ls, pid=pid, routing_id=rid,
+                     dma_engine_mask=topo.mask(core, T.cores[nxt]))
+
+    wait(GQ, s_t24)
+    to_archive(T.T24A, T.T24, T.sem.tf, T.sem.l_tf)
+
+    nb, hb = [T.b1[:, 0:24], T.b2[:, 0:24]], [T.b5[:, 0:24], T.b3[:, 0:24]]
+    code = T.b3[:, 0:24]
+    W, X, ACC, PX, MX = T.W[:, 0:24], T.X[:, 0:24], T.ACC[:, :], T.PX[:, :], T.MX[:, :]
+
+    def col(buf, k, n=1):
+        return buf[:, 24 * k:24 * (k + n)]
 
     v.wait_ge(T.sem.rq, arrived)
     cp(T.KLI[:, :], T.RQ[:, 6:32:8])
@@ -331,168 +301,129 @@ def rank_program(g, core, T, topo):
     for q in range(n_ranks):
         tt(T.N0[:, 6 * q:6 * q + 6], T.G0[:, 16 * q:16 * q + 6], T.G0[:, 16 * q + 8:16 * q + 14], A.add)
     sync(V)
-    cp(T.L0[:, :], T.N0[:, :])
-
-    nbank, hbank = [T.b1, T.b2], [T.b3, T.b5]
+    ts(col(T.L, 0), T.N0[:, :], 4096.0, A.min)
 
     def fetch(win, lst, mask, rst, to):
         sync(V)
-        tt(T.G[:, :], win.indirect(lst), mask, A.mult)
+        tt(T.G[:, :], win.indirect(lst), mask[:, :], A.mult)
         sync(V)
-        do(V, v.tensor_tensor_scan(T.S[:, :], rst, T.G[:, :], 0.0, A.mult, A.add), to)
+        do(V, v.tensor_tensor_scan(T.S[:, :], rst[:, :], T.G[:, :], 0.0, A.mult, A.add), to)
 
-    def follow(bank, s_in):
+    def follow(out, s_in):
         s = sig()
         wait(PE, s_in)
-        pe.matmul(bank[:, 0:24], T.SHLO[:, :], T.S[:, 7:384:16], True, False)
-        do(PE, pe.matmul(bank[:, 0:24], T.SHHI[:, :], T.S[:, 15:384:16], False, True), s)
+        mm2(out, T.SHLO[:, :], T.S[:, 7:384:16], T.SHHI[:, :], T.S[:, 15:384:16], s)
         return s
 
-    def judge(bank, k, t48, op):
+    def judge(out, k, t48, weight, start, stop):
         s1, s2 = sig(), sig()
         sync(V)
-        nh = T.NH[:, 48 * k:48 * k + 48]
-        tt(nh, T.S[:, 7:384:8], t48, op, s1)
+        a, z = 48 * k, 48 * k + 48
+        tt(T.NH[:, a:z], T.S[:, 7:384:8], t48, A.is_le, s1)
         wait(PE, s1)
-        pe.matmul(bank[:, 0:24], T.UPLO[:, :], T.NH[:, 48 * k:48 * k + 48:2], True, False)
-        do(PE, pe.matmul(bank[:, 0:24], T.UPHI[:, :], T.NH[:, 48 * k + 1:48 * k + 48:2], False, True), s2)
+        pe.matmul(out, ul[weight], T.NH[:, a:z:2], start, False)
+        ins = pe.matmul(out, uh[weight], T.NH[:, a + 1:z:2], False, stop)
+        if stop:
+            do(PE, ins, s2)
         return s2
 
-    def col(buf, k):
-        return buf[:, 24 * k:24 * k + 24]
-
-    def live(k, s_h):
-        wait(V, s_h)
-        if k == 0:
-            cp(col(T.NF, 0), hbank[0][:, 0:24])
-        else:
-            tt(col(T.NF, k), col(T.NF, k - 1), hbank[k % 2][:, 0:24], A.mult)
-
-    def place(k):
-        sync(V)
-        if k == 0:
-            ts(T.W[:, :], col(T.NF, 0), -1.0, A.mult, 1.0, A.add)
-        else:
-            tt(T.W[:, :], col(T.NF, k - 1), col(T.NF, k), A.subtract)
-        sync(V)
-        tt(T.ACC[:, :] if k == 0 else T.X[:, :], T.W[:, :], col(T.NL, k), A.mult)
-        if k:
-            sync(V)
-            tt(T.ACC[:, :], T.ACC[:, :], T.X[:, :], A.add)
-
-    lists = [T.L0, T.L1, T.L2, T.L3]
     wait(V, s_rst)
-    s_n, s_h = None, None
+    sync(V)
+    v.wait_ge(T.sem.ld_c, loads["ld_c"])
     for k in range(4):
-        if k == 0:
-            sync(V)
-            v.wait_ge(T.sem.ld_c, loads["ld_c"])
         s_s = sig()
-        fetch(T.C[:, :], lists[k][:, 0:24], T.MASK8[:, :], T.RST8[:, :], s_s)
-        s_n1 = follow(nbank[k % 2], s_s)
+        fetch(T.C[:, :], col(T.L, k), T.MASK8, T.RST8, s_s)
+        s_n = follow(nb[k % 2], s_s)
         wait(V, s_t48)
-        s_h1 = judge(hbank[k % 2], k, T.T48[:, :], A.is_gt)
-        ts(col(T.NL, k), T.N0[:, :] if k == 0 else nbank[(k - 1) % 2][:, 0:24], 8.0, A.add)
+        s_h = judge(code, k, T.T48[:, :], k, k == 0, k == 3)
         if k:
-            live(k - 1, s_h)
-            place(k - 1)
-        sync(V)
-        s_n, s_h = s_n1, s_h1
+            tt(MX, T.N0[:, :] if k == 1 else MX, nb[(k - 1) % 2], A.max)
         wait(V, s_n)
         if k < 3:
-            cp(lists[k + 1][:, :], nbank[k % 2][:, 0:24])
-    live(3, s_h)
+            ts(col(T.L, k + 1), nb[k % 2], 4096.0, A.min)
     sync(V)
-    tt(T.PX[:, :], col(T.NF, 3), nbank[1][:, 0:24], A.mult)
+    tt(MX, MX, nb[1], A.max)
+    wait(V, s_h)
+    ts(W, code, 0.0, A.is_equal)
+    sync(V)
+    tt(PX, W, MX, A.mult)
     sync(V)
     s_ls = sig()
-    ts(T.LS[:, :], T.PX[:, :], -4088.0, A.add, 0.0, A.max, to=s_ls)
+    ts(T.LS[:, :], PX, -4088.0, A.add, 0.0, A.max, to=s_ls)
     wait(GQ, s_ls)
-    g.remote_dma(out_ap=T.LSA[:, :], in_ap=T.LS[:, :], remote_sem=T.sem.ls, local_sem=T.sem.l_ls, pid=pid, routing_id=rid,
-                 dma_engine_mask=all8)
+    to_archive(T.LSA, T.LS, T.sem.ls, T.sem.l_ls)
 
-    place(3)
+    for k in range(4):
+        ts(col(T.CM, k + 1), code, float(8 >> k), A.is_ge)
+    ts(T.NL[:, :], T.L[:, :], 8.0, A.add)
     sync(V)
-    cp(T.LF[:, :], T.ACC[:, :])
+    tt(T.W[:, :], col(T.CM, 1, 4), col(T.CM, 0, 4), A.subtract)
+    sync(V)
+    tt(T.X[:, :], T.W[:, :], T.NL[:, :], A.mult)
+    sync(V)
+    tt(col(T.W, 0, 2), col(T.X, 0, 2), col(T.X, 2, 2), A.add)
+    sync(V)
+    tt(ACC, col(T.W, 0), col(T.W, 1), A.add)
+    sync(V)
+    cp(T.LF[:, :], ACC)
     sync(V)
     v.wait_ge(T.sem.ld_vv, loads["ld_vv"])
-    s_s = sig()
-    fetch(T.VV[:, :], T.LF[:, 0:24], T.MASK8[:, :], T.RST8[:, :], s_s)
-    s_v = follow(T.b4, s_s)
-    wait(PE, s_sh)
-    s_p4 = sig()
-    ts(T.LREP[:, :], T.J16[:, 0:128], pf[:, 1:2], A.is_equal, to=s_p4)
-    for x, rv in ((0, T.RV0), (1, T.RV1)):
-        ts(rv[:, :], T.I512[:, 0:16], pf[:, 10 + x:11 + x], A.is_equal, T.MC[:, x:x + 1], A.mult, to=s_p4)
+    s_s, s_ho = sig(), sig()
+    fetch(T.VV[:, :], T.LF[:, 0:24], T.MASK8, T.RST8, s_s)
+    s_v = follow(T.b6[:, 0:24], s_s)
     sync(V)
     wait(V, s_v)
-    s_ho = sig()
-    cp(T.HOUT[:, 0:24], T.b4[:, 0:24], s_ho)
+    cp(T.HOUT[:, 0:24], T.b6[:, 0:24], s_ho)
     sync(V)
     wait(GQ, s_ho)
     send3(lambda q: T.HOUT[:, 6 * q:6 * q + 8], 8 * r, T.ANSH, T.sem.ha, T.sem.l_ha, [4, 2, 2])
     cp(T.ANSH[:, 8 * r:8 * r + 8], T.HOUT[:, 6 * r:6 * r + 8])
-    for x, pm in ((0, T.PERM0), (1, T.PERM1)):
-        ts(pm[:, :], T.I512[:, 0:256], pf[:, 8 + x:9 + x], A.is_equal, to=s_p4)
-    ts(T.MASK16[:, :], T.J16[:, :], pf[:, 0:1], A.is_equal)
-    ts(T.SEL[:, :], T.I512[:, 0:8], pf[:, 3:4], A.is_equal, to=s_p4)
 
     pe.wait_ge(T.sem.tf, n8)
     s_t48a = spread(T.T24A[:, :], T.b7, T.T48A)
-    s_vl, s_mp, s_mk = sig(), sig(), sig()
-    wait(PE, s_p4)
-    pe.matmul(T.b0[:, 0:16], T.LREP[:, :], T.RV0[:, :], True, False)
-    do(PE, pe.matmul(T.b0[:, 0:16], T.LREP[:, :], T.RV1[:, :], False, True), s_vl)
-    pe.matmul(T.b4[:, 0:256], T.LT0[:, :], T.PERM0[:, :], True, False)
-    do(PE, pe.matmul(T.b4[:, 0:256], T.LT1[:, :], T.PERM1[:, :], False, True), s_mp)
-    wait(S, s_mp)
-    do(S, act.activation(T.MSK[:, :], T.b4[:, 0:256], F.Copy), s_mk)
-    sync(V)
-    wait(V, s_vl)
-    cp(T.VL[:, :], T.b0[:, 0:16])
 
     sync(V)
     v.wait_ge(T.sem.ls, n8)
     v.wait_ge(T.sem.ld_ac, loads["ld_ac"])
     ml = [T.LSA, T.M1, T.M2]
-    s_n, s_hs = None, []
+    s_hs = []
     for k in range(3):
         s_s = sig()
-        fetch(T.AC[:, :], ml[k][:, 0:24], T.MASK8[:, :], T.RST8[:, :], s_s)
+        fetch(T.AC[:, :], ml[k][:, 0:24], T.MASK8, T.RST8, s_s)
         if k < 2:
-            s_n = follow(nbank[k % 2], s_s)
+            s_n = follow(nb[k % 2], s_s)
         wait(V, s_t48a)
-        s_hs.append(judge(hbank[k % 2], 4 + k, T.T48A[:, :], A.is_le))
+        s_hs.append(judge(hb[k % 2], 4 + k, T.T48A[:, :], 3, True, True))
         if k == 0:
             cp(col(T.NL, 0), T.LSA[:, :])
         elif k == 1:
-            ts(col(T.NL, 1), nbank[0][:, 0:24], 8.0, A.add)
+            ts(col(T.NL, 1), nb[0], 8.0, A.add)
             wait(V, s_hs[0])
-            tt(T.ACC[:, :], hbank[0][:, 0:24], col(T.NL, 0), A.mult)
-            ts(col(T.NF, 0), hbank[0][:, 0:24], -1.0, A.mult, 1.0, A.add)
+            tt(ACC, hb[0], col(T.NL, 0), A.mult)
+            ts(col(T.NF, 0), hb[0], -1.0, A.mult, 1.0, A.add)
         else:
-            ts(col(T.NL, 2), nbank[1][:, 0:24], 8.0, A.add)
+            ts(col(T.NL, 2), nb[1], 8.0, A.add)
             wait(V, s_hs[1])
-            tt(T.W[:, :], col(T.NF, 0), hbank[1][:, 0:24], A.mult)
+            tt(W, col(T.NF, 0), hb[1], A.mult)
             sync(V)
-            tt(col(T.NF, 1), col(T.NF, 0), T.W[:, :], A.subtract)
-            tt(T.X[:, :], T.W[:, :], col(T.NL, 1), A.mult)
+            tt(col(T.NF, 1), col(T.NF, 0), W, A.subtract)
+            tt(X, W, col(T.NL, 1), A.mult)
             sync(V)
-            tt(T.ACC[:, :], T.ACC[:, :], T.X[:, :], A.add)
-            tt(T.PX[:, :], col(T.NF, 1), col(T.NL, 2), A.mult)
-        sync(V)
+            tt(ACC, ACC, X, A.add)
+            tt(PX, col(T.NF, 1), col(T.NL, 2), A.mult)
+            sync(V)
         if k < 2:
             wait(V, s_n)
-            ts(ml[k + 1][:, :], nbank[k % 2][:, 0:24], 8.0, A.add)
+            ts(ml[k + 1][:, :], nb[k % 2], 8.0, A.add)
     wait(V, s_hs[2])
-    tt(T.X[:, :], hbank[0][:, 0:24], T.PX[:, :], A.mult)
+    tt(X, hb[0], PX, A.mult)
     sync(V)
-    tt(T.ACC[:, :], T.ACC[:, :], T.X[:, :], A.add)
+    tt(ACC, ACC, X, A.add)
     sync(V)
-    cp(T.MF[:, :], T.ACC[:, :])
+    cp(T.MF[:, :], ACC)
     sync(V)
     v.wait_ge(T.sem.ld_av, loads["ld_av"])
-    fetch(T.AV[:, :], T.MF[:, 0:24], T.MASK16[:, :], T.RST16[:, :], None)
+    fetch(T.AV[:, :], T.MF[:, 0:24], T.MASK16, T.RST16, None)
     sync(V)
     s_ao = sig()
     cp(T.AOUT[:, 0:24], T.S[:, 15:384:16], s_ao)
@@ -501,33 +432,33 @@ def rank_program(g, core, T, topo):
     send3(lambda q: T.AOUT[:, 6 * q:6 * q + 8], 8 * prv, T.ANSA, T.sem.aa, T.sem.l_aa, [4, 2, 2])
     cp(T.ANSA[:, 8 * prv:8 * prv + 8], T.AOUT[:, 6 * r:6 * r + 8])
 
-    def landed(senders, counts=(4, 2, 2)):
-        t = 0
-        for q in senders:
-            t += counts[[o for o in range(n_ranks) if o != q].index(r)]
-        return t
-
-    s_xh, s_xa, s_y, s_ys = sig(), sig(), sig(), sig()
+    landed = sum((4, 2, 2)[[o for o in range(n_ranks) if o != q].index(r)] for q in others)
+    s_xh, s_x = sig(), [sig(), sig()]
+    s_y, s_ys = [sig(), sig()], [sig(), sig()]
     sync(V)
     wait(V, s_mk)
-    v.wait_ge(T.sem.ha, landed(others))
+    v.wait_ge(T.sem.ha, landed)
     tt(T.XH[:, :], T.ANSH[:, :].indirect(T.VL[:, 0:16]), T.MSK[:, :], A.mult, s_xh)
-    v.wait_ge(T.sem.aa, landed(others))
-    tt(T.XA[:, :], T.ANSA[:, :].indirect(T.VL[:, 0:16]), T.MSK[:, :], A.mult, s_xa)
-    wait(PE, s_xh)
-    pe.matmul(T.b6[0:8, 0:256], T.SEL[:, :], T.XH[:, :], True, False)
-    wait(PE, s_xa)
-    do(PE, pe.matmul(T.b6[0:8, 0:256], T.SEL[:, :], T.XA[:, :], False, True), s_y)
-    wait(S, s_y)
-    do(S, act.activation(T.YS[:, :], T.b6[0:8, 0:256], F.Copy), s_ys)
-    wait(S, s_ys)
-    g.scalar.dma_start(T.y[:, :], T.YS[:, :]).then_inc(T.sem.st, 16)
+    v.wait_ge(T.sem.aa, landed)
+    wait(PE, s_p4, s_xh)
+    half = [slice(0, 128), slice(128, 256)]
+    bank = [T.b6[0:8, 0:128], T.b7[0:8, 0:128]]
+    for i in range(2):
+        tt(T.XA[:, half[i]], T.ANSA[:, :].indirect(T.VL[:, 8 * i:8 * i + 8]), T.MSK[:, half[i]], A.mult, s_x[i])
+        pe.matmul(bank[i], T.SEL[:, :], T.XH[:, half[i]], True, False)
+    for i in range(2):
+        wait(PE, s_x[i])
+        do(PE, pe.matmul(bank[i], T.SEL[:, :], T.XA[:, half[i]], False, True), s_y[i])
+    wait(S, s_y[0])
+    do(S, act.activation(T.YS[:, half[0]], bank[0], F.Copy), s_ys[0])
+    sync(S)
+    g.scalar.dma_start(T.y[:, half[0]], T.YS[:, half[0]]).then_inc(T.sem.st, 16)
+    wait(V, s_y[1])
+    cp(T.YS[:, half[1]], bank[1], s_ys[1])
+    wait(SQ, s_ys[1])
+    g.sync.dma_start(T.y[:, half[1]], T.YS[:, half[1]]).then_inc(T.sem.st, 16)
     sync(V)
     sync(PE)
-    sync(S)
-    g.scalar.wait_ge(T.sem.st, 16)
-    g.wait_ge(T.sem.l_rq, 6)
-    g.wait_ge(T.sem.l_tf, n8)
-    g.wait_ge(T.sem.l_ls, n8)
-    g.wait_ge(T.sem.l_ha, 8)
-    g.wait_ge(T.sem.l_aa, 8)
+    g.sync.wait_ge(T.sem.st, 32)
+    for s, n in ((T.sem.l_rq, 6), (T.sem.l_tf, n8), (T.sem.l_ls, n8), (T.sem.l_ha, 8), (T.sem.l_aa, 8)):
+        g.wait_ge(s, n)

@@ -3,21 +3,23 @@ from concourse.bass import DstId, RemoteDMATransfer
 from concourse.mybir import AluOpType as A, AxisListType, ActivationFunctionType as F
 
 WIDTHS = {
-    "int32": dict(RKI=2, RTI=2, PCI=1, PBI=8, OWI=2, KLO=2, SLI=2, GMI=4, HD=2048, C=4104, AC=2064),
-    "float32": dict(PFC=16, I256=256, RGH=128, J8=384, J16=384, JH=64, OWF=2, OW8=2, KLF=2, RTF=2, Z=8, SLF=2, GMF=4,
-                    MC=2, K8=2, KC=2, LT0=128, LT1=128, RB0=32, RB1=32, REQ=32, RQ=32, SHLO=128, SHHI=128, UPHF=128,
-                    MASKHD=64, MASK8=384, MASK16=384, RST8=384, RST16=384, VV=4104, AV=2064, G0=64, N0=24, G=384, S=384,
-                    T24=24, T24A=24, T48=48, T48A=48, NL=96, NF=48, CM=120, W=96, X=96, ACC=24, PX=24, MX=24, HOUT=32,
-                    AOUT=32, ANSH=32, ANSA=32, PERM0=256, PERM1=256, MSK=256, SEL=8, XH=256, XA=256),
-    "bfloat16": dict(TRI=128, ONES=128, E=8, UL=512, UH=512, NH=384, LREP=128, RV0=16, RV1=16),
-    "float16": dict(LK0=128, LK1=128, RK0=4, RK1=4),
-    "uint16": dict(KLI=4, L=96, LF=24, LS=24, LSA=24, M1=24, M2=24, MF=24, VL=16),
+    "int32": dict(RKI=2, RTI=2, PCI=1, PBI=8, OWI=2, KVI=6, SLI=2, GMI=6, HD=2048, C=6152, AC=2064),
+    "float32": dict(PFC=16, EXC=8, I128=128, I512=512, RG=128, SR=128, J8=384, J16=128, JH=16, R12=12, M12=12, OW12=2,
+                    KVF=6, SLF=2, GMF=6, MA=2, MC=2, EF=8, LT0=128, LT1=128, TH=4, TL=4, TK=4, THA=4, TLA=4, TKA=4, TX=48,
+                    TXA=48, GRP=128, SHLO=128, SHHI=128, MASKHD=16, MASK8=384, RST8=384, VV=4104, AV=2064, G0=64, N0=24,
+                    G=384, S0=384, S1=384, GA=384, V0=384, V1=384, V2=384, T48=48, T48A=48, NL=96, DC=96, D0=96, HP=96,
+                    HS=96, Z=48, W0=48, W1=48, A0=48, A1=48, X=48, ACC=48, PX=48, HOUT=48, AOUT=48, ANSH=48, ANSA=48,
+                    PERM0=256, PERM1=256, MSK=256, SEL=8, XH=256, XA=256),
+    "bfloat16": dict(TRI=128, EYE=128, TRIP=128, TRIN=128, ONES=128, NONES=128, GE=10, UL=128, UH=128, UL2=128,
+                     ZL=128, ZH=128, NH=384, LREP=128, RV0=16, RV1=16),
+    "float16": dict(LK0=128, LK1=128, RK0=16, RK1=16),
+    "uint16": dict(KREQ=16, RQ=32, RQA=32, L=96, LF=24, LS=24, LSA=24, M1=24, M2=24, VL=16),
 }
 SCRATCH = {b: ("sbuf", [128, w], d) for d in WIDTHS for b, w in WIDTHS[d].items()}
 SCRATCH["YS"] = ("sbuf", [8, 256], "float32")
 SCRATCH.update({"b%d" % i: ("psum", [128, 512], "float32") for i in range(8)})
-SEMAPHORES = ["vq", "tq", "aq", "rq", "tf", "ls", "ha", "aa", "l_rq", "l_tf", "l_ls", "l_ha", "l_aa", "sent",
-              "ld_rk", "ld_rt", "ld_hd", "ld_c", "ld_vv", "ld_ac", "ld_av", "st"] + ["k%d" % i for i in range(100)]
+SEMAPHORES = ["vq", "tq", "aq", "rq", "ra", "ls", "ha", "aa", "l_rq", "l_ra", "l_ls", "l_ha", "l_aa", "sent",
+              "ld_rk", "ld_rt", "ld_hd", "ld_c", "ld_vv", "ld_ac", "ld_av", "st"] + ["k%d" % i for i in range(120)]
 
 
 def queue(eng, own):
@@ -42,10 +44,14 @@ def wait(Q, *sigs):
             Q["seen"][s["k"]] = s["n"]
 
 
-def sync(Q):
+def sync_own(Q):
     if Q["n"] > Q["w"]:
         Q["e"].wait_ge(Q["own"], Q["n"])
         Q["w"] = Q["n"]
+
+
+def sync(Q):
+    sync_own(Q)
     wait(Q, *Q["p"])
     Q["p"].clear()
 
@@ -67,13 +73,13 @@ def rank_program(g, core, T, topo):
     GQ, SQ = {"e": g, "seen": {}}, {"e": g.sync, "seen": {}}
     v, pe, act = g.vector, g.tensor, g.scalar
 
-    def send3(src, dst_col, dst, rs, ls, counts):
+    def send3(src, dst, rs, ls, counts):
         first, trs = 0, []
         for i, q in enumerate(others):
             rid, pid, _ = topo.addr(T.cores[q])
             m = sum(1 << e for e in topo.engines(core, T.cores[q])[first:first + counts[i]])
             trs.append(RemoteDMATransfer(dst_ids=[DstId(rid=rid, pnc=pid)], dma_engine_mask=m, remote_sem=rs, src=src(q),
-                                         dst=dst[:, dst_col:dst_col + 8]))
+                                         dst=dst))
             first += counts[i]
         g.remote_dma_fused(trs, local_sem=ls)
 
@@ -91,19 +97,21 @@ def rank_program(g, core, T, topo):
     for k in range(8):
         load(g.sync if k % 2 == 0 else g.scalar, "ld_c", T.C[16 * k:16 * k + 8, 0:4096], T.vp[:, :])
 
-    s_pc, s_i, s_gh, s_j8, s_j16, s_jh = sig(), sig(), sig(), sig(), sig(), sig()
+    s_pc, s_i, s_sr, s_j8, s_i5, s_ot = sig(), sig(), sig(), sig(), sig(), sig()
 
-    def iota(out, pattern, cm, s, flag=True):
+    def iota(out, pattern, s, base=0, cm=0, flag=True):
         kw = {"allow_small_or_imprecise_dtypes": True} if flag else {}
-        g.iota(out, pattern, 0, cm, **kw).then_inc(s["s"], 1)
+        g.iota(out, pattern, base, cm, **kw).then_inc(s["s"], 1)
         s["n"] += 1
 
-    iota(T.PCI[:, :], [[0, 1]], 1, s_pc, False)
-    iota(T.I256[:, :], [[1, 256]], 0, s_i)
-    iota(T.J8[:, :], [[0, 48], [1, 8]], 0, s_j8)
-    iota(T.RGH[:, :], [[1, 16], [0, 8]], 0, s_gh)
-    iota(T.JH[:, :], [[0, 4], [1, 2], [0, 8]], 0, s_jh)
-    iota(T.J16[:, :], [[0, 24], [1, 16]], 0, s_j16)
+    iota(T.PCI[:, :], [[0, 1]], s_pc, 0, 1, False)
+    iota(T.I128[:, :], [[1, 128]], s_i)
+    iota(T.SR[:, :], [[1, 16], [16, 8]], s_sr, 512)
+    iota(T.J8[:, :], [[0, 48], [1, 8]], s_j8)
+    iota(T.I512[:, :], [[1, 512]], s_i5)
+    iota(T.RG[:, :], [[1, 8], [0, 16]], s_ot)
+    iota(T.R12[:, :], [[1, 6], [8, 2]], s_ot)
+    iota(T.JH[:, :], [[1, 2], [0, 8]], s_ot)
 
     def ts(out, in0, s1, op0, s2=None, op1=None, to=None):
         do(V, v.tensor_scalar(out, in0, s1, None, op0) if op1 is None else v.tensor_scalar(out, in0, s1, s2, op0, op1), to)
@@ -114,106 +122,98 @@ def rank_program(g, core, T, topo):
     def cp(out, in_, to=None):
         do(V, v.tensor_copy(out, in_), to)
 
-    s_one, s_sh = sig(), sig()
+    s_one, s_ge, s_sh, s_gp, s_kk = sig(), sig(), sig(), sig(), sig()
     do(V, v.memset(T.ONES[:, :], 1.0), s_one)
+    do(V, v.memset(T.NONES[:, :], -1.0), s_one)
+    do(V, v.memset(T.GE[:, 0:10:5], 1.0), s_ge)
+    do(V, v.memset(T.GE[:, 4:10:5], 0.0), s_ge)
     wait(V, s_pc)
     pb, pf = T.PBI, T.PFC
-    ts(pb[:, 0:1], T.PCI[:, :], 15, A.bitwise_and)
-    ts(pb[:, 1:2], T.PCI[:, :], 3, A.arith_shift_right)
-    ts(pb[:, 2:3], T.PCI[:, :], 3, A.arith_shift_right, 1, A.bitwise_and)
-    ts(pb[:, 3:4], T.PCI[:, :], 7, A.bitwise_and)
-    cp(pb[:, 4:5], T.PCI[:, :])
+    for i, a, b in ((0, 0, 15), (1, 3, 15), (2, 3, 1), (3, 0, 7), (4, 0, 127), (14, 4, 7)):
+        ts(pb[:, min(i, 5):min(i, 5) + 1], T.PCI[:, :], a, A.arith_shift_right, b, A.bitwise_and)
     sync(V)
     cp(pf[:, 0:5], pb[:, 0:5])
+    cp(pf[:, 14:15], pb[:, 5:6])
     sync(V)
     big = float(1048576)
-    ts(pf[:, 5:6], pf[:, 2:3], -1.0, A.mult, 1.0, A.add)
-    ts(pf[:, 6:7], pf[:, 4:5], 8.0, A.add)
-    ts(pf[:, 7:8], pf[:, 4:5], -8.0, A.add)
+    i128, p, hi, lo = T.I128[:, :], pf[:, 4:5], pf[:, 2:3], pf[:, 5:6]
+    wait(V, s_i)
+    ts(T.TRI[:, :], i128, p, A.is_gt)
+    ts(T.EYE[:, :], i128, p, A.is_equal, 512.0, A.mult)
+    ts(lo, hi, -1.0, A.mult, 1.0, A.add)
+    ts(pf[:, 6:7], p, 8.0, A.add)
+    ts(pf[:, 7:8], p, -8.0, A.add)
     ts(pf[:, 10:11], pf[:, 3:4], 2.0, A.mult)
     ts(pf[:, 11:12], pf[:, 3:4], 2.0, A.mult, 1.0, A.add)
     ts(pf[:, 12:13], pf[:, 3:4], 32.0, A.mult)
-    ts(pf[:, 13:14], pf[:, 2:3], big - 4096.0, A.mult, 4096.0, A.add)
-    wait(V, s_i)
-    ts(T.TRI[:, :], T.I256[:, 0:128], pf[:, 4:5], A.is_gt, to=s_one)
     sync(V)
+    tt(T.TRIP[:, :], T.TRI[:, :], T.EYE[:, :], A.add, s_one)
     tt(pf[:, 8:9], pf[:, 12:13], pf[:, 1:2], A.add)
-    i128, p, lo, hi = T.I256[:, 0:128], pf[:, 4:5], pf[:, 5:6], pf[:, 2:3]
-    ul, uh = [T.UL[:, 128 * i:128 * i + 128] for i in range(4)], [T.UH[:, 128 * i:128 * i + 128] for i in range(4)]
-    for out, at, role in ((T.SHHI[:, :], pf[:, 6:7], lo), (T.UPHF[:, :], p, hi), (T.SHLO[:, :], p, lo),
-                          (ul[3], pf[:, 7:8], hi), (uh[3], p, hi)):
-        ts(out, i128, at, A.is_equal, role, A.mult, to=s_sh)
+    for b in range(5):
+        ts(T.EXC[:, b:b + 1], lo, float(4096 + 512 * b) - big, A.mult, big, A.add)
     sync(V)
+    ts(T.TRIN[:, :], T.TRIP[:, :], -1.0, A.mult, to=s_one)
     ts(pf[:, 9:10], pf[:, 8:9], 16.0, A.add)
-    wait(V, s_j8)
-    ts(T.MASK8[:, :], T.J8[:, :], pf[:, 3:4], A.is_equal)
+    for out, at, role in ((T.SHHI, pf[:, 6:7], lo), (T.SHLO, p, lo), (T.UL, pf[:, 7:8], hi), (T.UH, p, hi)):
+        ts(out[:, :], i128, at, A.is_equal, role, A.mult, to=s_sh)
+    for rk in (T.RK0, T.RK1):
+        ts(rk[:, 3:16:4], i128[:, 0:4], 0.0, A.mult, to=s_kk)
 
+    s_pos, s_kp, s_kq, s_own, s_ef = (sig() for _ in range(5))
     v.wait_ge(T.sem.ld_rk, loads["ld_rk"])
-    ts(T.OWI[:, :], T.RKI[:, :], 11, A.arith_shift_right)
-    ts(T.KLO[:, :], T.RKI[:, :], 2047, A.bitwise_and)
     sync(V)
-    s_e, s_pos = sig(), sig()
-    for q in range(n_ranks):
-        ts(T.E[:, q:8:4], T.OWI[:, :], q, A.is_equal, to=s_e)
-    cp(T.OWF[:, :], T.OWI[:, :])
-    ts(T.OW8[:, :], T.OWI[:, :], 8.0, A.mult)
-    cp(T.KLF[:, :], T.KLO[:, :])
+    for q in range(1, n_ranks):
+        ts(T.GE[:, q:10:5], T.RKI[:, :], 2048 * q, A.is_ge, to=s_ge)
     v.wait_ge(T.sem.ld_rt, loads["ld_rt"])
-    cp(T.RTF[:, :], T.RTI[:, :])
-    wait(PE, s_one, s_e)
-    do(PE, pe.matmul(T.b0[:, 0:4], T.TRI[:, :], T.E[:, 0:4], True, True), s_pos)
-    pe.matmul(T.b0[:, 4:8], T.TRI[:, :], T.E[:, 4:8], True, False)
-    do(PE, pe.matmul(T.b0[:, 4:8], T.ONES[:, :], T.E[:, 0:4], False, True), s_pos)
-    sync(V)
-    wait(V, s_pos)
-    tt(T.Z[:, :], T.b0[:, 0:8], T.E[:, :], A.mult)
-    sync(V)
-    do(V, v.tensor_reduce(T.SLF[:, 0:1], T.Z[:, 0:4], AxisListType.X, A.add))
-    do(V, v.tensor_reduce(T.SLF[:, 1:2], T.Z[:, 4:8], AxisListType.X, A.add))
-    sync(V)
-    cp(T.SLI[:, :], T.SLF[:, :])
-    sync(V)
-    ts(T.GMI[:, 0:2], T.SLI[:, :], 15, A.bitwise_and)
-    ts(T.GMI[:, 2:4], T.SLI[:, :], 4, A.arith_shift_right)
-    sync(V)
-    cp(T.GMF[:, :], T.GMI[:, :])
-    sync(V)
-    wait(V, s_gh)
-    tt(T.MC[:, :], T.GMF[:, 2:4], T.OW8[:, :], A.add)
-    ts(T.K8[:, :], T.GMF[:, 0:2], 8.0, A.mult)
-    s_c0, s_c1, s_kk, s_kp, s_rq, s_own = sig(), sig(), sig(), sig(), sig(), sig()
-    ts(T.LT0[:, :], T.RGH[:, :], T.GMF[:, 0:1], A.is_equal, to=s_c0)
-    sync(V)
-    ts(T.RB0[:, :], T.I256[:, 0:32], T.MC[:, 0:1], A.is_equal, T.RTF[:, 0:1], A.mult, to=s_c0)
-    tt(T.KC[:, :], T.K8[:, :], T.GMF[:, 2:4], A.add)
-    ts(T.LT1[:, :], T.RGH[:, :], T.GMF[:, 1:2], A.is_equal, to=s_c1)
-    ts(T.RB1[:, :], T.I256[:, 0:32], T.MC[:, 1:2], A.is_equal, T.RTF[:, 1:2], A.mult, to=s_c1)
-    sync(V)
-    for x, lk, rk in ((0, T.LK0, T.RK0), (1, T.LK1, T.RK1)):
-        ts(lk[:, :], i128, T.KC[:, x:x + 1], A.is_equal, to=s_kk)
-        ts(rk[:, :], T.I256[:, 0:4], T.OWF[:, x:x + 1], A.is_equal, T.KLF[:, x:x + 1], A.mult, to=s_kk)
+    ts(T.KVI[:, 0:6:3], T.RKI[:, :], 2047, A.bitwise_and)
+    ts(T.KVI[:, 1:6:3], T.RTI[:, :], 10, A.arith_shift_right)
+    ts(T.KVI[:, 2:6:3], T.RTI[:, :], 1023, A.bitwise_and)
+    wait(PE, s_one, s_ge)
 
-    def mm2(out, l0, r0, l1, r1, to, *between):
-        pe.matmul(out, l0, r0, True, False)
-        wait(PE, *between)
-        do(PE, pe.matmul(out, l1, r1, False, True), to)
+    def mms(out, pairs, to):
+        for i, (a, b) in enumerate(pairs):
+            ins = pe.matmul(out, a, b, i == 0, i == len(pairs) - 1)
+        do(PE, ins, to)
 
-    wait(PE, s_c0)
-    mm2(T.b1[:, 0:32], T.LT0[:, :], T.RB0[:, :], T.LT1[:, :], T.RB1[:, :], s_kp, s_c1)
+    ge = [T.GE[:, i:i + 4] for i in (0, 1, 5, 6)]
+    mms(T.b0[:, 0:4], [(T.TRIP[:, :], ge[0]), (T.TRIN[:, :], ge[1])], s_pos)
+    mms(T.b0[:, 4:8], [(T.TRIP[:, :], ge[2]), (T.TRIN[:, :], ge[3]), (T.ONES[:, :], ge[0]), (T.NONES[:, :], ge[1])], s_pos)
+    sync(V)
+    cp(T.KVF[:, :], T.KVI[:, :], s_ef)
+    tt(T.EF[:, 0:4], ge[0], ge[1], A.subtract, s_ef)
+    tt(T.EF[:, 4:8], ge[2], ge[3], A.subtract, s_ef)
+    wait(V, s_pos, s_sr)
+    do(V, v.tensor_reduce(T.SLF[:, 0:1], T.b0[:, 0:4], AxisListType.X, A.max))
+    do(V, v.tensor_reduce(T.SLF[:, 1:2], T.b0[:, 4:8], AxisListType.X, A.max))
+    wait(V, s_ef)
+    for x, rk in ((0, T.RK0), (1, T.RK1)):
+        for i in range(3):
+            ts(rk[:, i:16:4], T.EF[:, 4 * x:4 * x + 4], T.KVF[:, 3 * x + i:3 * x + i + 1], A.mult, to=s_kk)
+    sync_own(V)
+    for x, lk in ((0, T.LK0), (1, T.LK1)):
+        ts(lk[:, :], T.SR[:, :], T.SLF[:, x:x + 1], A.is_equal, to=s_kk)
     wait(PE, s_kk)
-    mm2(T.b1[:, 6:32:8], T.LK0[:, :], T.RK0[:, :], T.LK1[:, :], T.RK1[:, :], s_kp)
-    sync(V)
+    mms(T.b1[:, 0:16], [(T.LK0[:, :], T.RK0[:, :]), (T.LK1[:, :], T.RK1[:, :])], s_kp)
     wait(V, s_kp)
-    cp(T.REQ[:, :], T.b1[:, 0:32], s_rq)
-    cp(T.RQ[:, 8 * r:8 * r + 8], T.b1[:, 8 * r:8 * r + 8], s_own)
-    wait(GQ, s_rq)
-    send3(lambda q: T.REQ[:, 8 * q:8 * q + 8], 8 * r, T.RQ, T.sem.rq, T.sem.l_rq, [2, 2, 2])
+    cp(T.KREQ[:, :], T.b1[:, 0:16], s_kq)
+    cp(T.RQ[:, 8 * r:8 * r + 4], T.b1[:, 4 * r:4 * r + 4], s_own)
+    cp(T.RQA[:, 8 * r:8 * r + 4], T.b1[:, 4 * prv:4 * prv + 4], s_own)
+    wait(GQ, s_kq)
+    send3(lambda q: T.KREQ[:, 4 * q:4 * q + 4], T.RQ[:, 8 * r:8 * r + 4], T.sem.rq, T.sem.l_rq, [2, 2, 2])
     g.sem_inc(T.sem.sent, 1)
 
-    s_rst, s_z = sig(), sig()
-    wait(S, s_j8, s_j16)
+    def of_archive(z):
+        q = (z - 1) % n_ranks
+        return T.KREQ[:, 4 * q:4 * q + 4]
+
+    send3(of_archive, T.RQA[:, 8 * r:8 * r + 4], T.sem.ra, T.sem.l_ra, [2, 2, 2])
+    s_j16, s_za = sig(), sig()
+    iota(T.J16[:, :], [[0, 8], [1, 16]], s_j16)
+    iota(T.AV[:, :], [[0, 2064]], s_za)
+
+    s_rst, s_z, s_m12 = sig(), sig(), sig()
+    wait(S, s_j8)
     do(S, act.activation(T.RST8[:, :], T.J8[:, :], F.Sign), s_rst)
-    do(S, act.activation(T.RST16[:, :], T.J16[:, :], F.Sign), s_rst)
     for b in range(0, 4104, 384):
         n = min(384, 4104 - b)
         do(S, act.activation(T.VV[:, b:b + n], T.J8[:, 0:n], F.Copy, scale=0.0), s_z)
@@ -227,238 +227,266 @@ def rank_program(g, core, T, topo):
     for k in range(8):
         load(ys, "ld_ac", T.AC[16 * k:16 * k + 8, 8:2056], T["ap"][:, :])
         load(ys, "ld_ac", T.AC[16 * k + 8:16 * k + 16, 8:2056], T["at"][:, :])
-    for k in range(16):
-        load(ys, "ld_av", T.AV[8 * k:8 * k + 8, 8:2056], T["av"][:, :])
+    wait(SQ, s_za)
+    for k in range(8):
+        load(ys, "ld_av", T.AV[16 * k:16 * k + 8, 8:2056], T["av"][:, :])
 
-    wait(V, s_jh, s_j16)
+    wait(V, s_j8, s_i5, s_ot)
     ts(T.MASKHD[:, :], T.JH[:, :], hi, A.is_equal)
-    ts(T.C[:, 4096:4104], T.I256[:, 0:8], 0.0, A.mult, pf[:, 13:14], A.add)
-    for i in range(3):
-        ts(ul[i], ul[3], float(8 >> i), A.mult, to=s_sh)
-        ts(uh[i], uh[3], float(8 >> i), A.mult, to=s_sh)
-    s_p4, s_pm, s_vl, s_mp, s_mk = sig(), sig(), sig(), sig(), sig()
-    ts(T.LREP[:, :], T.J16[:, 0:128], pf[:, 1:2], A.is_equal, to=s_p4)
-    for x, rv in ((0, T.RV0), (1, T.RV1)):
-        ts(rv[:, :], T.I256[:, 0:16], pf[:, 10 + x:11 + x], A.is_equal, T.MC[:, x:x + 1], A.mult, to=s_p4)
-    for x, pm in ((0, T.PERM0), (1, T.PERM1)):
-        ts(pm[:, :], T.I256[:, :], pf[:, 8 + x:9 + x], A.is_equal, to=s_pm)
-    wait(PE, s_p4)
-    mm2(T.b0[:, 0:16], T.LREP[:, :], T.RV0[:, :], T.LREP[:, :], T.RV1[:, :], s_vl)
-    wait(PE, s_pm)
-    mm2(T.b4[:, 0:256], T.LT0[:, :], T.PERM0[:, :], T.LT1[:, :], T.PERM1[:, :], s_mp)
-    wait(S, s_mp)
-    do(S, act.activation(T.MSK[:, :], T.b4[:, 0:256], F.Copy), s_mk)
-    ts(T.SEL[:, :], T.I256[:, 0:8], pf[:, 3:4], A.is_equal, to=s_p4)
-    for ap, c in ((T.AC[:, 0:8], 2048), (T.AC[:, 2056:2064], 2048), (T.AV[:, 0:8], 0.0), (T.AV[:, 2056:2064], 0.0),
-                  (T.HOUT[:, :], 0.0), (T.AOUT[:, :], 0.0), (T.CM[:, 0:24], 0.0)):
-        do(V, v.memset(ap, c))
-    ts(T.MASK16[:, :], T.J16[:, :], pf[:, 0:1], A.is_equal)
-    wait(V, s_vl)
-    cp(T.VL[:, :], T.b0[:, 0:16])
+    ts(T.M12[:, :], T.R12[:, :], pf[:, 0:1], A.is_equal, to=s_m12)
+    ts(T.GRP[:, :], T.RG[:, :], pf[:, 14:15], A.is_equal, to=s_gp)
+    ts(T.MASK8[:, :], T.J8[:, :], pf[:, 3:4], A.is_equal)
+    ts(T.ZL[:, :], T.UL[:, :], -8192.0, A.mult, to=s_sh)
+    ts(T.ZH[:, :], T.UH[:, :], -8192.0, A.mult, to=s_sh)
+    ts(T.UL2[:, :], T.UL[:, :], 2.0, A.mult, to=s_sh)
+    for b in range(5):
+        n = 512 if b < 4 else 8
+        ts(T.C[:, 4096 + 512 * b:4096 + 512 * b + n], T.I512[:, 0:n], lo, A.mult, T.EXC[:, b:b + 1], A.add)
+    do(V, v.memset(T.DC[:, :], 0.5))
     sync(V)
+    do(V, v.memset(T.DC[:, 0:96:4], -1.0))
+    do(V, v.memset(T.AC[:, 0:8], 2048))
+    do(V, v.memset(T.AC[:, 2056:2064], 2048))
 
     arrived = 2 * len(others)
-    act.wait_ge(T.sem.rq, arrived)
-    wait(S, s_own)
-    s_t24 = sig()
-    for q in range(n_ranks):
-        do(S, act.activation(T.T24[:, 6 * q:6 * q + 6], T.RQ[:, 8 * q:8 * q + 6], F.Copy), s_t24)
 
-    def spread(t24, bank, t48):
-        s1, s2 = sig(), sig()
-        do(PE, pe.matmul(bank[:, 0:24], T.SHHI[:, :], t24, True, True), s1)
-        do(PE, pe.matmul(bank[:, 24:48], T.UPHF[:, :], t24, True, True), s1)
-        wait(S, s1)
-        do(S, act.activation(t48[:, 0:48:2], bank[:, 0:24], F.Copy), s2)
-        do(S, act.activation(t48[:, 1:48:2], bank[:, 24:48], F.Copy), s2)
-        return s2
+    def halves(rq, th, tl):
+        ts(th[:, :], rq[:, 1:32:8], 1024.0, A.mult)
+        cp(tl[:, :], rq[:, 2:32:8])
 
-    wait(PE, s_sh, s_t24)
-    s_t48 = spread(T.T24[:, :], T.b6, T.T48)
-    rid, pid, _ = topo.addr(T.cores[nxt])
-    n8 = len(topo.engines(core, T.cores[nxt]))
+    def spread(tk, s_tk, tx, bank, t48):
+        s_tx, s_p, s_t = sig(), sig(), sig()
+        wait(S, s_tk, s_m12)
+        for q in range(n_ranks):
+            do(S, act.activation(tx[:, 12 * q:12 * q + 12], T.M12[:, :], F.Copy, scale=tk[:, q:q + 1]), s_tx)
+        wait(PE, s_sh, s_gp, s_tx)
+        mms(bank[:, 0:48], [(T.GRP[:, :], tx[:, :])], s_p)
+        wait(S, s_p)
+        do(S, act.activation(t48[:, :], bank[:, 0:48], F.Copy), s_t)
+        return s_t
 
-    def to_archive(dst, src, rs, ls):
-        g.remote_dma(out_ap=dst[:, :], in_ap=src[:, :], remote_sem=rs, local_sem=ls, pid=pid, routing_id=rid,
-                     dma_engine_mask=topo.mask(core, T.cores[nxt]))
+    def col(buf, k):
+        return buf[:, 24 * k:24 * k + 24]
 
-    wait(GQ, s_t24)
-    to_archive(T.T24A, T.T24, T.sem.tf, T.sem.l_tf)
-
-    nb, hb = [T.b1[:, 0:24], T.b2[:, 0:24]], [T.b5[:, 0:24], T.b3[:, 0:24]]
-    code = T.b3[:, 0:24]
-    W, X, ACC, PX, MX = T.W[:, 0:24], T.X[:, 0:24], T.ACC[:, :], T.PX[:, :], T.MX[:, :]
-
-    def col(buf, k, n=1):
-        return buf[:, 24 * k:24 * (k + n)]
-
+    nb = [T.b1[:, 0:24], T.b2[:, 0:24]]
+    s_tk, s_g0, s_ad = sig(), sig(), sig()
+    wait(V, s_own)
     v.wait_ge(T.sem.rq, arrived)
-    cp(T.KLI[:, :], T.RQ[:, 6:32:8])
-    sync(V)
     v.wait_ge(T.sem.ld_hd, loads["ld_hd"])
-    tt(T.G0[:, :], T.HD[:, :].indirect(T.KLI[:, 0:4]), T.MASKHD[:, :], A.mult)
     sync(V)
     for q in range(n_ranks):
-        tt(T.N0[:, 6 * q:6 * q + 6], T.G0[:, 16 * q:16 * q + 6], T.G0[:, 16 * q + 8:16 * q + 14], A.add)
+        tt(T.G0[:, 16 * q:16 * q + 16], T.HD[:, :].indirect(T.RQ[:, 8 * q:8 * q + 1]), T.MASKHD[:, :], A.mult, s_g0)
+    halves(T.RQ, T.TH, T.TL)
+    wait(V, s_g0)
+    for q in range(n_ranks):
+        tt(T.N0[:, 6 * q:6 * q + 6], T.G0[:, 16 * q:16 * q + 6], T.G0[:, 16 * q + 8:16 * q + 14], A.add, s_ad)
     sync(V)
-    ts(col(T.L, 0), T.N0[:, :], 4096.0, A.min)
+    cp(col(T.L, 0), T.N0[:, :])
+    tt(T.TK[:, :], T.TH[:, :], T.TL[:, :], A.add, s_tk)
+    s_t48 = spread(T.TK, s_tk, T.TX, T.b6, T.T48)
 
-    def fetch(win, lst, mask, rst, to):
-        sync(V)
-        tt(T.G[:, :], win.indirect(lst), mask[:, :], A.mult)
-        sync(V)
-        do(V, v.tensor_tensor_scan(T.S[:, :], rst[:, :], T.G[:, :], 0.0, A.mult, A.add), to)
+    def gather(out, win, lst, to=None):
+        tt(out[:, :], win[:, :].indirect(lst), T.MASK8[:, :], A.mult, to)
 
-    def follow(out, s_in):
-        s = sig()
-        wait(PE, s_in)
-        mm2(out, T.SHLO[:, :], T.S[:, 7:384:16], T.SHHI[:, :], T.S[:, 15:384:16], s)
-        return s
+    def scan(out, data, to=None):
+        do(V, v.tensor_tensor_scan(out[:, :], T.RST8[:, :], data[:, :], 0.0, A.mult, A.add), to)
 
-    def judge(out, k, t48, weight, start, stop):
-        s1, s2 = sig(), sig()
-        sync(V)
-        a, z = 48 * k, 48 * k + 48
-        tt(T.NH[:, a:z], T.S[:, 7:384:8], t48, A.is_le, s1)
-        wait(PE, s1)
-        pe.matmul(out, ul[weight], T.NH[:, a:z:2], start, False)
-        ins = pe.matmul(out, uh[weight], T.NH[:, a + 1:z:2], False, stop)
-        if stop:
-            do(PE, ins, s2)
-        return s2
+    def shift(s):
+        return [(T.SHLO[:, :], s[:, 7:384:16]), (T.SHHI[:, :], s[:, 15:384:16])]
+
+    def judge(k, s, t48):
+        done = sig()
+        tt(T.NH[:, 48 * k:48 * k + 48], s[:, 7:384:8], t48[:, :], A.is_le, done)
+        wait(PE, done)
+
+    z, s_zz, s_hh, s_p4, s_pm = T.b3[:, 0:24], sig(), sig(), sig(), sig()
+    ss = [T.S0, T.S1]
+
+    def tally(k):
+        wait(V, s_t48)
+        judge(k, ss[k % 2], T.T48)
+        even, odd = T.NH[:, 48 * k:48 * k + 48:2], T.NH[:, 48 * k + 1:48 * k + 48:2]
+        pe.matmul(z, T.ZL[:, :], even, k == 0, False)
+        ins = pe.matmul(z, T.ZH[:, :], odd, False, k == 3)
+        if k == 3:
+            do(PE, ins, s_zz)
+        mms(T.b5[:, 3 - k:96:4], [(T.UL[:, :], even), (T.UH[:, :], odd)], s_hh)
+
+    def other_work(k):
+        if k == 0:
+            wait(V, s_j16)
+            cp(T.SLI[:, :], T.SLF[:, :])
+            ts(T.OWI[:, :], T.RKI[:, :], 11, A.arith_shift_right)
+            ts(T.LREP[:, :], T.J16[:, :], pf[:, 1:2], A.is_equal, to=s_p4)
+            ts(T.SEL[:, :], T.I128[:, 0:8], pf[:, 0:1], A.is_equal, to=s_p4)
+        elif k == 1:
+            ts(T.GMI[:, 0:2], T.SLI[:, :], 1, A.arith_shift_right, 7, A.bitwise_and)
+            ts(T.GMI[:, 2:4], T.SLI[:, :], 3, A.arith_shift_right, 62, A.bitwise_and)
+            ts(T.GMI[:, 4:6], T.SLI[:, :], 1, A.bitwise_and)
+            ts(T.OW12[:, :], T.OWI[:, :], 12.0, A.mult)
+            ts(T.PERM0[:, :], T.I512[:, 0:256], pf[:, 8:9], A.is_equal, to=s_pm)
+        elif k == 2:
+            cp(T.GMF[:, :], T.GMI[:, :])
+            ts(T.PERM1[:, :], T.I512[:, 0:256], pf[:, 9:10], A.is_equal, to=s_pm)
 
     wait(V, s_rst)
-    sync(V)
-    v.wait_ge(T.sem.ld_c, loads["ld_c"])
     for k in range(4):
-        s_s = sig()
-        fetch(T.C[:, :], col(T.L, k), T.MASK8, T.RST8, s_s)
-        s_n = follow(nb[k % 2], s_s)
-        wait(V, s_t48)
-        s_h = judge(code, k, T.T48[:, :], k, k == 0, k == 3)
+        s_g, s_s, s_n = sig(), sig(), sig()
+        sync(V)
+        if k == 0:
+            v.wait_ge(T.sem.ld_c, loads["ld_c"])
+        gather(T.G, T.C, col(T.L, k), s_g)
+        ts(T.NL[:, 3 - k:96:4], col(T.L, k), 8.0, A.add)
         if k:
-            tt(MX, T.N0[:, :] if k == 1 else MX, nb[(k - 1) % 2], A.max)
-        wait(V, s_n)
+            tally(k - 1)
+        wait(V, s_g)
+        scan(ss[k % 2], T.G, s_s)
+        wait(PE, s_s)
         if k < 3:
-            ts(col(T.L, k + 1), nb[k % 2], 4096.0, A.min)
-    sync(V)
-    tt(MX, MX, nb[1], A.max)
-    wait(V, s_h)
-    ts(W, code, 0.0, A.is_equal)
-    sync(V)
-    tt(PX, W, MX, A.mult)
-    sync(V)
+            mms(nb[k % 2], shift(ss[k % 2]), s_n)
+            other_work(k)
+            wait(V, s_n)
+            cp(col(T.L, k + 1), nb[k % 2])
+        else:
+            for a, b in shift(ss[1]):
+                pe.matmul(z, a, b, False, False)
+            wait(V, s_s)
+            tally(3)
+    ts(T.LT0[:, :], T.RG[:, :], T.GMF[:, 0:1], A.is_equal, to=s_pm)
+    ts(T.LT1[:, :], T.RG[:, :], T.GMF[:, 1:2], A.is_equal, to=s_pm)
+    tt(T.MA[:, :], T.GMF[:, 2:4], T.GMF[:, 4:6], A.add)
     s_ls = sig()
-    ts(T.LS[:, :], PX, -4088.0, A.add, 0.0, A.max, to=s_ls)
+    wait(V, s_zz)
+    ts(T.LS[:, :], z, -4088.0, A.add, 0.0, A.max, to=s_ls)
+    rid, pid, _ = topo.addr(T.cores[nxt])
+    n8 = len(topo.engines(core, T.cores[nxt]))
     wait(GQ, s_ls)
-    to_archive(T.LSA, T.LS, T.sem.ls, T.sem.l_ls)
+    g.remote_dma(out_ap=T.LSA[:, :], in_ap=T.LS[:, :], remote_sem=T.sem.ls, local_sem=T.sem.l_ls, pid=pid, routing_id=rid,
+                 dma_engine_mask=topo.mask(core, T.cores[nxt]))
 
-    for k in range(4):
-        ts(col(T.CM, k + 1), code, float(8 >> k), A.is_ge)
-    ts(T.NL[:, :], T.L[:, :], 8.0, A.add)
+    s_ho, s_vl, s_mp, s_mk, s_tka = (sig() for _ in range(5))
+    wait(PE, s_pm)
+    mms(T.b4[:, 0:256], [(T.LT0[:, :], T.PERM0[:, :]), (T.LT1[:, :], T.PERM1[:, :])], s_mp)
+    wait(S, s_mp)
+    do(S, act.activation(T.MSK[:, :], T.b4[:, 0:256], F.Copy), s_mk)
+    wait(V, s_hh)
     sync(V)
-    tt(T.W[:, :], col(T.CM, 1, 4), col(T.CM, 0, 4), A.subtract)
+    tt(T.HP[:, :], T.b5[:, 0:96], T.NL[:, :], A.mult)
+    tt(T.D0[:, :], T.b5[:, 0:96], T.DC[:, :], A.is_lt)
+    tt(T.MC[:, :], T.MA[:, :], T.OW12[:, :], A.add)
     sync(V)
-    tt(T.X[:, :], T.W[:, :], T.NL[:, :], A.mult)
+    do(V, v.tensor_tensor_scan(T.HS[:, :], T.D0[:, :], T.HP[:, :], 0.0, A.mult, A.add))
+    for x, rv in ((0, T.RV0), (1, T.RV1)):
+        ts(rv[:, :], T.I128[:, 0:16], pf[:, 10 + x:11 + x], A.is_equal, T.MC[:, x:x + 1], A.mult, to=s_p4)
     sync(V)
-    tt(col(T.W, 0, 2), col(T.X, 0, 2), col(T.X, 2, 2), A.add)
-    sync(V)
-    tt(ACC, col(T.W, 0), col(T.W, 1), A.add)
-    sync(V)
-    cp(T.LF[:, :], ACC)
+    wait(PE, s_p4)
+    mms(T.b0[:, 0:16], [(T.LREP[:, :], T.RV0[:, :]), (T.LREP[:, :], T.RV1[:, :])], s_vl)
+    cp(T.LF[:, :], T.HS[:, 3:96:4])
+    v.wait_ge(T.sem.ra, arrived)
+    halves(T.RQA, T.THA, T.TLA)
     sync(V)
     v.wait_ge(T.sem.ld_vv, loads["ld_vv"])
-    s_s, s_ho = sig(), sig()
-    fetch(T.VV[:, :], T.LF[:, 0:24], T.MASK8, T.RST8, s_s)
-    s_v = follow(T.b6[:, 0:24], s_s)
+    gather(T.G, T.VV, T.LF[:, 0:24])
+    tt(T.TKA[:, :], T.THA[:, :], T.TLA[:, :], A.add, s_tka)
     sync(V)
-    wait(V, s_v)
-    cp(T.HOUT[:, 0:24], T.b6[:, 0:24], s_ho)
+    scan(T.S0, T.G)
     sync(V)
+    cp(T.HOUT[:, :], T.S0[:, 7:384:8], s_ho)
     wait(GQ, s_ho)
-    send3(lambda q: T.HOUT[:, 6 * q:6 * q + 8], 8 * r, T.ANSH, T.sem.ha, T.sem.l_ha, [4, 2, 2])
-    cp(T.ANSH[:, 8 * r:8 * r + 8], T.HOUT[:, 6 * r:6 * r + 8])
-
-    pe.wait_ge(T.sem.tf, n8)
-    s_t48a = spread(T.T24A[:, :], T.b7, T.T48A)
+    send3(lambda q: T.HOUT[:, 12 * q:12 * q + 12], T.ANSH[:, 12 * r:12 * r + 12], T.sem.ha, T.sem.l_ha, [4, 2, 2])
+    s_t48a = spread(T.TKA, s_tka, T.TXA, T.b7, T.T48A)
+    wait(V, s_ho)
+    cp(T.ANSH[:, 12 * r:12 * r + 12], T.HOUT[:, 12 * r:12 * r + 12])
 
     sync(V)
     v.wait_ge(T.sem.ls, n8)
     v.wait_ge(T.sem.ld_ac, loads["ld_ac"])
-    ml = [T.LSA, T.M1, T.M2]
-    s_hs = []
+    ml, vals = [T.LSA, T.M1, T.M2], [T.V0, T.V1, T.V2]
+    p01, h2 = T.b3[:, 0:48], T.b5[:, 0:48]
+    ends = slice(7, 384, 8)
+    s_01, s_h2, s_va, s_a, s_px, s_x2 = (sig() for _ in range(6))
     for k in range(3):
-        s_s = sig()
-        fetch(T.AC[:, :], ml[k][:, 0:24], T.MASK8, T.RST8, s_s)
+        s_g, s_ga, s_s, s_n = sig(), sig(), sig(), sig()
+        places = ml[k][:, 0:24]
+        hits = T.NH[:, 48 * (4 + k):48 * (5 + k)]
+        if k == 2:
+            wait(V, s_01)
+            ts(T.Z[:, :], p01, 0.0, A.is_equal)
+            ts(T.W1[:, :], p01, 1.0, A.is_equal)
+            ts(T.W0[:, :], p01, 2.0, A.is_ge)
+        sync(V)
+        gather(T.G, T.AC, places, s_g)
         if k < 2:
-            s_n = follow(nb[k % 2], s_s)
-        wait(V, s_t48a)
-        s_hs.append(judge(hb[k % 2], 4 + k, T.T48A[:, :], 3, True, True))
-        if k == 0:
-            cp(col(T.NL, 0), T.LSA[:, :])
-        elif k == 1:
-            ts(col(T.NL, 1), nb[0], 8.0, A.add)
-            wait(V, s_hs[0])
-            tt(ACC, hb[0], col(T.NL, 0), A.mult)
-            ts(col(T.NF, 0), hb[0], -1.0, A.mult, 1.0, A.add)
-        else:
-            ts(col(T.NL, 2), nb[1], 8.0, A.add)
-            wait(V, s_hs[1])
-            tt(W, col(T.NF, 0), hb[1], A.mult)
-            sync(V)
-            tt(col(T.NF, 1), col(T.NF, 0), W, A.subtract)
-            tt(X, W, col(T.NL, 1), A.mult)
-            sync(V)
-            tt(ACC, ACC, X, A.add)
-            tt(PX, col(T.NF, 1), col(T.NL, 2), A.mult)
-            sync(V)
-        if k < 2:
+            wait(V, s_g)
+            scan(T.S0, T.G, s_s)
+            wait(PE, s_s)
+            mms(nb[k % 2], shift(T.S0), s_n)
+            if k == 0:
+                v.wait_ge(T.sem.ld_av, loads["ld_av"])
+            gather(T.GA, T.AV, places, s_ga)
+            wait(V, s_t48a, s_s)
+            judge(4 + k, T.S0, T.T48A)
+            ins = pe.matmul(p01, (T.UL2, T.UL)[k][:, :], hits, k == 0, k == 1)
+            if k == 1:
+                do(PE, ins, s_01)
+            wait(V, s_ga)
+            scan(vals[k], T.GA)
             wait(V, s_n)
             ts(ml[k + 1][:, :], nb[k % 2], 8.0, A.add)
-    wait(V, s_hs[2])
-    tt(X, hb[0], PX, A.mult)
-    sync(V)
-    tt(ACC, ACC, X, A.add)
-    sync(V)
-    cp(T.MF[:, :], ACC)
-    sync(V)
-    v.wait_ge(T.sem.ld_av, loads["ld_av"])
-    fetch(T.AV[:, :], T.MF[:, 0:24], T.MASK16, T.RST16, None)
-    sync(V)
+        else:
+            gather(T.GA, T.AV, places, s_ga)
+            wait(V, s_g)
+            scan(T.S0, T.G, s_s)
+            wait(V, s_ga)
+            scan(T.V2, T.GA, s_va)
+            wait(V, s_s)
+            judge(6, T.S0, T.T48A)
+            mms(h2, [(T.UL[:, :], hits)], s_h2)
+            tt(T.A0[:, :], T.W0[:, :], T.V0[:, ends], A.mult, s_a)
+            tt(T.A1[:, :], T.W1[:, :], T.V1[:, ends], A.mult, s_a)
+            wait(V, s_va)
+            tt(T.PX[:, :], T.Z[:, :], T.V2[:, ends], A.mult, s_px)
+            wait(V, s_a)
+            tt(T.ACC[:, :], T.A0[:, :], T.A1[:, :], A.add, s_x2)
     s_ao = sig()
-    cp(T.AOUT[:, 0:24], T.S[:, 15:384:16], s_ao)
-    sync(V)
+    wait(V, s_h2, s_px)
+    tt(T.X[:, :], h2, T.PX[:, :], A.mult, s_x2)
+    wait(V, s_x2)
+    tt(T.AOUT[:, :], T.ACC[:, :], T.X[:, :], A.add, s_ao)
     wait(GQ, s_ao)
-    send3(lambda q: T.AOUT[:, 6 * q:6 * q + 8], 8 * prv, T.ANSA, T.sem.aa, T.sem.l_aa, [4, 2, 2])
-    cp(T.ANSA[:, 8 * prv:8 * prv + 8], T.AOUT[:, 6 * r:6 * r + 8])
+    send3(lambda q: T.AOUT[:, 12 * q:12 * q + 12], T.ANSA[:, 12 * prv:12 * prv + 12], T.sem.aa, T.sem.l_aa, [4, 2, 2])
 
+    wait(V, s_vl)
+    cp(T.VL[:, :], T.b0[:, 0:16])
     landed = sum((4, 2, 2)[[o for o in range(n_ranks) if o != q].index(r)] for q in others)
     s_xh, s_x = sig(), [sig(), sig()]
     s_y, s_ys = [sig(), sig()], [sig(), sig()]
     sync(V)
+    cp(T.ANSA[:, 12 * prv:12 * prv + 12], T.AOUT[:, 12 * r:12 * r + 12])
     wait(V, s_mk)
     v.wait_ge(T.sem.ha, landed)
     tt(T.XH[:, :], T.ANSH[:, :].indirect(T.VL[:, 0:16]), T.MSK[:, :], A.mult, s_xh)
+    sync(V)
     v.wait_ge(T.sem.aa, landed)
-    wait(PE, s_p4, s_xh)
-    half = [slice(0, 128), slice(128, 256)]
+    wait(PE, s_xh)
+    part = [slice(0, 128), slice(128, 256)]
     bank = [T.b6[0:8, 0:128], T.b7[0:8, 0:128]]
     for i in range(2):
-        tt(T.XA[:, half[i]], T.ANSA[:, :].indirect(T.VL[:, 8 * i:8 * i + 8]), T.MSK[:, half[i]], A.mult, s_x[i])
-        pe.matmul(bank[i], T.SEL[:, :], T.XH[:, half[i]], True, False)
+        tt(T.XA[:, part[i]], T.ANSA[:, :].indirect(T.VL[:, 8 * i:8 * i + 8]), T.MSK[:, part[i]], A.mult, s_x[i])
+        pe.matmul(bank[i], T.SEL[:, :], T.XH[:, part[i]], True, False)
     for i in range(2):
         wait(PE, s_x[i])
-        do(PE, pe.matmul(bank[i], T.SEL[:, :], T.XA[:, half[i]], False, True), s_y[i])
+        do(PE, pe.matmul(bank[i], T.SEL[:, :], T.XA[:, part[i]], False, True), s_y[i])
     wait(S, s_y[0])
-    do(S, act.activation(T.YS[:, half[0]], bank[0], F.Copy), s_ys[0])
+    do(S, act.activation(T.YS[:, part[0]], bank[0], F.Copy), s_ys[0])
     sync(S)
-    g.scalar.dma_start(T.y[:, half[0]], T.YS[:, half[0]]).then_inc(T.sem.st, 16)
+    g.scalar.dma_start(T.y[:, part[0]], T.YS[:, part[0]]).then_inc(T.sem.st, 16)
     wait(V, s_y[1])
-    cp(T.YS[:, half[1]], bank[1], s_ys[1])
+    cp(T.YS[:, part[1]], bank[1], s_ys[1])
     wait(SQ, s_ys[1])
-    g.sync.dma_start(T.y[:, half[1]], T.YS[:, half[1]]).then_inc(T.sem.st, 16)
+    g.sync.dma_start(T.y[:, part[1]], T.YS[:, part[1]]).then_inc(T.sem.st, 16)
     sync(V)
     sync(PE)
     g.sync.wait_ge(T.sem.st, 32)
-    for s, n in ((T.sem.l_rq, 6), (T.sem.l_tf, n8), (T.sem.l_ls, n8), (T.sem.l_ha, 8), (T.sem.l_aa, 8)):
+    for s, n in ((T.sem.l_rq, 6), (T.sem.l_ra, 6), (T.sem.l_ls, n8), (T.sem.l_ha, 8), (T.sem.l_aa, 8)):
         g.wait_ge(s, n)

@@ -3,23 +3,25 @@ from concourse.bass import DstId, RemoteDMATransfer
 from concourse.mybir import AluOpType as A, AxisListType, ActivationFunctionType as F
 
 WIDTHS = {
-    "int32": dict(RKI=2, RTI=2, PCI=1, PBI=8, OWI=2, KVI=6, SLI=2, GMI=6, HD=2048, C=6152, AC=2064),
-    "float32": dict(PFC=16, EXC=8, I128=128, I512=512, RG=128, SR=128, J8=384, J16=128, JH=16, R12=12, M12=12, OW12=2,
-                    KVF=6, SLF=2, GMF=6, MA=2, MC=2, EF=8, LT0=128, LT1=128, TH=4, TL=4, TK=4, THA=4, TLA=4, TKA=4, TX=48,
-                    TXA=48, GRP=128, SHLO=128, SHHI=128, MASKHD=16, MASK8=384, RST8=384, VV=4104, AV=2064, G0=64, N0=24,
-                    G=384, S0=384, S1=384, GA=384, V0=384, V1=384, V2=384, T48=48, T48A=48, NL=96, DC=96, D0=96, HP=96,
-                    HS=96, Z=48, W0=48, W1=48, A0=48, A1=48, X=48, ACC=48, PX=48, HOUT=48, AOUT=48, ANSH=48, ANSA=48,
-                    PERM0=256, PERM1=256, MSK=256, SEL=8, XH=256, XA=256),
+    "int32": dict(RKI=2, RTI=2, PCI=1, PBI=8, OWI=2, KVI=6, SLI=2, GMI=4, HD=2048, C=6152, DI=128, ATC=128, APC=128),
+    "float32": dict(PFC=20, EXC=8, I128=128, I512=512, RG=128, SR=128, J8=384, J16=128, JH=16, R12=12, M12=12, OW12=2,
+                    KVF=6, SLF=2, GMF=4, MC=2, EF=8, TM=24, TX=48, TXA=48, GRP=128, GRPA=128, SHLO=128, SHHI=128, SC0=128,
+                    SC1=128, IDF=128, MASKHD=16, MASK8=384, RST8=384, VV=4104, FW=2064, F1=2048, RAW=2064, LV1=2064,
+                    LV2=2064, DF=128, D2=128, TCF=128, APF=128, G0=64, N0=24, G=384, GB=384, GD=384, S0=384, S1=384,
+                    V0=384, V1=384, V2=384, NL=96, DC=96, D0=96, HP=96, HS=96, WK=384, HOUT=48, AOUT=48, ANSH=48, ANSA=48,
+                    MSK=512, SEL=8, SELA=8, XH=256, XA=256),
     "bfloat16": dict(TRI=128, EYE=128, TRIP=128, TRIN=128, ONES=128, NONES=128, GE=10, UL=128, UH=128, UL2=128,
-                     ZL=128, ZH=128, NH=384, LREP=128, RV0=16, RV1=16),
+                     ZL=128, ZH=128, NH=384, LREP=128, RV0=16, RV1=16, LT0=128, LT1=128, LTA0=128, LTA1=128,
+                     PERM0=256, PERM1=256),
     "float16": dict(LK0=128, LK1=128, RK0=16, RK1=16),
-    "uint16": dict(KREQ=16, RQ=32, RQA=32, L=96, LF=24, LS=24, LSA=24, M1=24, M2=24, VL=16),
+    "uint16": dict(KREQ=16, RQ=32, RQA=32, L=96, LF=24, LS=24, LSA=24, VL=16, L1=128, L2=128),
 }
 SCRATCH = {b: ("sbuf", [128, w], d) for d in WIDTHS for b, w in WIDTHS[d].items()}
 SCRATCH["YS"] = ("sbuf", [8, 256], "float32")
 SCRATCH.update({"b%d" % i: ("psum", [128, 512], "float32") for i in range(8)})
 SEMAPHORES = ["vq", "tq", "aq", "rq", "ra", "ls", "ha", "aa", "l_rq", "l_ra", "l_ls", "l_ha", "l_aa", "sent",
-              "ld_rk", "ld_rt", "ld_hd", "ld_c", "ld_vv", "ld_ac", "ld_av", "st"] + ["k%d" % i for i in range(120)]
+              "ld_rk", "ld_rt", "ld_hd", "ld_c", "ld_vv", "ld_d", "ld_at", "ld_fw", "ld_av", "ld_d2", "st"]
+SEMAPHORES += ["k%d" % i for i in range(120)]
 
 
 def queue(eng, own):
@@ -89,8 +91,13 @@ def rank_program(g, core, T, topo):
         q.dma_start(out, in_).then_inc(T.sem[name], 16)
         loads[name] = loads.get(name, 0) + 16
 
+    ap, at, av = T["ap"], T["at"], T["av"]
     load(g.sync, "ld_rk", T.RKI[:, :], T.rk[:, :])
     load(g.scalar, "ld_rt", T.RTI[:, :], T.rt[:, :])
+    load(g.scalar, "ld_at", T.ATC[:, :], at[:, :])
+    load(g.sync, "ld_at", T.APC[:, :], ap[:, :])
+    for c in range(8):
+        load((g.sync, g.scalar)[c % 2], "ld_d", T.DI[:, 16 * c:16 * c + 16], ap[c:c + 1, :])
     for k in range(8):
         load(g.sync, "ld_hd", T.HD[16 * k:16 * k + 8, :], T.hd[:, :])
         load(g.scalar, "ld_hd", T.HD[16 * k + 8:16 * k + 16, :], T.hd[:, :])
@@ -106,7 +113,7 @@ def rank_program(g, core, T, topo):
 
     iota(T.PCI[:, :], [[0, 1]], s_pc, 0, 1, False)
     iota(T.I128[:, :], [[1, 128]], s_i)
-    iota(T.SR[:, :], [[1, 16], [16, 8]], s_sr, 512)
+    iota(T.SR[:, :], [[1, 8], [8, 2], [16, 8]], s_sr, 512)
     iota(T.J8[:, :], [[0, 48], [1, 8]], s_j8)
     iota(T.I512[:, :], [[1, 512]], s_i5)
     iota(T.RG[:, :], [[1, 8], [0, 16]], s_ot)
@@ -122,7 +129,7 @@ def rank_program(g, core, T, topo):
     def cp(out, in_, to=None):
         do(V, v.tensor_copy(out, in_), to)
 
-    s_one, s_ge, s_sh, s_gp, s_kk = sig(), sig(), sig(), sig(), sig()
+    s_one, s_ge, s_sh, s_gp, s_gpa, s_kk, s_id, s_eb, s_zl, s_u2 = (sig() for _ in range(10))
     do(V, v.memset(T.ONES[:, :], 1.0), s_one)
     do(V, v.memset(T.NONES[:, :], -1.0), s_one)
     do(V, v.memset(T.GE[:, 0:10:5], 1.0), s_ge)
@@ -146,16 +153,20 @@ def rank_program(g, core, T, topo):
     ts(pf[:, 10:11], pf[:, 3:4], 2.0, A.mult)
     ts(pf[:, 11:12], pf[:, 3:4], 2.0, A.mult, 1.0, A.add)
     ts(pf[:, 12:13], pf[:, 3:4], 32.0, A.mult)
+    ts(pf[:, 13:14], pf[:, 3:4], 16.0, A.mult, pf[:, 14:15], A.add)
     sync(V)
     tt(T.TRIP[:, :], T.TRI[:, :], T.EYE[:, :], A.add, s_one)
     tt(pf[:, 8:9], pf[:, 12:13], pf[:, 1:2], A.add)
+    ts(pf[:, 15:16], pf[:, 13:14], 8.0, A.add)
+    ts(pf[:, 16:17], hi, big, A.mult, to=s_eb)
+    ts(pf[:, 17:18], hi, -8192.0, A.mult)
     for b in range(5):
         ts(T.EXC[:, b:b + 1], lo, float(4096 + 512 * b) - big, A.mult, big, A.add)
     sync(V)
     ts(T.TRIN[:, :], T.TRIP[:, :], -1.0, A.mult, to=s_one)
     ts(pf[:, 9:10], pf[:, 8:9], 16.0, A.add)
-    for out, at, role in ((T.SHHI, pf[:, 6:7], lo), (T.SHLO, p, lo), (T.UL, pf[:, 7:8], hi), (T.UH, p, hi)):
-        ts(out[:, :], i128, at, A.is_equal, role, A.mult, to=s_sh)
+    for out, col_, role in ((T.SHHI, pf[:, 6:7], lo), (T.SHLO, p, lo), (T.UL, pf[:, 7:8], hi), (T.UH, p, hi)):
+        ts(out[:, :], i128, col_, A.is_equal, role, A.mult, to=s_sh)
     for rk in (T.RK0, T.RK1):
         ts(rk[:, 3:16:4], i128[:, 0:4], 0.0, A.mult, to=s_kk)
 
@@ -182,6 +193,7 @@ def rank_program(g, core, T, topo):
     cp(T.KVF[:, :], T.KVI[:, :], s_ef)
     tt(T.EF[:, 0:4], ge[0], ge[1], A.subtract, s_ef)
     tt(T.EF[:, 4:8], ge[2], ge[3], A.subtract, s_ef)
+    ts(T.IDF[:, :], i128, p, A.is_equal, to=s_id)
     wait(V, s_pos, s_sr)
     do(V, v.tensor_reduce(T.SLF[:, 0:1], T.b0[:, 0:4], AxisListType.X, A.max))
     do(V, v.tensor_reduce(T.SLF[:, 1:2], T.b0[:, 4:8], AxisListType.X, A.max))
@@ -194,6 +206,8 @@ def rank_program(g, core, T, topo):
         ts(lk[:, :], T.SR[:, :], T.SLF[:, x:x + 1], A.is_equal, to=s_kk)
     wait(PE, s_kk)
     mms(T.b1[:, 0:16], [(T.LK0[:, :], T.RK0[:, :]), (T.LK1[:, :], T.RK1[:, :])], s_kp)
+    for out, col_ in ((T.SC0, 13), (T.SC1, 15)):
+        ts(out[:, :], i128, pf[:, col_:col_ + 1], A.is_equal, lo, A.mult, to=s_sh)
     wait(V, s_kp)
     cp(T.KREQ[:, :], T.b1[:, 0:16], s_kq)
     cp(T.RQ[:, 8 * r:8 * r + 4], T.b1[:, 4 * r:4 * r + 4], s_own)
@@ -207,63 +221,71 @@ def rank_program(g, core, T, topo):
         return T.KREQ[:, 4 * q:4 * q + 4]
 
     send3(of_archive, T.RQA[:, 8 * r:8 * r + 4], T.sem.ra, T.sem.l_ra, [2, 2, 2])
-    s_j16, s_za = sig(), sig()
+    s_j16 = sig()
     iota(T.J16[:, :], [[0, 8], [1, 16]], s_j16)
-    iota(T.AV[:, :], [[0, 2064]], s_za)
 
-    s_rst, s_z, s_m12 = sig(), sig(), sig()
+    s_rst, s_z, s_zf, s_df, s_cf, s_l1p, s_l1, s_re, s_le = (sig() for _ in range(9))
     wait(S, s_j8)
     do(S, act.activation(T.RST8[:, :], T.J8[:, :], F.Sign), s_rst)
-    for b in range(0, 4104, 384):
-        n = min(384, 4104 - b)
-        do(S, act.activation(T.VV[:, b:b + n], T.J8[:, 0:n], F.Copy, scale=0.0), s_z)
+
+    def fill(buf, width, s, bias=0.0):
+        for b in range(0, width, 384):
+            n = min(384, width - b)
+            do(S, act.activation(buf[:, b:b + n], T.J8[:, 0:n], F.Copy, bias=bias, scale=0.0), s)
+
+    fill(T.FW, 2064, s_zf, 2056.0)
+    fill(T.VV, 4104, s_z)
+    wait(S, s_eb)
+    for buf, s in ((T.RAW, s_re), (T.LV1, s_le), (T.LV2, s_le)):
+        for a in (0, 2056):
+            do(S, act.activation(buf[:, a:a + 8], T.J8[:, 0:8], F.Identity, bias=pf[:, 16:17], scale=0.0), s)
+
+    wait(V, s_j8, s_i5, s_ot)
+    v.wait_ge(T.sem.ld_d, loads["ld_d"])
+    v.wait_ge(T.sem.ld_at, loads["ld_at"])
+    ts(T.DF[:, :], T.DI[:, :], 8.0, A.add, to=s_df)
+    ts(T.APF[:, :], T.APC[:, :], 8.0, A.add, to=s_cf)
+    cp(T.TCF[:, :], T.ATC[:, :], s_cf)
+    wait(PE, s_df, s_id)
+    mms(T.b7[:, 0:128], [(T.DF[:, :], T.IDF[:, :])], s_l1p)
+
     ys = g.sync
     ys.wait_ge(T.sem.sent, 1)
     for k in range(8):
         load(ys, "ld_c", T.C[16 * k + 8:16 * k + 16, 0:4096], T.vt[:, :])
+    wait(SQ, s_cf, s_zf)
+    load(ys, "ld_fw", T.FW[0:128:16, 8:2056], T.APF[:, :])
+    for i in range(8):
+        load(ys, "ld_av", T.RAW[i:128:16, 8:2056], av[:, :])
+        load(ys, "ld_av", T.RAW[8 + i:128:16, 8:2056], T.TCF[:, :])
     wait(SQ, s_z)
     for k in range(8):
         load(ys, "ld_vv", T.VV[16 * k:16 * k + 8, 8:4104], T.vv[:, :])
-    for k in range(8):
-        load(ys, "ld_ac", T.AC[16 * k:16 * k + 8, 8:2056], T["ap"][:, :])
-        load(ys, "ld_ac", T.AC[16 * k + 8:16 * k + 16, 8:2056], T["at"][:, :])
-    wait(SQ, s_za)
-    for k in range(8):
-        load(ys, "ld_av", T.AV[16 * k:16 * k + 8, 8:2056], T["av"][:, :])
 
-    wait(V, s_j8, s_i5, s_ot)
     ts(T.MASKHD[:, :], T.JH[:, :], hi, A.is_equal)
-    ts(T.M12[:, :], T.R12[:, :], pf[:, 0:1], A.is_equal, to=s_m12)
-    ts(T.GRP[:, :], T.RG[:, :], pf[:, 14:15], A.is_equal, to=s_gp)
+    ts(T.M12[:, :], T.R12[:, :], pf[:, 0:1], A.is_equal)
     ts(T.MASK8[:, :], T.J8[:, :], pf[:, 3:4], A.is_equal)
-    ts(T.ZL[:, :], T.UL[:, :], -8192.0, A.mult, to=s_sh)
-    ts(T.ZH[:, :], T.UH[:, :], -8192.0, A.mult, to=s_sh)
-    ts(T.UL2[:, :], T.UL[:, :], 2.0, A.mult, to=s_sh)
     for b in range(5):
         n = 512 if b < 4 else 8
         ts(T.C[:, 4096 + 512 * b:4096 + 512 * b + n], T.I512[:, 0:n], lo, A.mult, T.EXC[:, b:b + 1], A.add)
     do(V, v.memset(T.DC[:, :], 0.5))
-    sync(V)
-    do(V, v.memset(T.DC[:, 0:96:4], -1.0))
-    do(V, v.memset(T.AC[:, 0:8], 2048))
-    do(V, v.memset(T.AC[:, 2056:2064], 2048))
+    wait(V, s_l1p)
+    cp(T.L1[:, :], T.b7[:, 0:128], s_l1)
 
     arrived = 2 * len(others)
+    TH, TL, TK, THA, TLA, TKA = (T.TM[:, 4 * i:4 * i + 4] for i in range(6))
 
     def halves(rq, th, tl):
-        ts(th[:, :], rq[:, 1:32:8], 1024.0, A.mult)
-        cp(tl[:, :], rq[:, 2:32:8])
+        ts(th, rq[:, 1:32:8], 1024.0, A.mult)
+        cp(tl, rq[:, 2:32:8])
 
-    def spread(tk, s_tk, tx, bank, t48):
-        s_tx, s_p, s_t = sig(), sig(), sig()
-        wait(S, s_tk, s_m12)
+    def spread(tk, tx, bank, grp, s_grp):
+        s_tx, s_p = sig(), sig()
         for q in range(n_ranks):
-            do(S, act.activation(tx[:, 12 * q:12 * q + 12], T.M12[:, :], F.Copy, scale=tk[:, q:q + 1]), s_tx)
-        wait(PE, s_sh, s_gp, s_tx)
-        mms(bank[:, 0:48], [(T.GRP[:, :], tx[:, :])], s_p)
-        wait(S, s_p)
-        do(S, act.activation(t48[:, :], bank[:, 0:48], F.Copy), s_t)
-        return s_t
+            ts(tx[:, 12 * q:12 * q + 12], T.M12[:, :], tk[:, q:q + 1], A.mult, to=s_tx)
+        wait(PE, s_grp, s_tx)
+        mms(bank[:, 0:48], [(grp[:, :], tx[:, :])], s_p)
+        return s_p
 
     def col(buf, k):
         return buf[:, 24 * k:24 * k + 24]
@@ -276,14 +298,15 @@ def rank_program(g, core, T, topo):
     sync(V)
     for q in range(n_ranks):
         tt(T.G0[:, 16 * q:16 * q + 16], T.HD[:, :].indirect(T.RQ[:, 8 * q:8 * q + 1]), T.MASKHD[:, :], A.mult, s_g0)
-    halves(T.RQ, T.TH, T.TL)
+    halves(T.RQ, TH, TL)
     wait(V, s_g0)
     for q in range(n_ranks):
         tt(T.N0[:, 6 * q:6 * q + 6], T.G0[:, 16 * q:16 * q + 6], T.G0[:, 16 * q + 8:16 * q + 14], A.add, s_ad)
     sync(V)
     cp(col(T.L, 0), T.N0[:, :])
-    tt(T.TK[:, :], T.TH[:, :], T.TL[:, :], A.add, s_tk)
-    s_t48 = spread(T.TK, s_tk, T.TX, T.b6, T.T48)
+    tt(TK, TH, TL, A.add, s_tk)
+    do(V, v.memset(T.DC[:, 0:96:4], -1.0))
+    s_t48 = [None]
 
     def gather(out, win, lst, to=None):
         tt(out[:, :], win[:, :].indirect(lst), T.MASK8[:, :], A.mult, to)
@@ -296,16 +319,17 @@ def rank_program(g, core, T, topo):
 
     def judge(k, s, t48):
         done = sig()
-        tt(T.NH[:, 48 * k:48 * k + 48], s[:, 7:384:8], t48[:, :], A.is_le, done)
+        tt(T.NH[:, 48 * k:48 * k + 48], s[:, 7:384:8], t48, A.is_le, done)
         wait(PE, done)
 
     z, s_zz, s_hh, s_p4, s_pm = T.b3[:, 0:24], sig(), sig(), sig(), sig()
     ss = [T.S0, T.S1]
 
     def tally(k):
-        wait(V, s_t48)
-        judge(k, ss[k % 2], T.T48)
+        wait(V, s_t48[0])
+        judge(k, ss[k % 2], T.b6[:, 0:48])
         even, odd = T.NH[:, 48 * k:48 * k + 48:2], T.NH[:, 48 * k + 1:48 * k + 48:2]
+        wait(PE, s_zl)
         pe.matmul(z, T.ZL[:, :], even, k == 0, False)
         ins = pe.matmul(z, T.ZH[:, :], odd, False, k == 3)
         if k == 3:
@@ -314,22 +338,21 @@ def rank_program(g, core, T, topo):
 
     def other_work(k):
         if k == 0:
-            wait(V, s_j16)
+            ts(T.GRP[:, :], T.RG[:, :], pf[:, 14:15], A.is_equal, to=s_gp)
+            s_t48[0] = spread(TK, T.TX, T.b6, T.GRP, s_gp)
+        elif k == 1:
+            v.wait_ge(T.sem.ra, arrived)
+            halves(T.RQA, THA, TLA)
             cp(T.SLI[:, :], T.SLF[:, :])
             ts(T.OWI[:, :], T.RKI[:, :], 11, A.arith_shift_right)
-            ts(T.LREP[:, :], T.J16[:, :], pf[:, 1:2], A.is_equal, to=s_p4)
-            ts(T.SEL[:, :], T.I128[:, 0:8], pf[:, 0:1], A.is_equal, to=s_p4)
-        elif k == 1:
-            ts(T.GMI[:, 0:2], T.SLI[:, :], 1, A.arith_shift_right, 7, A.bitwise_and)
-            ts(T.GMI[:, 2:4], T.SLI[:, :], 3, A.arith_shift_right, 62, A.bitwise_and)
-            ts(T.GMI[:, 4:6], T.SLI[:, :], 1, A.bitwise_and)
-            ts(T.OW12[:, :], T.OWI[:, :], 12.0, A.mult)
-            ts(T.PERM0[:, :], T.I512[:, 0:256], pf[:, 8:9], A.is_equal, to=s_pm)
         elif k == 2:
-            cp(T.GMF[:, :], T.GMI[:, :])
-            ts(T.PERM1[:, :], T.I512[:, 0:256], pf[:, 9:10], A.is_equal, to=s_pm)
+            tt(TKA, THA, TLA, A.add)
+            ts(T.GMI[:, 0:2], T.SLI[:, :], 7, A.bitwise_and)
+            ts(T.GMI[:, 2:4], T.SLI[:, :], 3, A.arith_shift_right, 31, A.bitwise_and)
+            ts(T.OW12[:, :], T.OWI[:, :], 12.0, A.mult)
 
     wait(V, s_rst)
+    wait(PE, s_sh)
     for k in range(4):
         s_g, s_s, s_n = sig(), sig(), sig()
         sync(V)
@@ -339,6 +362,11 @@ def rank_program(g, core, T, topo):
         ts(T.NL[:, 3 - k:96:4], col(T.L, k), 8.0, A.add)
         if k:
             tally(k - 1)
+        else:
+            for out, col_ in ((T.ZL, 13), (T.ZH, 15)):
+                ts(out[:, :], i128, pf[:, col_:col_ + 1], A.is_equal, pf[:, 17:18], A.mult, to=s_zl)
+        if k == 3:
+            cp(T.GMF[:, :], T.GMI[:, :])
         wait(V, s_g)
         scan(ss[k % 2], T.G, s_s)
         wait(PE, s_s)
@@ -348,13 +376,12 @@ def rank_program(g, core, T, topo):
             wait(V, s_n)
             cp(col(T.L, k + 1), nb[k % 2])
         else:
-            for a, b in shift(ss[1]):
-                pe.matmul(z, a, b, False, False)
+            pe.matmul(z, T.SC0[:, :], ss[1][:, 7:384:16], False, False)
+            pe.matmul(z, T.SC1[:, :], ss[1][:, 15:384:16], False, False)
             wait(V, s_s)
             tally(3)
-    ts(T.LT0[:, :], T.RG[:, :], T.GMF[:, 0:1], A.is_equal, to=s_pm)
-    ts(T.LT1[:, :], T.RG[:, :], T.GMF[:, 1:2], A.is_equal, to=s_pm)
-    tt(T.MA[:, :], T.GMF[:, 2:4], T.GMF[:, 4:6], A.add)
+    ts(T.GRPA[:, :], T.J8[:, 0:128], pf[:, 14:15], A.is_equal, to=s_gpa)
+    s_t48a = spread(TKA, T.TXA, T.b7, T.GRPA, s_gpa)
     s_ls = sig()
     wait(V, s_zz)
     ts(T.LS[:, :], z, -4088.0, A.add, 0.0, A.max, to=s_ls)
@@ -364,119 +391,135 @@ def rank_program(g, core, T, topo):
     g.remote_dma(out_ap=T.LSA[:, :], in_ap=T.LS[:, :], remote_sem=T.sem.ls, local_sem=T.sem.l_ls, pid=pid, routing_id=rid,
                  dma_engine_mask=topo.mask(core, T.cores[nxt]))
 
-    s_ho, s_vl, s_mp, s_mk, s_tka = (sig() for _ in range(5))
-    wait(PE, s_pm)
-    mms(T.b4[:, 0:256], [(T.LT0[:, :], T.PERM0[:, :]), (T.LT1[:, :], T.PERM1[:, :])], s_mp)
-    wait(S, s_mp)
-    do(S, act.activation(T.MSK[:, :], T.b4[:, 0:256], F.Copy), s_mk)
+    s_f1, s_lv1, s_lv2, s_l2p, s_l2 = (sig() for _ in range(5))
+    wait(S, s_l1, s_zf)
+    act.wait_ge(T.sem.ld_fw, loads["ld_fw"])
+    do(S, act.activation(T.F1[:, :], T.FW[:, :].indirect(T.L1[:, :]), F.Copy), s_f1)
+    wait(SQ, s_f1)
+    for c in range(8):
+        load(ys, "ld_d2", T.D2[:, 16 * c:16 * c + 16], T.F1[16 * c:16 * c + 1, :])
+    wait(S, s_re)
+    act.wait_ge(T.sem.ld_av, loads["ld_av"])
+    do(S, act.activation(T.LV1[:, 8:2056], T.RAW[:, :].indirect(T.L1[:, :]), F.Copy), s_lv1)
+    pe.wait_ge(T.sem.ld_d2, loads["ld_d2"])
+    mms(T.b2[:, 0:128], [(T.D2[:, :], T.IDF[:, :])], s_l2p)
+
+    s_ho, s_vl, s_mp, s_mk, s_vg, s_vs, s_se = (sig() for _ in range(7))
     wait(V, s_hh)
     sync(V)
     tt(T.HP[:, :], T.b5[:, 0:96], T.NL[:, :], A.mult)
     tt(T.D0[:, :], T.b5[:, 0:96], T.DC[:, :], A.is_lt)
-    tt(T.MC[:, :], T.MA[:, :], T.OW12[:, :], A.add)
-    sync(V)
+    tt(T.MC[:, :], T.GMF[:, 2:4], T.OW12[:, :], A.add)
+    wait(V, s_l2p)
+    cp(T.L2[:, :], T.b2[:, 0:128], s_l2)
+    wait(S, s_l2)
+    do(S, act.activation(T.LV2[:, 8:2056], T.RAW[:, :].indirect(T.L2[:, :]), F.Copy), s_lv2)
+    sync_own(V)
     do(V, v.tensor_tensor_scan(T.HS[:, :], T.D0[:, :], T.HP[:, :], 0.0, A.mult, A.add))
-    for x, rv in ((0, T.RV0), (1, T.RV1)):
-        ts(rv[:, :], T.I128[:, 0:16], pf[:, 10 + x:11 + x], A.is_equal, T.MC[:, x:x + 1], A.mult, to=s_p4)
-    sync(V)
-    wait(PE, s_p4)
-    mms(T.b0[:, 0:16], [(T.LREP[:, :], T.RV0[:, :]), (T.LREP[:, :], T.RV1[:, :])], s_vl)
+    for x in (0, 1):
+        ts((T.LT0, T.LT1)[x][:, :], T.RG[:, :], T.GMF[:, x:x + 1], A.is_equal, to=s_pm)
+    sync_own(V)
     cp(T.LF[:, :], T.HS[:, 3:96:4])
-    v.wait_ge(T.sem.ra, arrived)
-    halves(T.RQA, T.THA, T.TLA)
-    sync(V)
+    for x in (0, 1):
+        ts((T.LTA0, T.LTA1)[x][:, :], T.J8[:, 0:128], T.GMF[:, x:x + 1], A.is_equal, to=s_pm)
     v.wait_ge(T.sem.ld_vv, loads["ld_vv"])
-    gather(T.G, T.VV, T.LF[:, 0:24])
-    tt(T.TKA[:, :], T.THA[:, :], T.TLA[:, :], A.add, s_tka)
-    sync(V)
-    scan(T.S0, T.G)
-    sync(V)
+    sync_own(V)
+    gather(T.G, T.VV, T.LF[:, 0:24], s_vg)
+
+    p01, h2, t48a = T.b3[:, 0:48], T.b5[:, 0:48], T.b7[:, 0:48]
+    ends = slice(7, 384, 8)
+    W0, W1, Z, A0, A1, ACC, PX, X = (T.WK[:, 48 * i:48 * i + 48] for i in range(8))
+    s_01, s_h2, s_a, s_px, s_x2 = (sig() for _ in range(5))
+    s_g, s_v = [sig() for _ in range(3)], [sig() for _ in range(3)]
+    places = T.LSA[:, 0:24]
+    hits = [T.NH[:, 48 * (4 + k):48 * (5 + k)] for k in range(3)]
+    wait(V, s_re, s_le)
+    v.wait_ge(T.sem.ld_av, loads["ld_av"])
+    v.wait_ge(T.sem.ls, n8)
+    gather(T.GB, T.RAW, places, s_g[0])
+    wait(V, s_vg)
+    scan(T.S0, T.G, s_vs)
+    wait(V, s_lv1)
+    gather(T.GD, T.LV1, places, s_g[1])
+    wait(V, s_vs)
     cp(T.HOUT[:, :], T.S0[:, 7:384:8], s_ho)
     wait(GQ, s_ho)
     send3(lambda q: T.HOUT[:, 12 * q:12 * q + 12], T.ANSH[:, 12 * r:12 * r + 12], T.sem.ha, T.sem.l_ha, [4, 2, 2])
-    s_t48a = spread(T.TKA, s_tka, T.TXA, T.b7, T.T48A)
-    wait(V, s_ho)
-    cp(T.ANSH[:, 12 * r:12 * r + 12], T.HOUT[:, 12 * r:12 * r + 12])
-
-    sync(V)
-    v.wait_ge(T.sem.ls, n8)
-    v.wait_ge(T.sem.ld_ac, loads["ld_ac"])
-    ml, vals = [T.LSA, T.M1, T.M2], [T.V0, T.V1, T.V2]
-    p01, h2 = T.b3[:, 0:48], T.b5[:, 0:48]
-    ends = slice(7, 384, 8)
-    s_01, s_h2, s_va, s_a, s_px, s_x2 = (sig() for _ in range(6))
-    for k in range(3):
-        s_g, s_ga, s_s, s_n = sig(), sig(), sig(), sig()
-        places = ml[k][:, 0:24]
-        hits = T.NH[:, 48 * (4 + k):48 * (5 + k)]
-        if k == 2:
-            wait(V, s_01)
-            ts(T.Z[:, :], p01, 0.0, A.is_equal)
-            ts(T.W1[:, :], p01, 1.0, A.is_equal)
-            ts(T.W0[:, :], p01, 2.0, A.is_ge)
-        sync(V)
-        gather(T.G, T.AC, places, s_g)
-        if k < 2:
-            wait(V, s_g)
-            scan(T.S0, T.G, s_s)
-            wait(PE, s_s)
-            mms(nb[k % 2], shift(T.S0), s_n)
-            if k == 0:
-                v.wait_ge(T.sem.ld_av, loads["ld_av"])
-            gather(T.GA, T.AV, places, s_ga)
-            wait(V, s_t48a, s_s)
-            judge(4 + k, T.S0, T.T48A)
-            ins = pe.matmul(p01, (T.UL2, T.UL)[k][:, :], hits, k == 0, k == 1)
-            if k == 1:
-                do(PE, ins, s_01)
-            wait(V, s_ga)
-            scan(vals[k], T.GA)
-            wait(V, s_n)
-            ts(ml[k + 1][:, :], nb[k % 2], 8.0, A.add)
-        else:
-            gather(T.GA, T.AV, places, s_ga)
-            wait(V, s_g)
-            scan(T.S0, T.G, s_s)
-            wait(V, s_ga)
-            scan(T.V2, T.GA, s_va)
-            wait(V, s_s)
-            judge(6, T.S0, T.T48A)
-            mms(h2, [(T.UL[:, :], hits)], s_h2)
-            tt(T.A0[:, :], T.W0[:, :], T.V0[:, ends], A.mult, s_a)
-            tt(T.A1[:, :], T.W1[:, :], T.V1[:, ends], A.mult, s_a)
-            wait(V, s_va)
-            tt(T.PX[:, :], T.Z[:, :], T.V2[:, ends], A.mult, s_px)
-            wait(V, s_a)
-            tt(T.ACC[:, :], T.A0[:, :], T.A1[:, :], A.add, s_x2)
+    wait(V, s_g[0])
+    scan(T.V0, T.GB, s_v[0])
+    wait(V, s_g[1])
+    scan(T.V1, T.GD, s_v[1])
+    wait(V, s_t48a, s_v[0])
+    judge(4, T.V0, t48a)
+    wait(V, s_lv2)
+    gather(T.G, T.LV2, places, s_g[2])
+    wait(V, s_v[1])
+    judge(5, T.V1, t48a)
+    ts(T.UL2[:, :], T.UL[:, :], 2.0, A.mult, to=s_u2)
+    wait(PE, s_u2)
+    mms(p01, [(T.UL2[:, :], hits[0]), (T.UL[:, :], hits[1])], s_01)
+    wait(V, s_g[2])
+    scan(T.V2, T.G, s_v[2])
+    wait(V, s_01)
+    ts(Z, p01, 0.0, A.is_equal, to=s_a)
+    ts(W1, p01, 1.0, A.is_equal, to=s_a)
+    ts(W0, p01, 2.0, A.is_ge, to=s_a)
+    wait(V, s_v[2])
+    judge(6, T.V2, t48a)
+    mms(h2, [(T.UL[:, :], hits[2])], s_h2)
+    wait(V, s_a)
+    tt(PX, Z, T.V2[:, ends], A.mult, s_px)
+    tt(A0, W0, T.V0[:, ends], A.mult)
+    tt(A1, W1, T.V1[:, ends], A.mult)
+    sync_own(V)
+    tt(ACC, A0, A1, A.add, s_x2)
     s_ao = sig()
     wait(V, s_h2, s_px)
-    tt(T.X[:, :], h2, T.PX[:, :], A.mult, s_x2)
+    tt(X, h2, PX, A.mult, s_x2)
     wait(V, s_x2)
-    tt(T.AOUT[:, :], T.ACC[:, :], T.X[:, :], A.add, s_ao)
+    tt(T.AOUT[:, :], ACC, X, A.add, s_ao)
     wait(GQ, s_ao)
     send3(lambda q: T.AOUT[:, 12 * q:12 * q + 12], T.ANSA[:, 12 * prv:12 * prv + 12], T.sem.aa, T.sem.l_aa, [4, 2, 2])
 
+    for out, col_ in ((T.PERM0, 8), (T.PERM1, 9)):
+        ts(out[:, :], T.I512[:, 0:256], pf[:, col_:col_ + 1], A.is_equal, to=s_pm)
+    wait(PE, s_pm)
+    perms = (T.PERM0[:, :], T.PERM1[:, :])
+    mms(T.b4[:, 0:256], [(T.LT0[:, :], perms[0]), (T.LT1[:, :], perms[1])], s_mp)
+    mms(T.b4[:, 256:512], [(T.LTA0[:, :], perms[0]), (T.LTA1[:, :], perms[1])], s_mp)
+    for x, rv in ((0, T.RV0), (1, T.RV1)):
+        ts(rv[:, :], T.I128[:, 0:16], pf[:, 10 + x:11 + x], A.is_equal, T.MC[:, x:x + 1], A.mult, to=s_p4)
+    wait(V, s_j16)
+    ts(T.LREP[:, :], T.J16[:, :], pf[:, 1:2], A.is_equal, to=s_p4)
+    wait(PE, s_p4)
+    mms(T.b0[:, 0:16], [(T.LREP[:, :], T.RV0[:, :]), (T.LREP[:, :], T.RV1[:, :])], s_vl)
+    wait(S, s_mp)
+    do(S, act.activation(T.MSK[:, :], T.b4[:, :], F.Copy), s_mk)
+    wait(V, s_ho, s_ao)
+    cp(T.ANSH[:, 12 * r:12 * r + 12], T.HOUT[:, 12 * r:12 * r + 12])
+    cp(T.ANSA[:, 12 * prv:12 * prv + 12], T.AOUT[:, 12 * r:12 * r + 12])
+    ts(T.SEL[:, :], T.I128[:, 0:8], pf[:, 0:1], A.is_equal, to=s_se)
+    ts(T.SELA[:, :], T.I128[:, 0:8], pf[:, 14:15], A.is_equal, to=s_se)
     wait(V, s_vl)
     cp(T.VL[:, :], T.b0[:, 0:16])
     landed = sum((4, 2, 2)[[o for o in range(n_ranks) if o != q].index(r)] for q in others)
     s_xh, s_x = sig(), [sig(), sig()]
     s_y, s_ys = [sig(), sig()], [sig(), sig()]
     sync(V)
-    cp(T.ANSA[:, 12 * prv:12 * prv + 12], T.AOUT[:, 12 * r:12 * r + 12])
     wait(V, s_mk)
     v.wait_ge(T.sem.ha, landed)
-    tt(T.XH[:, :], T.ANSH[:, :].indirect(T.VL[:, 0:16]), T.MSK[:, :], A.mult, s_xh)
-    sync(V)
+    tt(T.XH[:, :], T.ANSH[:, :].indirect(T.VL[:, 0:16]), T.MSK[:, 0:256], A.mult, s_xh)
     v.wait_ge(T.sem.aa, landed)
-    wait(PE, s_xh)
+    wait(PE, s_xh, s_se)
     part = [slice(0, 128), slice(128, 256)]
     bank = [T.b6[0:8, 0:128], T.b7[0:8, 0:128]]
     for i in range(2):
-        tt(T.XA[:, part[i]], T.ANSA[:, :].indirect(T.VL[:, 8 * i:8 * i + 8]), T.MSK[:, part[i]], A.mult, s_x[i])
+        tt(T.XA[:, part[i]], T.ANSA[:, :].indirect(T.VL[:, 8 * i:8 * i + 8]), T.MSK[:, 256 + 128 * i:384 + 128 * i], A.mult,
+           s_x[i])
         pe.matmul(bank[i], T.SEL[:, :], T.XH[:, part[i]], True, False)
     for i in range(2):
         wait(PE, s_x[i])
-        do(PE, pe.matmul(bank[i], T.SEL[:, :], T.XA[:, part[i]], False, True), s_y[i])
+        do(PE, pe.matmul(bank[i], T.SELA[:, :], T.XA[:, part[i]], False, True), s_y[i])
     wait(S, s_y[0])
     do(S, act.activation(T.YS[:, part[0]], bank[0], F.Copy), s_ys[0])
     sync(S)

@@ -3,25 +3,25 @@ from concourse.bass import DstId, RemoteDMATransfer
 from concourse.mybir import AluOpType as A, AxisListType, ActivationFunctionType as F
 
 WIDTHS = {
-    "int32": dict(RKI=2, RTI=2, PCI=1, PBI=8, OWI=2, KVI=6, SLI=2, GMI=4, HD=2048, C=6152, DI=128, ATC=128, APC=128),
-    "float32": dict(PFC=20, EXC=8, I128=128, I512=512, RG=128, SR=128, J8=384, J16=128, JH=16, R12=12, M12=12, OW12=2,
-                    KVF=6, SLF=2, GMF=4, MC=2, EF=8, TM=24, TX=48, TXA=48, GRP=128, GRPA=128, SHLO=128, SHHI=128, SC0=128,
-                    SC1=128, IDF=128, MASKHD=16, MASK8=384, RST8=384, VV=4104, FW=2064, F1=2048, RAW=2064, LV1=2064,
-                    LV2=2064, DF=128, D2=128, TCF=128, APF=128, G0=64, N0=24, G=384, GB=384, GD=384, S0=384, S1=384,
-                    V0=384, V1=384, V2=384, NL=96, DC=96, D0=96, HP=96, HS=96, WK=384, HOUT=48, AOUT=48, ANSH=48, ANSA=48,
-                    MSK=512, SEL=8, SELA=8, XH=256, XA=256),
-    "bfloat16": dict(TRI=128, EYE=128, TRIP=128, TRIN=128, ONES=128, NONES=128, GE=10, UL=128, UH=128, UL2=128,
-                     ZL=128, ZH=128, NH=384, LREP=128, RV0=16, RV1=16, LT0=128, LT1=128, LTA0=128, LTA1=128,
-                     PERM0=256, PERM1=256),
-    "float16": dict(LK0=128, LK1=128, RK0=16, RK1=16),
-    "uint16": dict(KREQ=16, RQ=32, RQA=32, L=96, LF=24, LS=24, LSA=24, VL=16, L1=128, L2=128),
+    "int32": dict(RKI=2, RTI=2, PCI=1, PBI=9, OWI=2, KVI=6, SLI=2, GMI=4, HD=2048, C=4104, DI=128, ATC=128),
+    "float32": dict(PFC=36, I128=128, I512=512, RG=128, SR=128, J8=384, J2=384, J16=128, JH=16, R12=12, M12=12, OW12=2,
+                    KVF=6, SLF=2, GMF=4, MC=2, EF=8, TM=24, TX=48, TXA=192, M48=48, GRP=128, GRPA=128, SHLO=128, SHHI=128,
+                    SC0=128, SC1=128, SCL=128, MASKHD=16, MASK8=384, MASK2=384, RST8=384, VV=4104, RAW=2064,
+                    LV1=2064, LV2=2064, TCF=128, G0=64, N0=24, G=384, GB=384, S0=384, S1=384, BB=192, XV=192,
+                    CA0=128, CA1=128, CA2=128, CA3=128, MX=96, NL=96, DC=96, D0=96, HP=96, HS=96, HOUT=48, AOUT=48,
+                    ANSH=48, ANSA=48, MSK=256, MSKA=256, SEL=8, SELA=8, XH=256, XA=256),
+    "bfloat16": dict(TRI=128, EYE=128, TRIP=128, TRIN=128, ONES=128, NONES=128, GE=10, UL=128, UH=128,
+                     ZL=128, ZH=128, NH=192, NHA=192, SA=128, SB=128, LREP=128, RV0=16, RV1=16, LT0=128, LT1=128,
+                     LTA0=128, LTA1=128, PERM0=256, PERM1=256),
+    "float16": dict(LK0=128, LK1=128, RK0=16, RK1=16, DF=128, IDF=128),
+    "uint16": dict(KREQ=16, RQ=32, RQA=32, L=96, LF=24, LS=24, LSA=24, VL=16, L1=128),
 }
 SCRATCH = {b: ("sbuf", [128, w], d) for d in WIDTHS for b, w in WIDTHS[d].items()}
 SCRATCH["YS"] = ("sbuf", [8, 256], "float32")
 SCRATCH.update({"b%d" % i: ("psum", [128, 512], "float32") for i in range(8)})
 SEMAPHORES = ["vq", "tq", "aq", "rq", "ra", "ls", "ha", "aa", "l_rq", "l_ra", "l_ls", "l_ha", "l_aa", "sent",
-              "ld_rk", "ld_rt", "ld_hd", "ld_c", "ld_vv", "ld_d", "ld_at", "ld_fw", "ld_av", "ld_d2", "st"]
-SEMAPHORES += ["k%d" % i for i in range(120)]
+              "ld_rk", "ld_rt", "ld_hd", "ld_c", "ld_vv", "ld_d", "ld_at", "ld_av", "ld_mg", "st"]
+SEMAPHORES += ["k%d" % i for i in range(126)]
 
 
 def queue(eng, own):
@@ -52,10 +52,12 @@ def sync_own(Q):
         Q["w"] = Q["n"]
 
 
-def sync(Q):
+def sync(Q, *but):
     sync_own(Q)
-    wait(Q, *Q["p"])
+    left = [s for s in Q["p"] if s in but]
+    wait(Q, *[s for s in Q["p"] if s not in but])
     Q["p"].clear()
+    Q["p"].extend(left)
 
 
 def rank_program(g, core, T, topo):
@@ -94,17 +96,15 @@ def rank_program(g, core, T, topo):
     ap, at, av = T["ap"], T["at"], T["av"]
     load(g.sync, "ld_rk", T.RKI[:, :], T.rk[:, :])
     load(g.scalar, "ld_rt", T.RTI[:, :], T.rt[:, :])
-    load(g.scalar, "ld_at", T.ATC[:, :], at[:, :])
-    load(g.sync, "ld_at", T.APC[:, :], ap[:, :])
-    for c in range(8):
-        load((g.sync, g.scalar)[c % 2], "ld_d", T.DI[:, 16 * c:16 * c + 16], ap[c:c + 1, :])
     for k in range(8):
         load(g.sync, "ld_hd", T.HD[16 * k:16 * k + 8, :], T.hd[:, :])
         load(g.scalar, "ld_hd", T.HD[16 * k + 8:16 * k + 16, :], T.hd[:, :])
     for k in range(8):
         load(g.sync if k % 2 == 0 else g.scalar, "ld_c", T.C[16 * k:16 * k + 8, 0:4096], T.vp[:, :])
+    load(g.scalar, "ld_at", T.ATC[:, :], at[:, :])
+    load(g.sync, "ld_c", T.C[8:16, 0:4096], T.vt[:, :])
 
-    s_pc, s_i, s_sr, s_j8, s_i5, s_ot = sig(), sig(), sig(), sig(), sig(), sig()
+    s_pc, s_i, s_sr, s_j8, s_i5, s_ot, s_j2, s_j16, s_zg = (sig() for _ in range(9))
 
     def iota(out, pattern, s, base=0, cm=0, flag=True):
         kw = {"allow_small_or_imprecise_dtypes": True} if flag else {}
@@ -115,7 +115,6 @@ def rank_program(g, core, T, topo):
     iota(T.I128[:, :], [[1, 128]], s_i)
     iota(T.SR[:, :], [[1, 8], [8, 2], [16, 8]], s_sr, 512)
     iota(T.J8[:, :], [[0, 48], [1, 8]], s_j8)
-    iota(T.I512[:, :], [[1, 512]], s_i5)
     iota(T.RG[:, :], [[1, 8], [0, 16]], s_ot)
     iota(T.R12[:, :], [[1, 6], [8, 2]], s_ot)
     iota(T.JH[:, :], [[1, 2], [0, 8]], s_ot)
@@ -129,50 +128,36 @@ def rank_program(g, core, T, topo):
     def cp(out, in_, to=None):
         do(V, v.tensor_copy(out, in_), to)
 
-    s_one, s_ge, s_sh, s_gp, s_gpa, s_kk, s_id, s_eb, s_zl, s_u2 = (sig() for _ in range(10))
+    s_one, s_ge, s_sh, s_gp, s_gpa, s_kk, s_id, s_eb, s_zl, s_ca, s_u2, s_m2 = (sig() for _ in range(12))
     do(V, v.memset(T.ONES[:, :], 1.0), s_one)
     do(V, v.memset(T.NONES[:, :], -1.0), s_one)
     do(V, v.memset(T.GE[:, 0:10:5], 1.0), s_ge)
     do(V, v.memset(T.GE[:, 4:10:5], 0.0), s_ge)
     wait(V, s_pc)
     pb, pf = T.PBI, T.PFC
-    for i, a, b in ((0, 0, 15), (1, 3, 15), (2, 3, 1), (3, 0, 7), (4, 0, 127), (14, 4, 7)):
-        ts(pb[:, min(i, 5):min(i, 5) + 1], T.PCI[:, :], a, A.arith_shift_right, b, A.bitwise_and)
-    sync(V)
-    cp(pf[:, 0:5], pb[:, 0:5])
-    cp(pf[:, 14:15], pb[:, 5:6])
-    sync(V)
     big = float(1048576)
     i128, p, hi, lo = T.I128[:, :], pf[:, 4:5], pf[:, 2:3], pf[:, 5:6]
+
+    def f(i):
+        return pf[:, i:i + 1]
+
+    cp(p, T.PCI[:, :])
+    ts(pb[:, 2:3], T.PCI[:, :], 3, A.arith_shift_right, 1, A.bitwise_and)
     wait(V, s_i)
+    sync(V)
     ts(T.TRI[:, :], i128, p, A.is_gt)
     ts(T.EYE[:, :], i128, p, A.is_equal, 512.0, A.mult)
-    ts(lo, hi, -1.0, A.mult, 1.0, A.add)
-    ts(pf[:, 6:7], p, 8.0, A.add)
-    ts(pf[:, 7:8], p, -8.0, A.add)
-    ts(pf[:, 10:11], pf[:, 3:4], 2.0, A.mult)
-    ts(pf[:, 11:12], pf[:, 3:4], 2.0, A.mult, 1.0, A.add)
-    ts(pf[:, 12:13], pf[:, 3:4], 32.0, A.mult)
-    ts(pf[:, 13:14], pf[:, 3:4], 16.0, A.mult, pf[:, 14:15], A.add)
-    sync(V)
-    tt(T.TRIP[:, :], T.TRI[:, :], T.EYE[:, :], A.add, s_one)
-    tt(pf[:, 8:9], pf[:, 12:13], pf[:, 1:2], A.add)
-    ts(pf[:, 15:16], pf[:, 13:14], 8.0, A.add)
-    ts(pf[:, 16:17], hi, big, A.mult, to=s_eb)
-    ts(pf[:, 17:18], hi, -8192.0, A.mult)
-    for b in range(5):
-        ts(T.EXC[:, b:b + 1], lo, float(4096 + 512 * b) - big, A.mult, big, A.add)
-    sync(V)
-    ts(T.TRIN[:, :], T.TRIP[:, :], -1.0, A.mult, to=s_one)
-    ts(pf[:, 9:10], pf[:, 8:9], 16.0, A.add)
-    for out, col_, role in ((T.SHHI, pf[:, 6:7], lo), (T.SHLO, p, lo), (T.UL, pf[:, 7:8], hi), (T.UH, p, hi)):
-        ts(out[:, :], i128, col_, A.is_equal, role, A.mult, to=s_sh)
+    cp(hi, pb[:, 2:3])
     for rk in (T.RK0, T.RK1):
         ts(rk[:, 3:16:4], i128[:, 0:4], 0.0, A.mult, to=s_kk)
+    sync(V)
+    tt(T.TRIP[:, :], T.TRI[:, :], T.EYE[:, :], A.add, s_one)
+    ts(f(16), hi, big, A.mult, to=s_eb)
+    sync(V)
+    ts(T.TRIN[:, :], T.TRIP[:, :], -1.0, A.mult, to=s_one)
 
     s_pos, s_kp, s_kq, s_own, s_ef = (sig() for _ in range(5))
     v.wait_ge(T.sem.ld_rk, loads["ld_rk"])
-    sync(V)
     for q in range(1, n_ranks):
         ts(T.GE[:, q:10:5], T.RKI[:, :], 2048 * q, A.is_ge, to=s_ge)
     v.wait_ge(T.sem.ld_rt, loads["ld_rt"])
@@ -193,7 +178,6 @@ def rank_program(g, core, T, topo):
     cp(T.KVF[:, :], T.KVI[:, :], s_ef)
     tt(T.EF[:, 0:4], ge[0], ge[1], A.subtract, s_ef)
     tt(T.EF[:, 4:8], ge[2], ge[3], A.subtract, s_ef)
-    ts(T.IDF[:, :], i128, p, A.is_equal, to=s_id)
     wait(V, s_pos, s_sr)
     do(V, v.tensor_reduce(T.SLF[:, 0:1], T.b0[:, 0:4], AxisListType.X, A.max))
     do(V, v.tensor_reduce(T.SLF[:, 1:2], T.b0[:, 4:8], AxisListType.X, A.max))
@@ -206,8 +190,9 @@ def rank_program(g, core, T, topo):
         ts(lk[:, :], T.SR[:, :], T.SLF[:, x:x + 1], A.is_equal, to=s_kk)
     wait(PE, s_kk)
     mms(T.b1[:, 0:16], [(T.LK0[:, :], T.RK0[:, :]), (T.LK1[:, :], T.RK1[:, :])], s_kp)
-    for out, col_ in ((T.SC0, 13), (T.SC1, 15)):
-        ts(out[:, :], i128, pf[:, col_:col_ + 1], A.is_equal, lo, A.mult, to=s_sh)
+    bits = ((0, 15), (3, 15), (3, 1), (0, 7), (4, 7), (0, 1), (4, 1), (5, 3))
+    for i in (0, 1, 3, 4):
+        ts(pb[:, i:i + 1], T.PCI[:, :], bits[i][0], A.arith_shift_right, bits[i][1], A.bitwise_and)
     wait(V, s_kp)
     cp(T.KREQ[:, :], T.b1[:, 0:16], s_kq)
     cp(T.RQ[:, 8 * r:8 * r + 4], T.b1[:, 4 * r:4 * r + 4], s_own)
@@ -221,56 +206,81 @@ def rank_program(g, core, T, topo):
         return T.KREQ[:, 4 * q:4 * q + 4]
 
     send3(of_archive, T.RQA[:, 8 * r:8 * r + 4], T.sem.ra, T.sem.l_ra, [2, 2, 2])
-    s_j16 = sig()
+    iota(T.J2[:, :], [[0, 192], [1, 2]], s_j2)
+    iota(T.I512[:, :], [[1, 512]], s_i5)
     iota(T.J16[:, :], [[0, 8], [1, 16]], s_j16)
+    iota(T.VV[:, 2048:4104], [[0, 2056]], s_zg)
 
-    s_rst, s_z, s_zf, s_df, s_cf, s_l1p, s_l1, s_re, s_le = (sig() for _ in range(9))
+    s_rst, s_z, s_df, s_cf, s_l1p, s_l1, s_re, s_le, s_sc, s_fc, s_m8, s_ul, s_fd, s_sb = (sig() for _ in range(14))
+    for i in (5, 6, 7):
+        ts(pb[:, i:i + 1], T.PCI[:, :], bits[i][0], A.arith_shift_right, bits[i][1], A.bitwise_and)
+    ts(lo, hi, -1.0, A.mult, 1.0, A.add, to=s_fc)
+    ts(f(7), p, -8.0, A.add, to=s_fc)
+    ts(f(6), p, 8.0, A.add)
+    sync_own(V)
+    cp(f(3), pb[:, 3:4], s_fc)
+    cp(pf[:, 0:2], pb[:, 0:2])
+    cp(f(14), pb[:, 4:5])
+    cp(pf[:, 18:21], pb[:, 5:8])
     wait(S, s_j8)
     do(S, act.activation(T.RST8[:, :], T.J8[:, :], F.Sign), s_rst)
-
-    def fill(buf, width, s, bias=0.0):
-        for b in range(0, width, 384):
-            n = min(384, width - b)
-            do(S, act.activation(buf[:, b:b + n], T.J8[:, 0:n], F.Copy, bias=bias, scale=0.0), s)
-
-    fill(T.FW, 2064, s_zf, 2056.0)
-    fill(T.VV, 4104, s_z)
     wait(S, s_eb)
-    for buf, s in ((T.RAW, s_re), (T.LV1, s_le), (T.LV2, s_le)):
-        for a in (0, 2056):
-            do(S, act.activation(buf[:, a:a + 8], T.J8[:, 0:8], F.Identity, bias=pf[:, 16:17], scale=0.0), s)
+    for b in range(0, 2064, 384):
+        n = min(384, 2064 - b)
+        do(S, act.activation(T.RAW[:, b:b + n], T.J8[:, 0:n], F.Identity, bias=f(16), scale=0.0), s_re)
 
-    wait(V, s_j8, s_i5, s_ot)
-    v.wait_ge(T.sem.ld_d, loads["ld_d"])
-    v.wait_ge(T.sem.ld_at, loads["ld_at"])
-    ts(T.DF[:, :], T.DI[:, :], 8.0, A.add, to=s_df)
-    ts(T.APF[:, :], T.APC[:, :], 8.0, A.add, to=s_cf)
-    cp(T.TCF[:, :], T.ATC[:, :], s_cf)
-    wait(PE, s_df, s_id)
-    mms(T.b7[:, 0:128], [(T.DF[:, :], T.IDF[:, :])], s_l1p)
+    def one_hot(items, to):
+        mid = sig()
+        for out, in_, col_, role in items:
+            do(S, act.activation(out, in_, F.Abs, bias=col_, scale=-1.0), mid)
+        wait(S, mid)
+        for out, in_, col_, role in items:
+            do(S, act.activation(out, out, F.Relu, bias=role, scale=-1.0), to)
+
+    wait(S, s_fc)
+    one_hot([(T.MASK8[:, :], T.J8[:, :], f(3), 1.0)], s_m8)
+    one_hot([(T.UL[:, :], i128, f(7), hi), (T.UH[:, :], i128, p, hi)], s_ul)
+    for b in range(0, 2048, 384):
+        n = min(384, 2048 - b)
+        do(S, act.activation(T.VV[:, b:b + n], T.J8[:, 0:n], F.Copy, scale=0.0), s_z)
+    for a in (0, 2056):
+        do(S, act.activation(T.LV1[:, a:a + 8], T.J8[:, 0:8], F.Identity, bias=f(16), scale=0.0), s_le)
 
     ys = g.sync
     ys.wait_ge(T.sem.sent, 1)
-    for k in range(8):
+    for k in range(1, 8):
         load(ys, "ld_c", T.C[16 * k + 8:16 * k + 16, 0:4096], T.vt[:, :])
-    wait(SQ, s_cf, s_zf)
-    load(ys, "ld_fw", T.FW[0:128:16, 8:2056], T.APF[:, :])
-    for i in range(8):
+    for c in range(8):
+        load(ys, "ld_d", T.DI[:, 16 * c:16 * c + 16], ap[c:c + 1, :])
+    wait(SQ, s_re)
+    for i in range(2):
         load(ys, "ld_av", T.RAW[i:128:16, 8:2056], av[:, :])
-        load(ys, "ld_av", T.RAW[8 + i:128:16, 8:2056], T.TCF[:, :])
-    wait(SQ, s_z)
-    for k in range(8):
-        load(ys, "ld_vv", T.VV[16 * k:16 * k + 8, 8:4104], T.vv[:, :])
 
+    wait(V, s_j8, s_ot)
+    sync(V)
     ts(T.MASKHD[:, :], T.JH[:, :], hi, A.is_equal)
-    ts(T.M12[:, :], T.R12[:, :], pf[:, 0:1], A.is_equal)
-    ts(T.MASK8[:, :], T.J8[:, :], pf[:, 3:4], A.is_equal)
-    for b in range(5):
-        n = 512 if b < 4 else 8
-        ts(T.C[:, 4096 + 512 * b:4096 + 512 * b + n], T.I512[:, 0:n], lo, A.mult, T.EXC[:, b:b + 1], A.add)
-    do(V, v.memset(T.DC[:, :], 0.5))
-    wait(V, s_l1p)
-    cp(T.L1[:, :], T.b7[:, 0:128], s_l1)
+    for out, col_ in ((T.SHHI, f(6)), (T.SHLO, p)):
+        ts(out[:, :], i128, col_, A.is_equal, lo, A.mult, to=s_sh)
+    ts(T.C[:, 4096:4104], i128[:, 0:8], 0.0, A.mult, f(16), A.add)
+    ts(f(30), lo, 4096.0, A.mult)
+    ts(f(13), f(3), 16.0, A.mult, f(14), A.add, to=s_fd)
+    ts(f(17), hi, -8192.0, A.mult)
+    ts(f(22), f(0), -1.0, A.mult, p, A.add)
+    ts(f(20), f(3), 8.0, A.mult, f(20), A.add)
+    ts(T.M12[:, :], T.R12[:, :], f(0), A.is_equal)
+    ts(f(32), f(18), 2.0, A.mult, -1.0, A.add, to=s_fd)
+    ts(f(33), f(18), -1.0, A.mult, 1.0, A.add, to=s_fd)
+    ts(f(34), f(19), 2.0, A.mult, -1.0, A.add, to=s_fd)
+    ts(f(35), f(19), -1.0, A.mult, 1.0, A.add, to=s_fd)
+    sync(V)
+    ts(T.C[:, 4096:4104], T.C[:, 4096:4104], f(30), A.add)
+    ts(f(15), f(13), 8.0, A.add, to=s_fd)
+    ts(f(31), hi, 8.0, A.mult, f(13), A.add)
+    ts(f(20), hi, 4.0, A.mult, f(20), A.add)
+    ts(f(22), f(22), f(18), A.add, to=s_fd)
+    ts(f(21), f(0), 6.0, A.is_lt, to=s_fd)
+    ts(f(27), p, -5.0, A.add, to=s_fd)
+    ts(T.IDF[:, :], i128, p, A.is_equal, to=s_id)
 
     arrived = 2 * len(others)
     TH, TL, TK, THA, TLA, TKA = (T.TM[:, 4 * i:4 * i + 4] for i in range(6))
@@ -279,18 +289,19 @@ def rank_program(g, core, T, topo):
         ts(th, rq[:, 1:32:8], 1024.0, A.mult)
         cp(tl, rq[:, 2:32:8])
 
-    def spread(tk, tx, bank, grp, s_grp):
+    def spread(tk, tx, width, mask, bank, grp, s_grp):
         s_tx, s_p = sig(), sig()
         for q in range(n_ranks):
-            ts(tx[:, 12 * q:12 * q + 12], T.M12[:, :], tk[:, q:q + 1], A.mult, to=s_tx)
+            ts(tx[:, width * q:width * q + width], mask[:, :], tk[:, q:q + 1], A.mult, to=s_tx)
         wait(PE, s_grp, s_tx)
-        mms(bank[:, 0:48], [(grp[:, :], tx[:, :])], s_p)
+        mms(bank, [(grp[:, :], tx[:, :])], s_p)
         return s_p
 
     def col(buf, k):
         return buf[:, 24 * k:24 * k + 24]
 
     nb = [T.b1[:, 0:24], T.b2[:, 0:24]]
+    ca = [T.CA0, T.CA1, T.CA2, T.CA3]
     s_tk, s_g0, s_ad = sig(), sig(), sig()
     wait(V, s_own)
     v.wait_ge(T.sem.rq, arrived)
@@ -303,10 +314,30 @@ def rank_program(g, core, T, topo):
     for q in range(n_ranks):
         tt(T.N0[:, 6 * q:6 * q + 6], T.G0[:, 16 * q:16 * q + 6], T.G0[:, 16 * q + 8:16 * q + 14], A.add, s_ad)
     sync(V)
-    cp(col(T.L, 0), T.N0[:, :])
+    ts(col(T.L, 0), T.N0[:, :], 4096.0, A.min)
     tt(TK, TH, TL, A.add, s_tk)
+    do(V, v.memset(T.DC[:, :], 0.5))
+    ts(T.GRP[:, :], T.RG[:, :], f(14), A.is_equal, to=s_gp)
+    sync_own(V)
+    wait(V, s_tk)
+    s_t48 = spread(TK, T.TX, 12, T.M12, T.b6[:, 0:48], T.GRP, s_gp)
     do(V, v.memset(T.DC[:, 0:96:4], -1.0))
-    s_t48 = [None]
+    v.wait_ge(T.sem.ld_at, loads["ld_at"])
+    cp(T.TCF[:, :], T.ATC[:, :], s_cf)
+    for a in range(1, 4):
+        ts(f(22 + a), f(22), 2.0 * a, A.add, to=s_fd)
+    ts(T.SCL[:, :], i128, f(31), A.is_equal, to=s_zl)
+    for out, col_ in ((T.ZL, 13), (T.ZH, 15)):
+        ts(out[:, :], i128, f(col_), A.is_equal, f(17), A.mult, to=s_zl)
+    wait(S, s_fd, s_j2)
+    one_hot([(T.SC0[:, :], i128, f(13), lo), (T.SC1[:, :], i128, f(15), lo)], s_sc)
+    do(S, act.activation(T.MASK2[:, :], T.J2[:, :], F.Identity, bias=f(33), scale=f(32)), s_m2)
+    do(S, act.activation(T.GRPA[:, :], T.J2[:, 0:128], F.Identity, bias=f(35), scale=f(34)), s_gpa)
+    do(S, act.activation(T.SB[:, :], i128, F.Abs, bias=f(27), scale=-1.0), s_u2)
+    wait(S, s_u2)
+    one_hot([(T.SB[:, :], T.SB[:, :], 1.0, hi)], s_u2)
+    wait(S, s_u2)
+    do(S, act.activation(T.SB[:, :], T.SB[:, :], F.Copy, scale=-8.0), s_sb)
 
     def gather(out, win, lst, to=None):
         tt(out[:, :], win[:, :].indirect(lst), T.MASK8[:, :], A.mult, to)
@@ -317,205 +348,220 @@ def rank_program(g, core, T, topo):
     def shift(s):
         return [(T.SHLO[:, :], s[:, 7:384:16]), (T.SHHI[:, :], s[:, 15:384:16])]
 
-    def judge(k, s, t48):
-        done = sig()
-        tt(T.NH[:, 48 * k:48 * k + 48], s[:, 7:384:8], t48, A.is_le, done)
-        wait(PE, done)
-
     z, s_zz, s_hh, s_p4, s_pm = T.b3[:, 0:24], sig(), sig(), sig(), sig()
     ss = [T.S0, T.S1]
+    pend = []
 
-    def tally(k):
-        wait(V, s_t48[0])
-        judge(k, ss[k % 2], T.b6[:, 0:48])
-        even, odd = T.NH[:, 48 * k:48 * k + 48:2], T.NH[:, 48 * k + 1:48 * k + 48:2]
-        wait(PE, s_zl)
-        pe.matmul(z, T.ZL[:, :], even, k == 0, False)
-        ins = pe.matmul(z, T.ZH[:, :], odd, False, k == 3)
-        if k == 3:
-            do(PE, ins, s_zz)
-        mms(T.b5[:, 3 - k:96:4], [(T.UL[:, :], even), (T.UH[:, :], odd)], s_hh)
+    def judge(k):
+        wait(V, s_t48)
+        done = sig()
+        tt(T.NH[:, 48 * k:48 * k + 48], ss[k % 2][:, 7:384:8], T.b6[:, 0:48], A.is_le, done)
+        pend.append((k, done))
+
+    def tally():
+        while pend:
+            k, done = pend.pop()
+            wait(PE, done, s_zl)
+            even, odd = T.NH[:, 48 * k:48 * k + 48:2], T.NH[:, 48 * k + 1:48 * k + 48:2]
+            pe.matmul(z, T.ZL[:, :], even, False, False)
+            ins = pe.matmul(z, T.ZH[:, :], odd, False, k == 3)
+            if k == 3:
+                do(PE, ins, s_zz)
+            wait(PE, s_ul)
+            mms(T.b5[:, 3 - k:96:4], [(T.UL[:, :], even), (T.UH[:, :], odd)], s_hh)
 
     def other_work(k):
         if k == 0:
-            ts(T.GRP[:, :], T.RG[:, :], pf[:, 14:15], A.is_equal, to=s_gp)
-            s_t48[0] = spread(TK, T.TX, T.b6, T.GRP, s_gp)
+            v.wait_ge(T.sem.ld_d, loads["ld_d"])
+            cp(T.DF[:, :], T.DI[:, :], s_df)
+            ts(T.NL[:, 3:96:4], col(T.L, 0), 8.0, A.add)
+            ts(f(12), f(3), 32.0, A.mult)
+            ts(f(10), f(3), 2.0, A.mult)
+            ts(f(11), f(3), 2.0, A.mult, 1.0, A.add)
         elif k == 1:
             v.wait_ge(T.sem.ra, arrived)
             halves(T.RQA, THA, TLA)
             cp(T.SLI[:, :], T.SLF[:, :])
             ts(T.OWI[:, :], T.RKI[:, :], 11, A.arith_shift_right)
+            ts(f(8), f(12), f(1), A.add, to=s_fe)
         elif k == 2:
             tt(TKA, THA, TLA, A.add)
+            ts(f(9), f(8), 16.0, A.add, to=s_fe)
             ts(T.GMI[:, 0:2], T.SLI[:, :], 7, A.bitwise_and)
             ts(T.GMI[:, 2:4], T.SLI[:, :], 3, A.arith_shift_right, 31, A.bitwise_and)
             ts(T.OW12[:, :], T.OWI[:, :], 12.0, A.mult)
 
-    wait(V, s_rst)
+    wait(V, s_rst, s_m8)
     wait(PE, s_sh)
+    s_mx, s_sa, s_fe = sig(), sig(), sig()
     for k in range(4):
         s_g, s_s, s_n = sig(), sig(), sig()
-        sync(V)
         if k == 0:
+            sync(V)
             v.wait_ge(T.sem.ld_c, loads["ld_c"])
-        gather(T.G, T.C, col(T.L, k), s_g)
-        ts(T.NL[:, 3 - k:96:4], col(T.L, k), 8.0, A.add)
-        if k:
-            tally(k - 1)
         else:
-            for out, col_ in ((T.ZL, 13), (T.ZH, 15)):
-                ts(out[:, :], i128, pf[:, col_:col_ + 1], A.is_equal, pf[:, 17:18], A.mult, to=s_zl)
-        if k == 3:
-            cp(T.GMF[:, :], T.GMI[:, :])
+            sync(V, s_mx, s_l1)
+        gather(T.G, T.C, col(T.L, k), s_g)
+        if k == 0:
+            ts(col(T.MX, 0), T.N0[:, :], 4096.0, A.max, to=s_mx)
+        else:
+            ts(T.NL[:, 3 - k:96:4], col(T.L, k), 8.0, A.add)
         wait(V, s_g)
         scan(ss[k % 2], T.G, s_s)
-        wait(PE, s_s)
-        if k < 3:
-            mms(nb[k % 2], shift(ss[k % 2]), s_n)
-            other_work(k)
-            wait(V, s_n)
-            cp(col(T.L, k + 1), nb[k % 2])
+        if k == 3:
+            tally()
         else:
+            wait(PE, s_s)
+            mms(nb[k % 2], shift(ss[k % 2]), s_n)
+        if k == 0:
+            other_work(0)
+            wait(PE, s_df, s_id)
+            mms(T.b7[:, 0:128], [(T.DF[:, :], T.IDF[:, :])], s_l1p)
+        wait(PE, s_mx, s_zl)
+        pe.matmul(z, T.SCL[:, :], col(T.MX, k), k == 0, False)
+        if k < 3:
+            if k:
+                other_work(k)
+            wait(V, s_s)
+            judge(k)
+            if k < 2:
+                tally()
+            wait(V, s_n)
+            ts(col(T.L, k + 1), nb[k % 2], 4096.0, A.min)
+            ts(col(T.MX, k + 1), nb[k % 2], 4096.0, A.max, to=s_mx)
+            if k == 0:
+                wait(V, s_l1p)
+                ts(T.L1[:, :], T.b7[:, 0:128], 8.0, A.add, to=s_l1)
+        else:
+            wait(PE, s_sc, s_s)
             pe.matmul(z, T.SC0[:, :], ss[1][:, 7:384:16], False, False)
             pe.matmul(z, T.SC1[:, :], ss[1][:, 15:384:16], False, False)
             wait(V, s_s)
-            tally(3)
-    ts(T.GRPA[:, :], T.J8[:, 0:128], pf[:, 14:15], A.is_equal, to=s_gpa)
-    s_t48a = spread(TKA, T.TXA, T.b7, T.GRPA, s_gpa)
+            judge(3)
+            tally()
+            cp(T.GMF[:, :], T.GMI[:, :])
+            ts(T.M48[:, :], i128[:, 0:48], f(20), A.is_equal)
+            wait(V, s_sb, s_ul)
+            tt(T.SA[:, :], T.SB[:, :], T.UL[:, :], A.add, s_sa)
     s_ls = sig()
     wait(V, s_zz)
-    ts(T.LS[:, :], z, -4088.0, A.add, 0.0, A.max, to=s_ls)
+    ts(T.LS[:, :], z, 8.0 - 20480.0, A.add, 0.0, A.max, to=s_ls)
     rid, pid, _ = topo.addr(T.cores[nxt])
     n8 = len(topo.engines(core, T.cores[nxt]))
     wait(GQ, s_ls)
     g.remote_dma(out_ap=T.LSA[:, :], in_ap=T.LS[:, :], remote_sem=T.sem.ls, local_sem=T.sem.l_ls, pid=pid, routing_id=rid,
                  dma_engine_mask=topo.mask(core, T.cores[nxt]))
 
-    s_f1, s_lv1, s_lv2, s_l2p, s_l2 = (sig() for _ in range(5))
-    wait(S, s_l1, s_zf)
-    act.wait_ge(T.sem.ld_fw, loads["ld_fw"])
-    do(S, act.activation(T.F1[:, :], T.FW[:, :].indirect(T.L1[:, :]), F.Copy), s_f1)
-    wait(SQ, s_f1)
-    for c in range(8):
-        load(ys, "ld_d2", T.D2[:, 16 * c:16 * c + 16], T.F1[16 * c:16 * c + 1, :])
-    wait(S, s_re)
+    s_lv1, s_lv2s = sig(), [sig(), sig()]
+    wait(SQ, s_cf)
+    for i in range(2):
+        load(ys, "ld_av", T.RAW[8 + i:128:16, 8:2056], T.TCF[:, :])
+    wait(SQ, s_z, s_zg)
+    for k in range(8):
+        load(ys, "ld_vv", T.VV[16 * k:16 * k + 8, 8:4104], T.vv[:, :])
+    wait(S, s_l1, s_re)
     act.wait_ge(T.sem.ld_av, loads["ld_av"])
     do(S, act.activation(T.LV1[:, 8:2056], T.RAW[:, :].indirect(T.L1[:, :]), F.Copy), s_lv1)
-    pe.wait_ge(T.sem.ld_d2, loads["ld_d2"])
-    mms(T.b2[:, 0:128], [(T.D2[:, :], T.IDF[:, :])], s_l2p)
+    wait(S, s_lv1, s_le)
+    for x, s_lv2 in enumerate(s_lv2s):
+        do(S, act.activation(T.LV2[:, 8 + 1024 * x:1032 + 1024 * x], T.LV1[:, :].indirect(T.L1[:, 64 * x:64 * x + 64]), F.Copy),
+           s_lv2)
+    wait(SQ, s_lv1)
+    for i in range(2):
+        load(ys, "ld_mg", T.RAW[2 + i:128:8, 8:2056], T.LV1[i:128:8, 8:2056])
+    for x, s_lv2 in enumerate(s_lv2s):
+        wait(SQ, s_lv2)
+        for i in range(2):
+            load(ys, "ld_mg", T.RAW[4 + i:128:8, 8 + 1024 * x:1032 + 1024 * x], T.LV2[i:128:8, 8 + 1024 * x:1032 + 1024 * x])
+    one_hot([(ca[a][:, :], i128, f(22 + a), f(21)) for a in range(4)], s_ca)
+    wait(S, s_i5, s_fe)
+    perms = (T.PERM0[:, :], T.PERM1[:, :])
+    one_hot([(perms[0], T.I512[:, 0:256], f(8), 1.0), (perms[1], T.I512[:, 0:256], f(9), 1.0)], s_pm)
 
-    s_ho, s_vl, s_mp, s_mk, s_vg, s_vs, s_se = (sig() for _ in range(7))
+    s_ho, s_vl, s_mp, s_mpa, s_mk, s_mka, s_vg, s_vs, s_se, s_lt = (sig() for _ in range(10))
     wait(V, s_hh)
     sync(V)
     tt(T.HP[:, :], T.b5[:, 0:96], T.NL[:, :], A.mult)
     tt(T.D0[:, :], T.b5[:, 0:96], T.DC[:, :], A.is_lt)
     tt(T.MC[:, :], T.GMF[:, 2:4], T.OW12[:, :], A.add)
-    wait(V, s_l2p)
-    cp(T.L2[:, :], T.b2[:, 0:128], s_l2)
-    wait(S, s_l2)
-    do(S, act.activation(T.LV2[:, 8:2056], T.RAW[:, :].indirect(T.L2[:, :]), F.Copy), s_lv2)
     sync_own(V)
     do(V, v.tensor_tensor_scan(T.HS[:, :], T.D0[:, :], T.HP[:, :], 0.0, A.mult, A.add))
-    for x in (0, 1):
-        ts((T.LT0, T.LT1)[x][:, :], T.RG[:, :], T.GMF[:, x:x + 1], A.is_equal, to=s_pm)
     sync_own(V)
     cp(T.LF[:, :], T.HS[:, 3:96:4])
-    for x in (0, 1):
-        ts((T.LTA0, T.LTA1)[x][:, :], T.J8[:, 0:128], T.GMF[:, x:x + 1], A.is_equal, to=s_pm)
     v.wait_ge(T.sem.ld_vv, loads["ld_vv"])
     sync_own(V)
     gather(T.G, T.VV, T.LF[:, 0:24], s_vg)
+    s_t48a = spread(TKA, T.TXA, 48, T.M48, T.b7[:, 0:192], T.GRPA, s_gpa)
+    for x in (0, 1):
+        ts((T.LT0, T.LT1)[x][:, :], T.RG[:, :], T.GMF[:, x:x + 1], A.is_equal, to=s_lt)
 
-    p01, h2, t48a = T.b3[:, 0:48], T.b5[:, 0:48], T.b7[:, 0:48]
-    ends = slice(7, 384, 8)
-    W0, W1, Z, A0, A1, ACC, PX, X = (T.WK[:, 48 * i:48 * i + 48] for i in range(8))
-    s_01, s_h2, s_a, s_px, s_x2 = (sig() for _ in range(5))
-    s_g, s_v = [sig() for _ in range(3)], [sig() for _ in range(3)]
-    places = T.LSA[:, 0:24]
-    hits = [T.NH[:, 48 * (4 + k):48 * (5 + k)] for k in range(3)]
-    wait(V, s_re, s_le)
+    sel, out4, t48a = T.b3[:, 0:192], T.b5[:, 0:48], T.b7[:, 0:192]
+    s_ga, s_bb, s_h, s_sel, s_rl, s_xv, s_o4, s_ao = (sig() for _ in range(8))
+    wait(V, s_re, s_m2)
     v.wait_ge(T.sem.ld_av, loads["ld_av"])
+    v.wait_ge(T.sem.ld_mg, loads["ld_mg"])
     v.wait_ge(T.sem.ls, n8)
-    gather(T.GB, T.RAW, places, s_g[0])
+    tt(T.GB[:, :], T.RAW[:, :].indirect(T.LSA[:, 0:24]), T.MASK2[:, :], A.mult, s_ga)
     wait(V, s_vg)
     scan(T.S0, T.G, s_vs)
-    wait(V, s_lv1)
-    gather(T.GD, T.LV1, places, s_g[1])
+    wait(V, s_ga)
+    tt(T.BB[:, :], T.GB[:, 0:384:2], T.GB[:, 1:384:2], A.add, s_bb)
     wait(V, s_vs)
     cp(T.HOUT[:, :], T.S0[:, 7:384:8], s_ho)
     wait(GQ, s_ho)
     send3(lambda q: T.HOUT[:, 12 * q:12 * q + 12], T.ANSH[:, 12 * r:12 * r + 12], T.sem.ha, T.sem.l_ha, [4, 2, 2])
-    wait(V, s_g[0])
-    scan(T.V0, T.GB, s_v[0])
-    wait(V, s_g[1])
-    scan(T.V1, T.GD, s_v[1])
-    wait(V, s_t48a, s_v[0])
-    judge(4, T.V0, t48a)
-    wait(V, s_lv2)
-    gather(T.G, T.LV2, places, s_g[2])
-    wait(V, s_v[1])
-    judge(5, T.V1, t48a)
-    ts(T.UL2[:, :], T.UL[:, :], 2.0, A.mult, to=s_u2)
-    wait(PE, s_u2)
-    mms(p01, [(T.UL2[:, :], hits[0]), (T.UL[:, :], hits[1])], s_01)
-    wait(V, s_g[2])
-    scan(T.V2, T.G, s_v[2])
-    wait(V, s_01)
-    ts(Z, p01, 0.0, A.is_equal, to=s_a)
-    ts(W1, p01, 1.0, A.is_equal, to=s_a)
-    ts(W0, p01, 2.0, A.is_ge, to=s_a)
-    wait(V, s_v[2])
-    judge(6, T.V2, t48a)
-    mms(h2, [(T.UL[:, :], hits[2])], s_h2)
-    wait(V, s_a)
-    tt(PX, Z, T.V2[:, ends], A.mult, s_px)
-    tt(A0, W0, T.V0[:, ends], A.mult)
-    tt(A1, W1, T.V1[:, ends], A.mult)
-    sync_own(V)
-    tt(ACC, A0, A1, A.add, s_x2)
-    s_ao = sig()
-    wait(V, s_h2, s_px)
-    tt(X, h2, PX, A.mult, s_x2)
-    wait(V, s_x2)
-    tt(T.AOUT[:, :], ACC, X, A.add, s_ao)
-    wait(GQ, s_ao)
-    send3(lambda q: T.AOUT[:, 12 * q:12 * q + 12], T.ANSA[:, 12 * prv:12 * prv + 12], T.sem.aa, T.sem.l_aa, [4, 2, 2])
-
-    for out, col_ in ((T.PERM0, 8), (T.PERM1, 9)):
-        ts(out[:, :], T.I512[:, 0:256], pf[:, col_:col_ + 1], A.is_equal, to=s_pm)
-    wait(PE, s_pm)
-    perms = (T.PERM0[:, :], T.PERM1[:, :])
+    wait(V, s_t48a, s_bb)
+    tt(T.NHA[:, :], T.BB[:, :], t48a, A.is_le, s_h)
+    wait(PE, s_sa, s_h)
+    mms(sel, [(T.SA[:, :], T.NHA[:, :])], s_sel)
+    wait(PE, s_pm, s_lt)
     mms(T.b4[:, 0:256], [(T.LT0[:, :], perms[0]), (T.LT1[:, :], perms[1])], s_mp)
-    mms(T.b4[:, 256:512], [(T.LTA0[:, :], perms[0]), (T.LTA1[:, :], perms[1])], s_mp)
+    for x in (0, 1):
+        ts((T.LTA0, T.LTA1)[x][:, :], T.J8[:, 0:128], T.GMF[:, x:x + 1], A.is_equal, to=s_p4)
+    wait(V, s_sel)
+    ts(sel, sel, 0.0, A.max, to=s_rl)
+    wait(V, s_rl)
+    tt(T.XV[:, :], sel, T.BB[:, :], A.mult, s_xv)
+    wait(PE, s_ca, s_xv)
+    mms(out4, [(ca[a][:, :], T.XV[:, a:192:4]) for a in range(4)], s_o4)
+
     for x, rv in ((0, T.RV0), (1, T.RV1)):
-        ts(rv[:, :], T.I128[:, 0:16], pf[:, 10 + x:11 + x], A.is_equal, T.MC[:, x:x + 1], A.mult, to=s_p4)
+        ts(rv[:, :], T.I128[:, 0:16], f(10 + x), A.is_equal, T.MC[:, x:x + 1], A.mult, to=s_p4)
     wait(V, s_j16)
-    ts(T.LREP[:, :], T.J16[:, :], pf[:, 1:2], A.is_equal, to=s_p4)
+    ts(T.LREP[:, :], T.J16[:, :], f(1), A.is_equal, to=s_p4)
     wait(PE, s_p4)
     mms(T.b0[:, 0:16], [(T.LREP[:, :], T.RV0[:, :]), (T.LREP[:, :], T.RV1[:, :])], s_vl)
+    mms(T.b2[:, 0:256], [(T.LTA0[:, :], perms[0]), (T.LTA1[:, :], perms[1])], s_mpa)
     wait(S, s_mp)
-    do(S, act.activation(T.MSK[:, :], T.b4[:, :], F.Copy), s_mk)
-    wait(V, s_ho, s_ao)
+    do(S, act.activation(T.MSK[:, :], T.b4[:, 0:256], F.Copy), s_mk)
+    wait(S, s_mpa)
+    do(S, act.activation(T.MSKA[:, :], T.b2[:, 0:256], F.Copy), s_mka)
+    wait(V, s_ho)
     cp(T.ANSH[:, 12 * r:12 * r + 12], T.HOUT[:, 12 * r:12 * r + 12])
-    cp(T.ANSA[:, 12 * prv:12 * prv + 12], T.AOUT[:, 12 * r:12 * r + 12])
-    ts(T.SEL[:, :], T.I128[:, 0:8], pf[:, 0:1], A.is_equal, to=s_se)
-    ts(T.SELA[:, :], T.I128[:, 0:8], pf[:, 14:15], A.is_equal, to=s_se)
+    ts(T.SEL[:, :], T.I128[:, 0:8], f(0), A.is_equal, to=s_se)
+    ts(T.SELA[:, :], T.I128[:, 0:8], f(14), A.is_equal, to=s_se)
+    wait(V, s_o4)
+    cp(T.AOUT[:, :], out4, s_ao)
+    wait(GQ, s_ao)
+    send3(lambda q: T.AOUT[:, 12 * q:12 * q + 12], T.ANSA[:, 12 * prv:12 * prv + 12], T.sem.aa, T.sem.l_aa, [4, 2, 2])
     wait(V, s_vl)
     cp(T.VL[:, :], T.b0[:, 0:16])
+    wait(V, s_ao)
+    cp(T.ANSA[:, 12 * prv:12 * prv + 12], T.AOUT[:, 12 * r:12 * r + 12])
     landed = sum((4, 2, 2)[[o for o in range(n_ranks) if o != q].index(r)] for q in others)
     s_xh, s_x = sig(), [sig(), sig()]
     s_y, s_ys = [sig(), sig()], [sig(), sig()]
     sync(V)
     wait(V, s_mk)
     v.wait_ge(T.sem.ha, landed)
-    tt(T.XH[:, :], T.ANSH[:, :].indirect(T.VL[:, 0:16]), T.MSK[:, 0:256], A.mult, s_xh)
+    tt(T.XH[:, :], T.ANSH[:, :].indirect(T.VL[:, 0:16]), T.MSK[:, :], A.mult, s_xh)
+    wait(V, s_mka)
     v.wait_ge(T.sem.aa, landed)
     wait(PE, s_xh, s_se)
     part = [slice(0, 128), slice(128, 256)]
     bank = [T.b6[0:8, 0:128], T.b7[0:8, 0:128]]
     for i in range(2):
-        tt(T.XA[:, part[i]], T.ANSA[:, :].indirect(T.VL[:, 8 * i:8 * i + 8]), T.MSK[:, 256 + 128 * i:384 + 128 * i], A.mult,
-           s_x[i])
+        tt(T.XA[:, part[i]], T.ANSA[:, :].indirect(T.VL[:, 8 * i:8 * i + 8]), T.MSKA[:, part[i]], A.mult, s_x[i])
         pe.matmul(bank[i], T.SEL[:, :], T.XH[:, part[i]], True, False)
     for i in range(2):
         wait(PE, s_x[i])

import numpy as np
from concourse.bass import DstId, RemoteDMATransfer
from concourse.mybir import AluOpType as A, AxisListType, ActivationFunctionType as F

WIDTHS = {
    "int32": dict(RKI=2, RTI=2, PCI=1, PBI=9, OWI=2, KVI=6, SLI=2, GMI=4, HD=2048, C=4104, DI=128, ATC=128),
    "float32": dict(PFC=36, I128=128, I512=512, RG=128, SR=128, J8=384, J2=384, J16=128, JH=16, R12=12, M12=12, OW12=2,
                    KVF=6, SLF=2, GMF=4, MC=2, EF=8, TM=24, TX=48, TXA=192, M48=48, GRP=128, GRPA=128, SHLO=128, SHHI=128,
                    SC0=128, SC1=128, SCL=128, MASKHD=16, MASK8=384, MASK2=384, RST8=384, VV=4104, RAW=2064,
                    LV1=2064, LV2=2064, TCF=128, G0=64, N0=24, G=384, GB=384, S0=384, S1=384, BB=192, XV=192,
                    CA0=128, CA1=128, CA2=128, CA3=128, MX=96, NL=96, DC=96, D0=96, HP=96, HS=96, HOUT=48, AOUT=48,
                    ANSH=48, ANSA=48, MSK=256, MSKA=256, SEL=8, SELA=8, XH=256, XA=256),
    "bfloat16": dict(TRI=128, EYE=128, TRIP=128, TRIN=128, ONES=128, NONES=128, GE=10, UL=128, UH=128,
                     ZL=128, ZH=128, NH=192, NHA=192, SA=128, SB=128, LREP=128, RV0=16, RV1=16, LT0=128, LT1=128,
                     LTA0=128, LTA1=128, PERM0=256, PERM1=256),
    "float16": dict(LK0=128, LK1=128, RK0=16, RK1=16, DF=128, IDF=128),
    "uint16": dict(KREQ=16, RQ=32, RQA=32, L=96, LF=24, LS=24, LSA=24, VL=16, L1=128),
}
SCRATCH = {b: ("sbuf", [128, w], d) for d in WIDTHS for b, w in WIDTHS[d].items()}
SCRATCH["YS"] = ("sbuf", [8, 256], "float32")
SCRATCH.update({"b%d" % i: ("psum", [128, 512], "float32") for i in range(8)})
SEMAPHORES = ["vq", "tq", "aq", "rq", "ra", "ls", "ha", "aa", "l_rq", "l_ra", "l_ls", "l_ha", "l_aa", "sent",
              "ld_rk", "ld_rt", "ld_hd", "ld_c", "ld_vv", "ld_d", "ld_at", "ld_av", "ld_mg", "st"]
SEMAPHORES += ["k%d" % i for i in range(126)]


def queue(eng, own):
    return {"e": eng, "own": own, "n": 0, "w": 0, "p": [], "seen": {}}


def do(Q, ins, sig=None):
    if sig is None:
        ins.then_inc(Q["own"], 1)
        Q["n"] += 1
    else:
        ins.then_inc(sig["s"], 1)
        sig["n"] += 1
        if sig not in Q["p"]:
            Q["p"].append(sig)


def wait(Q, *sigs):
    for s in sigs:
        if Q["seen"].get(s["k"], 0) < s["n"]:
            Q["e"].wait_ge(s["s"], s["n"])
            Q["seen"][s["k"]] = s["n"]


def sync_own(Q):
    if Q["n"] > Q["w"]:
        Q["e"].wait_ge(Q["own"], Q["n"])
        Q["w"] = Q["n"]


def sync(Q, *but):
    sync_own(Q)
    left = [s for s in Q["p"] if s in but]
    wait(Q, *[s for s in Q["p"] if s not in but])
    Q["p"].clear()
    Q["p"].extend(left)


def rank_program(g, core, T, topo):
    r = T.rank_of(core)
    if r is None:
        return
    n_ranks = len(T.cores)
    nxt, prv = (r + 1) % n_ranks, (r - 1) % n_ranks
    others = [q for q in range(n_ranks) if q != r]
    num = [0]

    def sig():
        num[0] += 1
        return {"s": T.sem["k%d" % (num[0] - 1)], "n": 0, "k": num[0]}

    V, PE, S = queue(g.vector, T.sem.vq), queue(g.tensor, T.sem.tq), queue(g.scalar, T.sem.aq)
    GQ, SQ = {"e": g, "seen": {}}, {"e": g.sync, "seen": {}}
    v, pe, act = g.vector, g.tensor, g.scalar

    def send3(src, dst, rs, ls, counts):
        first, trs = 0, []
        for i, q in enumerate(others):
            rid, pid, _ = topo.addr(T.cores[q])
            m = sum(1 << e for e in topo.engines(core, T.cores[q])[first:first + counts[i]])
            trs.append(RemoteDMATransfer(dst_ids=[DstId(rid=rid, pnc=pid)], dma_engine_mask=m, remote_sem=rs, src=src(q),
                                         dst=dst))
            first += counts[i]
        g.remote_dma_fused(trs, local_sem=ls)

    loads = {}

    def load(q, name, out, in_):
        q.dma_start(out, in_).then_inc(T.sem[name], 16)
        loads[name] = loads.get(name, 0) + 16

    ap, at, av = T["ap"], T["at"], T["av"]
    load(g.sync, "ld_rk", T.RKI[:, :], T.rk[:, :])
    load(g.scalar, "ld_rt", T.RTI[:, :], T.rt[:, :])
    for k in range(8):
        load(g.sync, "ld_hd", T.HD[16 * k:16 * k + 8, :], T.hd[:, :])
        load(g.scalar, "ld_hd", T.HD[16 * k + 8:16 * k + 16, :], T.hd[:, :])
    for k in range(8):
        load(g.sync if k % 2 == 0 else g.scalar, "ld_c", T.C[16 * k:16 * k + 8, 0:4096], T.vp[:, :])
    load(g.scalar, "ld_at", T.ATC[:, :], at[:, :])
    load(g.sync, "ld_c", T.C[8:16, 0:4096], T.vt[:, :])

    s_pc, s_i, s_sr, s_j8, s_i5, s_ot, s_j2, s_j16, s_zg = (sig() for _ in range(9))

    def iota(out, pattern, s, base=0, cm=0, flag=True):
        kw = {"allow_small_or_imprecise_dtypes": True} if flag else {}
        g.iota(out, pattern, base, cm, **kw).then_inc(s["s"], 1)
        s["n"] += 1

    iota(T.PCI[:, :], [[0, 1]], s_pc, 0, 1, False)
    iota(T.I128[:, :], [[1, 128]], s_i)
    iota(T.SR[:, :], [[1, 8], [8, 2], [16, 8]], s_sr, 512)
    iota(T.J8[:, :], [[0, 48], [1, 8]], s_j8)
    iota(T.RG[:, :], [[1, 8], [0, 16]], s_ot)
    iota(T.R12[:, :], [[1, 6], [8, 2]], s_ot)
    iota(T.JH[:, :], [[1, 2], [0, 8]], s_ot)

    def ts(out, in0, s1, op0, s2=None, op1=None, to=None):
        do(V, v.tensor_scalar(out, in0, s1, None, op0) if op1 is None else v.tensor_scalar(out, in0, s1, s2, op0, op1), to)

    def tt(out, a, b, op, to=None):
        do(V, v.tensor_tensor(out, a, b, op), to)

    def cp(out, in_, to=None):
        do(V, v.tensor_copy(out, in_), to)

    s_one, s_ge, s_sh, s_gp, s_gpa, s_kk, s_id, s_eb, s_zl, s_ca, s_u2, s_m2 = (sig() for _ in range(12))
    do(V, v.memset(T.ONES[:, :], 1.0), s_one)
    do(V, v.memset(T.NONES[:, :], -1.0), s_one)
    do(V, v.memset(T.GE[:, 0:10:5], 1.0), s_ge)
    do(V, v.memset(T.GE[:, 4:10:5], 0.0), s_ge)
    wait(V, s_pc)
    pb, pf = T.PBI, T.PFC
    big = float(1048576)
    i128, p, hi, lo = T.I128[:, :], pf[:, 4:5], pf[:, 2:3], pf[:, 5:6]

    def f(i):
        return pf[:, i:i + 1]

    cp(p, T.PCI[:, :])
    ts(pb[:, 2:3], T.PCI[:, :], 3, A.arith_shift_right, 1, A.bitwise_and)
    wait(V, s_i)
    sync(V)
    ts(T.TRI[:, :], i128, p, A.is_gt)
    ts(T.EYE[:, :], i128, p, A.is_equal, 512.0, A.mult)
    cp(hi, pb[:, 2:3])
    for rk in (T.RK0, T.RK1):
        ts(rk[:, 3:16:4], i128[:, 0:4], 0.0, A.mult, to=s_kk)
    sync(V)
    tt(T.TRIP[:, :], T.TRI[:, :], T.EYE[:, :], A.add, s_one)
    ts(f(16), hi, big, A.mult, to=s_eb)
    sync(V)
    ts(T.TRIN[:, :], T.TRIP[:, :], -1.0, A.mult, to=s_one)

    s_pos, s_kp, s_kq, s_own, s_ef = (sig() for _ in range(5))
    v.wait_ge(T.sem.ld_rk, loads["ld_rk"])
    for q in range(1, n_ranks):
        ts(T.GE[:, q:10:5], T.RKI[:, :], 2048 * q, A.is_ge, to=s_ge)
    v.wait_ge(T.sem.ld_rt, loads["ld_rt"])
    ts(T.KVI[:, 0:6:3], T.RKI[:, :], 2047, A.bitwise_and)
    ts(T.KVI[:, 1:6:3], T.RTI[:, :], 10, A.arith_shift_right)
    ts(T.KVI[:, 2:6:3], T.RTI[:, :], 1023, A.bitwise_and)
    wait(PE, s_one, s_ge)

    def mms(out, pairs, to):
        for i, (a, b) in enumerate(pairs):
            ins = pe.matmul(out, a, b, i == 0, i == len(pairs) - 1)
        do(PE, ins, to)

    ge = [T.GE[:, i:i + 4] for i in (0, 1, 5, 6)]
    mms(T.b0[:, 0:4], [(T.TRIP[:, :], ge[0]), (T.TRIN[:, :], ge[1])], s_pos)
    mms(T.b0[:, 4:8], [(T.TRIP[:, :], ge[2]), (T.TRIN[:, :], ge[3]), (T.ONES[:, :], ge[0]), (T.NONES[:, :], ge[1])], s_pos)
    sync(V)
    cp(T.KVF[:, :], T.KVI[:, :], s_ef)
    tt(T.EF[:, 0:4], ge[0], ge[1], A.subtract, s_ef)
    tt(T.EF[:, 4:8], ge[2], ge[3], A.subtract, s_ef)
    wait(V, s_pos, s_sr)
    do(V, v.tensor_reduce(T.SLF[:, 0:1], T.b0[:, 0:4], AxisListType.X, A.max))
    do(V, v.tensor_reduce(T.SLF[:, 1:2], T.b0[:, 4:8], AxisListType.X, A.max))
    wait(V, s_ef)
    for x, rk in ((0, T.RK0), (1, T.RK1)):
        for i in range(3):
            ts(rk[:, i:16:4], T.EF[:, 4 * x:4 * x + 4], T.KVF[:, 3 * x + i:3 * x + i + 1], A.mult, to=s_kk)
    sync_own(V)
    for x, lk in ((0, T.LK0), (1, T.LK1)):
        ts(lk[:, :], T.SR[:, :], T.SLF[:, x:x + 1], A.is_equal, to=s_kk)
    wait(PE, s_kk)
    mms(T.b1[:, 0:16], [(T.LK0[:, :], T.RK0[:, :]), (T.LK1[:, :], T.RK1[:, :])], s_kp)
    bits = ((0, 15), (3, 15), (3, 1), (0, 7), (4, 7), (0, 1), (4, 1), (5, 3))
    for i in (0, 1, 3, 4):
        ts(pb[:, i:i + 1], T.PCI[:, :], bits[i][0], A.arith_shift_right, bits[i][1], A.bitwise_and)
    wait(V, s_kp)
    cp(T.KREQ[:, :], T.b1[:, 0:16], s_kq)
    cp(T.RQ[:, 8 * r:8 * r + 4], T.b1[:, 4 * r:4 * r + 4], s_own)
    cp(T.RQA[:, 8 * r:8 * r + 4], T.b1[:, 4 * prv:4 * prv + 4], s_own)
    wait(GQ, s_kq)
    send3(lambda q: T.KREQ[:, 4 * q:4 * q + 4], T.RQ[:, 8 * r:8 * r + 4], T.sem.rq, T.sem.l_rq, [2, 2, 2])
    g.sem_inc(T.sem.sent, 1)

    def of_archive(z):
        q = (z - 1) % n_ranks
        return T.KREQ[:, 4 * q:4 * q + 4]

    send3(of_archive, T.RQA[:, 8 * r:8 * r + 4], T.sem.ra, T.sem.l_ra, [2, 2, 2])
    iota(T.J2[:, :], [[0, 192], [1, 2]], s_j2)
    iota(T.I512[:, :], [[1, 512]], s_i5)
    iota(T.J16[:, :], [[0, 8], [1, 16]], s_j16)
    iota(T.VV[:, 2048:4104], [[0, 2056]], s_zg)

    s_rst, s_z, s_df, s_cf, s_l1p, s_l1, s_re, s_le, s_sc, s_fc, s_m8, s_ul, s_fd, s_sb = (sig() for _ in range(14))
    for i in (5, 6, 7):
        ts(pb[:, i:i + 1], T.PCI[:, :], bits[i][0], A.arith_shift_right, bits[i][1], A.bitwise_and)
    ts(lo, hi, -1.0, A.mult, 1.0, A.add, to=s_fc)
    ts(f(7), p, -8.0, A.add, to=s_fc)
    ts(f(6), p, 8.0, A.add)
    sync_own(V)
    cp(f(3), pb[:, 3:4], s_fc)
    cp(pf[:, 0:2], pb[:, 0:2])
    cp(f(14), pb[:, 4:5])
    cp(pf[:, 18:21], pb[:, 5:8])
    wait(S, s_j8)
    do(S, act.activation(T.RST8[:, :], T.J8[:, :], F.Sign), s_rst)
    wait(S, s_eb)
    for b in range(0, 2064, 384):
        n = min(384, 2064 - b)
        do(S, act.activation(T.RAW[:, b:b + n], T.J8[:, 0:n], F.Identity, bias=f(16), scale=0.0), s_re)

    def one_hot(items, to):
        mid = sig()
        for out, in_, col_, role in items:
            do(S, act.activation(out, in_, F.Abs, bias=col_, scale=-1.0), mid)
        wait(S, mid)
        for out, in_, col_, role in items:
            do(S, act.activation(out, out, F.Relu, bias=role, scale=-1.0), to)

    wait(S, s_fc)
    one_hot([(T.MASK8[:, :], T.J8[:, :], f(3), 1.0)], s_m8)
    one_hot([(T.UL[:, :], i128, f(7), hi), (T.UH[:, :], i128, p, hi)], s_ul)
    for b in range(0, 2048, 384):
        n = min(384, 2048 - b)
        do(S, act.activation(T.VV[:, b:b + n], T.J8[:, 0:n], F.Copy, scale=0.0), s_z)
    for a in (0, 2056):
        do(S, act.activation(T.LV1[:, a:a + 8], T.J8[:, 0:8], F.Identity, bias=f(16), scale=0.0), s_le)

    ys = g.sync
    ys.wait_ge(T.sem.sent, 1)
    for k in range(1, 8):
        load(ys, "ld_c", T.C[16 * k + 8:16 * k + 16, 0:4096], T.vt[:, :])
    for c in range(8):
        load(ys, "ld_d", T.DI[:, 16 * c:16 * c + 16], ap[c:c + 1, :])
    wait(SQ, s_re)
    for i in range(2):
        load(ys, "ld_av", T.RAW[i:128:16, 8:2056], av[:, :])

    wait(V, s_j8, s_ot)
    sync(V)
    ts(T.MASKHD[:, :], T.JH[:, :], hi, A.is_equal)
    for out, col_ in ((T.SHHI, f(6)), (T.SHLO, p)):
        ts(out[:, :], i128, col_, A.is_equal, lo, A.mult, to=s_sh)
    ts(T.C[:, 4096:4104], i128[:, 0:8], 0.0, A.mult, f(16), A.add)
    ts(f(30), lo, 4096.0, A.mult)
    ts(f(13), f(3), 16.0, A.mult, f(14), A.add, to=s_fd)
    ts(f(17), hi, -8192.0, A.mult)
    ts(f(22), f(0), -1.0, A.mult, p, A.add)
    ts(f(20), f(3), 8.0, A.mult, f(20), A.add)
    ts(T.M12[:, :], T.R12[:, :], f(0), A.is_equal)
    ts(f(32), f(18), 2.0, A.mult, -1.0, A.add, to=s_fd)
    ts(f(33), f(18), -1.0, A.mult, 1.0, A.add, to=s_fd)
    ts(f(34), f(19), 2.0, A.mult, -1.0, A.add, to=s_fd)
    ts(f(35), f(19), -1.0, A.mult, 1.0, A.add, to=s_fd)
    sync(V)
    ts(T.C[:, 4096:4104], T.C[:, 4096:4104], f(30), A.add)
    ts(f(15), f(13), 8.0, A.add, to=s_fd)
    ts(f(31), hi, 8.0, A.mult, f(13), A.add)
    ts(f(20), hi, 4.0, A.mult, f(20), A.add)
    ts(f(22), f(22), f(18), A.add, to=s_fd)
    ts(f(21), f(0), 6.0, A.is_lt, to=s_fd)
    ts(f(27), p, -5.0, A.add, to=s_fd)
    ts(T.IDF[:, :], i128, p, A.is_equal, to=s_id)

    arrived = 2 * len(others)
    TH, TL, TK, THA, TLA, TKA = (T.TM[:, 4 * i:4 * i + 4] for i in range(6))

    def halves(rq, th, tl):
        ts(th, rq[:, 1:32:8], 1024.0, A.mult)
        cp(tl, rq[:, 2:32:8])

    def spread(tk, tx, width, mask, bank, grp, s_grp):
        s_tx, s_p = sig(), sig()
        for q in range(n_ranks):
            ts(tx[:, width * q:width * q + width], mask[:, :], tk[:, q:q + 1], A.mult, to=s_tx)
        wait(PE, s_grp, s_tx)
        mms(bank, [(grp[:, :], tx[:, :])], s_p)
        return s_p

    def col(buf, k):
        return buf[:, 24 * k:24 * k + 24]

    nb = [T.b1[:, 0:24], T.b2[:, 0:24]]
    ca = [T.CA0, T.CA1, T.CA2, T.CA3]
    s_tk, s_g0, s_ad = sig(), sig(), sig()
    wait(V, s_own)
    v.wait_ge(T.sem.rq, arrived)
    v.wait_ge(T.sem.ld_hd, loads["ld_hd"])
    sync(V)
    for q in range(n_ranks):
        tt(T.G0[:, 16 * q:16 * q + 16], T.HD[:, :].indirect(T.RQ[:, 8 * q:8 * q + 1]), T.MASKHD[:, :], A.mult, s_g0)
    halves(T.RQ, TH, TL)
    wait(V, s_g0)
    for q in range(n_ranks):
        tt(T.N0[:, 6 * q:6 * q + 6], T.G0[:, 16 * q:16 * q + 6], T.G0[:, 16 * q + 8:16 * q + 14], A.add, s_ad)
    sync(V)
    ts(col(T.L, 0), T.N0[:, :], 4096.0, A.min)
    tt(TK, TH, TL, A.add, s_tk)
    do(V, v.memset(T.DC[:, :], 0.5))
    ts(T.GRP[:, :], T.RG[:, :], f(14), A.is_equal, to=s_gp)
    sync_own(V)
    wait(V, s_tk)
    s_t48 = spread(TK, T.TX, 12, T.M12, T.b6[:, 0:48], T.GRP, s_gp)
    do(V, v.memset(T.DC[:, 0:96:4], -1.0))
    v.wait_ge(T.sem.ld_at, loads["ld_at"])
    cp(T.TCF[:, :], T.ATC[:, :], s_cf)
    for a in range(1, 4):
        ts(f(22 + a), f(22), 2.0 * a, A.add, to=s_fd)
    ts(T.SCL[:, :], i128, f(31), A.is_equal, to=s_zl)
    for out, col_ in ((T.ZL, 13), (T.ZH, 15)):
        ts(out[:, :], i128, f(col_), A.is_equal, f(17), A.mult, to=s_zl)
    wait(S, s_fd, s_j2)
    one_hot([(T.SC0[:, :], i128, f(13), lo), (T.SC1[:, :], i128, f(15), lo)], s_sc)
    do(S, act.activation(T.MASK2[:, :], T.J2[:, :], F.Identity, bias=f(33), scale=f(32)), s_m2)
    do(S, act.activation(T.GRPA[:, :], T.J2[:, 0:128], F.Identity, bias=f(35), scale=f(34)), s_gpa)
    do(S, act.activation(T.SB[:, :], i128, F.Abs, bias=f(27), scale=-1.0), s_u2)
    wait(S, s_u2)
    one_hot([(T.SB[:, :], T.SB[:, :], 1.0, hi)], s_u2)
    wait(S, s_u2)
    do(S, act.activation(T.SB[:, :], T.SB[:, :], F.Copy, scale=-8.0), s_sb)

    def gather(out, win, lst, to=None):
        tt(out[:, :], win[:, :].indirect(lst), T.MASK8[:, :], A.mult, to)

    def scan(out, data, to=None):
        do(V, v.tensor_tensor_scan(out[:, :], T.RST8[:, :], data[:, :], 0.0, A.mult, A.add), to)

    def shift(s):
        return [(T.SHLO[:, :], s[:, 7:384:16]), (T.SHHI[:, :], s[:, 15:384:16])]

    z, s_zz, s_hh, s_p4, s_pm = T.b3[:, 0:24], sig(), sig(), sig(), sig()
    ss = [T.S0, T.S1]
    pend = []

    def judge(k):
        wait(V, s_t48)
        done = sig()
        tt(T.NH[:, 48 * k:48 * k + 48], ss[k % 2][:, 7:384:8], T.b6[:, 0:48], A.is_le, done)
        pend.append((k, done))

    def tally():
        while pend:
            k, done = pend.pop()
            wait(PE, done, s_zl)
            even, odd = T.NH[:, 48 * k:48 * k + 48:2], T.NH[:, 48 * k + 1:48 * k + 48:2]
            pe.matmul(z, T.ZL[:, :], even, False, False)
            ins = pe.matmul(z, T.ZH[:, :], odd, False, k == 3)
            if k == 3:
                do(PE, ins, s_zz)
            wait(PE, s_ul)
            mms(T.b5[:, 3 - k:96:4], [(T.UL[:, :], even), (T.UH[:, :], odd)], s_hh)

    def other_work(k):
        if k == 0:
            v.wait_ge(T.sem.ld_d, loads["ld_d"])
            cp(T.DF[:, :], T.DI[:, :], s_df)
            ts(T.NL[:, 3:96:4], col(T.L, 0), 8.0, A.add)
            ts(f(12), f(3), 32.0, A.mult)
            ts(f(10), f(3), 2.0, A.mult)
            ts(f(11), f(3), 2.0, A.mult, 1.0, A.add)
        elif k == 1:
            v.wait_ge(T.sem.ra, arrived)
            halves(T.RQA, THA, TLA)
            cp(T.SLI[:, :], T.SLF[:, :])
            ts(T.OWI[:, :], T.RKI[:, :], 11, A.arith_shift_right)
            ts(f(8), f(12), f(1), A.add, to=s_fe)
        elif k == 2:
            tt(TKA, THA, TLA, A.add)
            ts(f(9), f(8), 16.0, A.add, to=s_fe)
            ts(T.GMI[:, 0:2], T.SLI[:, :], 7, A.bitwise_and)
            ts(T.GMI[:, 2:4], T.SLI[:, :], 3, A.arith_shift_right, 31, A.bitwise_and)
            ts(T.OW12[:, :], T.OWI[:, :], 12.0, A.mult)

    wait(V, s_rst, s_m8)
    wait(PE, s_sh)
    s_mx, s_sa, s_fe = sig(), sig(), sig()
    for k in range(4):
        s_g, s_s, s_n = sig(), sig(), sig()
        if k == 0:
            sync(V)
            v.wait_ge(T.sem.ld_c, loads["ld_c"])
        else:
            sync(V, s_mx, s_l1)
        gather(T.G, T.C, col(T.L, k), s_g)
        if k == 0:
            ts(col(T.MX, 0), T.N0[:, :], 4096.0, A.max, to=s_mx)
        else:
            ts(T.NL[:, 3 - k:96:4], col(T.L, k), 8.0, A.add)
        wait(V, s_g)
        scan(ss[k % 2], T.G, s_s)
        if k == 3:
            tally()
        else:
            wait(PE, s_s)
            mms(nb[k % 2], shift(ss[k % 2]), s_n)
        if k == 0:
            other_work(0)
            wait(PE, s_df, s_id)
            mms(T.b7[:, 0:128], [(T.DF[:, :], T.IDF[:, :])], s_l1p)
        wait(PE, s_mx, s_zl)
        pe.matmul(z, T.SCL[:, :], col(T.MX, k), k == 0, False)
        if k < 3:
            if k:
                other_work(k)
            wait(V, s_s)
            judge(k)
            if k < 2:
                tally()
            wait(V, s_n)
            ts(col(T.L, k + 1), nb[k % 2], 4096.0, A.min)
            ts(col(T.MX, k + 1), nb[k % 2], 4096.0, A.max, to=s_mx)
            if k == 0:
                wait(V, s_l1p)
                ts(T.L1[:, :], T.b7[:, 0:128], 8.0, A.add, to=s_l1)
        else:
            wait(PE, s_sc, s_s)
            pe.matmul(z, T.SC0[:, :], ss[1][:, 7:384:16], False, False)
            pe.matmul(z, T.SC1[:, :], ss[1][:, 15:384:16], False, False)
            wait(V, s_s)
            judge(3)
            tally()
            cp(T.GMF[:, :], T.GMI[:, :])
            ts(T.M48[:, :], i128[:, 0:48], f(20), A.is_equal)
            wait(V, s_sb, s_ul)
            tt(T.SA[:, :], T.SB[:, :], T.UL[:, :], A.add, s_sa)
    s_ls = sig()
    wait(V, s_zz)
    ts(T.LS[:, :], z, 8.0 - 20480.0, A.add, 0.0, A.max, to=s_ls)
    rid, pid, _ = topo.addr(T.cores[nxt])
    n8 = len(topo.engines(core, T.cores[nxt]))
    wait(GQ, s_ls)
    g.remote_dma(out_ap=T.LSA[:, :], in_ap=T.LS[:, :], remote_sem=T.sem.ls, local_sem=T.sem.l_ls, pid=pid, routing_id=rid,
                 dma_engine_mask=topo.mask(core, T.cores[nxt]))

    s_lv1, s_lv2s = sig(), [sig(), sig()]
    wait(SQ, s_cf)
    for i in range(2):
        load(ys, "ld_av", T.RAW[8 + i:128:16, 8:2056], T.TCF[:, :])
    wait(SQ, s_z, s_zg)
    for k in range(8):
        load(ys, "ld_vv", T.VV[16 * k:16 * k + 8, 8:4104], T.vv[:, :])
    wait(S, s_l1, s_re)
    act.wait_ge(T.sem.ld_av, loads["ld_av"])
    do(S, act.activation(T.LV1[:, 8:2056], T.RAW[:, :].indirect(T.L1[:, :]), F.Copy), s_lv1)
    wait(S, s_lv1, s_le)
    for x, s_lv2 in enumerate(s_lv2s):
        do(S, act.activation(T.LV2[:, 8 + 1024 * x:1032 + 1024 * x], T.LV1[:, :].indirect(T.L1[:, 64 * x:64 * x + 64]), F.Copy),
           s_lv2)
    wait(SQ, s_lv1)
    for i in range(2):
        load(ys, "ld_mg", T.RAW[2 + i:128:8, 8:2056], T.LV1[i:128:8, 8:2056])
    for x, s_lv2 in enumerate(s_lv2s):
        wait(SQ, s_lv2)
        for i in range(2):
            load(ys, "ld_mg", T.RAW[4 + i:128:8, 8 + 1024 * x:1032 + 1024 * x], T.LV2[i:128:8, 8 + 1024 * x:1032 + 1024 * x])
    one_hot([(ca[a][:, :], i128, f(22 + a), f(21)) for a in range(4)], s_ca)
    wait(S, s_i5, s_fe)
    perms = (T.PERM0[:, :], T.PERM1[:, :])
    one_hot([(perms[0], T.I512[:, 0:256], f(8), 1.0), (perms[1], T.I512[:, 0:256], f(9), 1.0)], s_pm)

    s_ho, s_vl, s_mp, s_mpa, s_mk, s_mka, s_vg, s_vs, s_se, s_lt = (sig() for _ in range(10))
    wait(V, s_hh)
    sync(V)
    tt(T.HP[:, :], T.b5[:, 0:96], T.NL[:, :], A.mult)
    tt(T.D0[:, :], T.b5[:, 0:96], T.DC[:, :], A.is_lt)
    tt(T.MC[:, :], T.GMF[:, 2:4], T.OW12[:, :], A.add)
    sync_own(V)
    do(V, v.tensor_tensor_scan(T.HS[:, :], T.D0[:, :], T.HP[:, :], 0.0, A.mult, A.add))
    sync_own(V)
    cp(T.LF[:, :], T.HS[:, 3:96:4])
    v.wait_ge(T.sem.ld_vv, loads["ld_vv"])
    sync_own(V)
    gather(T.G, T.VV, T.LF[:, 0:24], s_vg)
    s_t48a = spread(TKA, T.TXA, 48, T.M48, T.b7[:, 0:192], T.GRPA, s_gpa)
    for x in (0, 1):
        ts((T.LT0, T.LT1)[x][:, :], T.RG[:, :], T.GMF[:, x:x + 1], A.is_equal, to=s_lt)

    sel, out4, t48a = T.b3[:, 0:192], T.b5[:, 0:48], T.b7[:, 0:192]
    s_ga, s_bb, s_h, s_sel, s_rl, s_xv, s_o4, s_ao = (sig() for _ in range(8))
    wait(V, s_re, s_m2)
    v.wait_ge(T.sem.ld_av, loads["ld_av"])
    v.wait_ge(T.sem.ld_mg, loads["ld_mg"])
    v.wait_ge(T.sem.ls, n8)
    tt(T.GB[:, :], T.RAW[:, :].indirect(T.LSA[:, 0:24]), T.MASK2[:, :], A.mult, s_ga)
    wait(V, s_vg)
    scan(T.S0, T.G, s_vs)
    wait(V, s_ga)
    tt(T.BB[:, :], T.GB[:, 0:384:2], T.GB[:, 1:384:2], A.add, s_bb)
    wait(V, s_vs)
    cp(T.HOUT[:, :], T.S0[:, 7:384:8], s_ho)
    wait(GQ, s_ho)
    send3(lambda q: T.HOUT[:, 12 * q:12 * q + 12], T.ANSH[:, 12 * r:12 * r + 12], T.sem.ha, T.sem.l_ha, [4, 2, 2])
    wait(V, s_t48a, s_bb)
    tt(T.NHA[:, :], T.BB[:, :], t48a, A.is_le, s_h)
    wait(PE, s_sa, s_h)
    mms(sel, [(T.SA[:, :], T.NHA[:, :])], s_sel)
    wait(PE, s_pm, s_lt)
    mms(T.b4[:, 0:256], [(T.LT0[:, :], perms[0]), (T.LT1[:, :], perms[1])], s_mp)
    for x in (0, 1):
        ts((T.LTA0, T.LTA1)[x][:, :], T.J8[:, 0:128], T.GMF[:, x:x + 1], A.is_equal, to=s_p4)
    wait(V, s_sel)
    ts(sel, sel, 0.0, A.max, to=s_rl)
    wait(V, s_rl)
    tt(T.XV[:, :], sel, T.BB[:, :], A.mult, s_xv)
    wait(PE, s_ca, s_xv)
    mms(out4, [(ca[a][:, :], T.XV[:, a:192:4]) for a in range(4)], s_o4)

    for x, rv in ((0, T.RV0), (1, T.RV1)):
        ts(rv[:, :], T.I128[:, 0:16], f(10 + x), A.is_equal, T.MC[:, x:x + 1], A.mult, to=s_p4)
    wait(V, s_j16)
    ts(T.LREP[:, :], T.J16[:, :], f(1), A.is_equal, to=s_p4)
    wait(PE, s_p4)
    mms(T.b0[:, 0:16], [(T.LREP[:, :], T.RV0[:, :]), (T.LREP[:, :], T.RV1[:, :])], s_vl)
    mms(T.b2[:, 0:256], [(T.LTA0[:, :], perms[0]), (T.LTA1[:, :], perms[1])], s_mpa)
    wait(S, s_mp)
    do(S, act.activation(T.MSK[:, :], T.b4[:, 0:256], F.Copy), s_mk)
    wait(S, s_mpa)
    do(S, act.activation(T.MSKA[:, :], T.b2[:, 0:256], F.Copy), s_mka)
    wait(V, s_ho)
    cp(T.ANSH[:, 12 * r:12 * r + 12], T.HOUT[:, 12 * r:12 * r + 12])
    ts(T.SEL[:, :], T.I128[:, 0:8], f(0), A.is_equal, to=s_se)
    ts(T.SELA[:, :], T.I128[:, 0:8], f(14), A.is_equal, to=s_se)
    wait(V, s_o4)
    cp(T.AOUT[:, :], out4, s_ao)
    wait(GQ, s_ao)
    send3(lambda q: T.AOUT[:, 12 * q:12 * q + 12], T.ANSA[:, 12 * prv:12 * prv + 12], T.sem.aa, T.sem.l_aa, [4, 2, 2])
    wait(V, s_vl)
    cp(T.VL[:, :], T.b0[:, 0:16])
    wait(V, s_ao)
    cp(T.ANSA[:, 12 * prv:12 * prv + 12], T.AOUT[:, 12 * r:12 * r + 12])
    landed = sum((4, 2, 2)[[o for o in range(n_ranks) if o != q].index(r)] for q in others)
    s_xh, s_x = sig(), [sig(), sig()]
    s_y, s_ys = [sig(), sig()], [sig(), sig()]
    sync(V)
    wait(V, s_mk)
    v.wait_ge(T.sem.ha, landed)
    tt(T.XH[:, :], T.ANSH[:, :].indirect(T.VL[:, 0:16]), T.MSK[:, :], A.mult, s_xh)
    wait(V, s_mka)
    v.wait_ge(T.sem.aa, landed)
    wait(PE, s_xh, s_se)
    part = [slice(0, 128), slice(128, 256)]
    bank = [T.b6[0:8, 0:128], T.b7[0:8, 0:128]]
    for i in range(2):
        tt(T.XA[:, part[i]], T.ANSA[:, :].indirect(T.VL[:, 8 * i:8 * i + 8]), T.MSKA[:, part[i]], A.mult, s_x[i])
        pe.matmul(bank[i], T.SEL[:, :], T.XH[:, part[i]], True, False)
    for i in range(2):
        wait(PE, s_x[i])
        do(PE, pe.matmul(bank[i], T.SELA[:, :], T.XA[:, part[i]], False, True), s_y[i])
    wait(S, s_y[0])
    do(S, act.activation(T.YS[:, part[0]], bank[0], F.Copy), s_ys[0])
    sync(S)
    g.scalar.dma_start(T.y[:, part[0]], T.YS[:, part[0]]).then_inc(T.sem.st, 16)
    wait(V, s_y[1])
    cp(T.YS[:, part[1]], bank[1], s_ys[1])
    wait(SQ, s_ys[1])
    g.sync.dma_start(T.y[:, part[1]], T.YS[:, part[1]]).then_inc(T.sem.st, 16)
    sync(V)
    sync(PE)
    g.sync.wait_ge(T.sem.st, 32)
    for s, n in ((T.sem.l_rq, 6), (T.sem.l_ra, 6), (T.sem.l_ls, n8), (T.sem.l_ha, 8), (T.sem.l_aa, 8)):
        g.wait_ge(s, n)
